import numpy as np
import ml_dtypes


def mxq(x, axis, fmt="e4m3"):
    dtype, down = {"e4m3": (ml_dtypes.float8_e4m3fn, 7), "e5m2": (ml_dtypes.float8_e5m2, 14)}[fmt]
    v = np.moveaxis(np.asarray(x, np.float32).astype(ml_dtypes.bfloat16).astype(np.float64), axis, -1)
    blocks = v.reshape(v.shape[:-1] + (-1, 32))
    amax = np.abs(blocks).max(-1, keepdims=True)
    byte = np.maximum(np.where(amax > 0, np.frexp(amax)[1] - 1 + 127, 0) - down, 1)
    scale = np.exp2(byte - 127.0)
    codes = (blocks / scale).astype(np.float32).astype(dtype).astype(np.float64)
    return np.moveaxis((codes * scale).reshape(v.shape), -1, axis)


WIDE = False


def mx_kscale(k):
    if not WIDE:
        return np.ones(k)
    levels = np.array([10, -10, 5, -5, 0])
    if k % 512:
        return np.exp2(np.random.permutation(np.resize(levels, k // 32))).repeat(32)
    a = np.empty((k // 512, 16))
    for p in range(k // 512):
        a[p, :8] = np.random.permutation(np.resize(levels, 8))
        for g in range(8):
            far = levels[np.abs(levels - a[p, g]) >= 10]
            a[p, g + 8] = far[np.random.randint(len(far))]
    return np.exp2(a.ravel()).repeat(32)


def f64(x):
    return np.asarray(x).astype(np.float64)


def striped(idx):
    return np.tile(idx.reshape(-1, 16).T, (8, 1)).astype(np.uint16)


def unstriped(offs):
    return offs[:16].T.reshape(-1).astype(np.int64)


E2M1 = np.array([0.0, 0.5, 1.0, 1.5, 2.0, 3.0, 4.0, 6.0, -0.0, -0.5, -1.0, -1.5, -2.0, -3.0, -4.0, -6.0])


def pack_weight(w, fmt):
    k, n = w.shape
    w = f64(np.asarray(w, np.float32).astype(ml_dtypes.bfloat16)).reshape(k // 32, 32, n)
    amax = np.abs(w).max(1)
    if fmt == "e4m3":
        byte = np.frexp(amax)[1] - 1 + 127 - 7
    else:
        mant, ex = np.frexp(amax / 6.0)
        byte = np.where(mant > 0.5, ex, ex - 1) + 127
    byte = np.clip(np.where(amax > 0, byte, 1), 1, 254)
    scaled = (w * np.exp2(127.0 - byte)[:, None, :]).reshape(k, n).astype(np.float32)
    by_word = np.ascontiguousarray(scaled.reshape(k // 512, 128, 4, n).transpose(0, 1, 3, 2))
    if fmt == "e4m3":
        words = by_word.astype(ml_dtypes.float8_e4m3fn).view(np.uint8)
    else:
        c = by_word.astype(ml_dtypes.float4_e2m1fn).view(np.uint8) & 0xF
        words = (c[..., 0::2] | (c[..., 1::2] << 4)).reshape(k // 512, 128, 2 * n)
    return np.ascontiguousarray(words), np.ascontiguousarray(byte.astype(np.uint8).reshape(k // 512, 16, n))


def unpack_weight(words, scales, fmt):
    g, _, n = scales.shape
    words = np.ascontiguousarray(words).reshape(g, 128, n, -1)
    if fmt == "e4m3":
        vals = words.view(ml_dtypes.float8_e4m3fn).astype(np.float64)
    else:
        nib = np.empty((g, 128, n, 4), np.uint8)
        nib[..., 0::2] = words & 0xF
        nib[..., 1::2] = words >> 4
        vals = E2M1[nib]
    vals = vals * np.repeat(np.exp2(scales.astype(np.float64) - 127.0), 8, axis=1)[..., None]
    return vals.transpose(0, 1, 3, 2).reshape(g * 512, n)


def gelu(v):
    return 0.5 * v * (1.0 + np.tanh(np.sqrt(2.0 / np.pi) * (v + 0.044715 * v**3)))


def striped8(idx):
    return np.concatenate([v.reshape(-1, 16).T for v in idx]).astype(np.uint16)


def unstriped8(offs):
    return np.stack([offs[16 * g:16 * g + 16].T.reshape(-1) for g in range(8)]).astype(np.int64)


def runs(v, idx8):
    k = np.arange(v.shape[0])
    return v[k[:, None], idx8[k % 512 // 64]]


def often(T, S):
    return np.random.permutation(T)[(T * np.random.uniform(0, 1, S) ** 4).astype(np.int64)]


K, T, S, H, N = 512, 2048, 1024, 1024, 768


def setup_inputs():
    n = np.random.standard_normal
    s = mx_kscale(K)[:, None]
    u = mx_kscale(H)[:, None]
    tab_words, tab_scales = pack_weight(n((K, T)) * s, "e4m3")
    offs = striped8(np.stack([often(T, S) for _ in range(8)]))
    w1 = (n((K, H)) / np.sqrt(K) / s).astype(np.float32)
    w2_words, w2_scales = pack_weight(n((K, H)) / np.sqrt(K) / s, "e2m1")
    w3_words, w3_scales = pack_weight(n((K, H)) / np.sqrt(K) / s, "e4m3")
    rel = np.random.choice([-1.0, 1.0], H) * np.random.uniform(0.5, 1.5, H)
    rel = (rel * u[:, 0]).astype(np.float32)
    cand = (n((H, N)) / np.sqrt(H) / u).astype(np.float32)
    prior = (0.5 * n(N)).astype(np.float32)
    return {"tab_words": tab_words, "tab_scales": tab_scales, "offs": offs,
            "w1": w1, "w2_words": w2_words, "w2_scales": w2_scales,
            "w3_words": w3_words, "w3_scales": w3_scales,
            "rel": rel, "cand": cand, "prior": prior}


def reference(tab_words, tab_scales, offs, w1, w2_words, w2_scales,
              w3_words, w3_scales, rel, cand, prior):
    v = runs(unpack_weight(tab_words, tab_scales, "e4m3"), unstriped8(offs))
    w2 = unpack_weight(w2_words, w2_scales, "e2m1")
    w3 = unpack_weight(w3_words, w3_scales, "e4m3")
    x1 = mxq(f64(w1), 0, "e4m3").T @ v
    x2 = w2.T @ v
    x3 = w3.T @ v
    h = f64(rel)[:, None] * (x1 * x2 * x3)
    scores = mxq(f64(cand), 0, "e4m3").T @ mxq(h, 0, "e4m3")
    return scores + f64(prior)[:, None]

@@ -1,0 +1,303 @@
+from contextlib import ExitStack
+
+import concourse.mybir as mybir
+from concourse.masks import make_identity
+
+K, T, S, H, N = 512, 2048, 1024, 1024, 768
+FLOPS = 2 * K * H * S * 3 + 2 * H * N * S
+
+F32 = mybir.dt.float32
+BF16 = mybir.dt.bfloat16
+I32 = mybir.dt.int32
+U32 = mybir.dt.uint32
+U16 = mybir.dt.uint16
+U8 = mybir.dt.uint8
+FP8X4 = mybir.dt.float8_e4m3fn_x4
+FP4X4 = mybir.dt.float4_e2m1fn_x4
+MULT = mybir.AluOpType.mult
+ADD = mybir.AluOpType.add
+ACT = mybir.ActivationFunctionType
+
+P = 128
+HALF = 512
+NT = N // P
+
+
+def tile_list_hyper_relational_scoring_kernel(
+    tc, tab_words, tab_scales, offs, w1, w2_words, w2_scales, w3_words, w3_scales, rel, cand, prior, out
+):
+    nc = tc.nc
+    with ExitStack() as ctx:
+        keep = ctx.enter_context(tc.tile_pool(name="keep", bufs=1))
+        work = ctx.enter_context(tc.tile_pool(name="work", bufs=2))
+        psum = ctx.enter_context(tc.psum_pool(name="psum", bufs=2))
+
+        offsets = keep.tile([P, S // 16], U16, name="offsets")
+        nc.sync.dma_start(offsets[:], offs)
+
+        tab_rows = keep.tile([P, T], U8, name="tab_rows", tag="share_a", align_bytes=64)
+        w_rows = keep.tile([P, 2, H], U8, name="w_rows", align_bytes=64)
+        nc.vector.memset(tab_rows[:].bitcast(I32), 0)
+        nc.vector.memset(w_rows[:].rearrange("p w c -> p (w c)").bitcast(I32), 0)
+        nc.scalar.dma_start(tab_rows[0:P:8, :].bitcast(I32), tab_scales[0].bitcast(I32))
+        nc.scalar.dma_start(w_rows[0:P:8, 0, :].bitcast(I32), w2_scales[0].bitcast(I32))
+        nc.scalar.dma_start(w_rows[0:P:8, 1, :].bitcast(I32), w3_scales[0].bitcast(I32))
+
+        table = keep.tile([P, T], I32, name="table", align_bytes=64)
+        nc.sync.dma_start(table[:], tab_words[0].rearrange("p n t -> p (n t)").bitcast(I32))
+        w2_raw = keep.tile([P, H // 2], I32, name="w2_raw", tag="share_c", align_bytes=64)
+        nc.sync.dma_start(w2_raw[:], w2_words[0].bitcast(I32))
+        w3_raw = keep.tile([P, H], I32, name="w3_raw", tag="share_b", align_bytes=64)
+        nc.sync.dma_start(w3_raw[:], w3_words[0].rearrange("p n t -> p (n t)").bitcast(I32))
+
+        def load_w1(b, tag):
+            raw = keep.tile([P, 4, HALF], F32, name="w1_raw%d" % b, tag=tag, align_bytes=64)
+            nc.sync.dma_start(raw[:], w1[:, b * HALF : (b + 1) * HALF].rearrange("(p j) c -> p j c", j=4))
+            return raw
+
+        w1_raw = [load_w1(0, "w1_first")]
+
+        vec_rows = keep.tile([P, 3 * P], F32, name="vec_rows", align_bytes=64)
+        nc.gpsimd.memset(vec_rows[:], 0.0)
+        nc.gpsimd.dma_start(vec_rows[0:4, 0 : 2 * P], rel.rearrange("(i t u) -> t i u", t=4, u=8))
+        identity = keep.tile([P, P], F32, name="identity", align_bytes=64)
+        make_identity(nc, identity[:])
+        nc.gpsimd.dma_start(vec_rows[0:NT, 2 * P :], prior.rearrange("(c p) -> c p", p=P))
+        rel_bank = psum.tile([P, 2, P], F32, name="scores")
+        for b in range(2):
+            nc.tensor.transpose(rel_bank[:, b, :], vec_rows[:, b * P : (b + 1) * P], identity[:])
+        rel_cols = keep.tile([P, 2, 4], F32, name="rel_cols", align_bytes=64)
+        nc.scalar.copy(rel_cols[:], rel_bank[:, :, 0:4])
+        prior_cols = keep.tile([P, NT], F32, name="prior_cols", align_bytes=64)
+
+        def turn_prior():
+            prior_bank = psum.tile([P, P], F32, name="scores")
+            nc.tensor.transpose(prior_bank[:], vec_rows[:, 2 * P :], identity[:])
+            nc.scalar.copy(prior_cols[:], prior_bank[:, 0:NT])
+
+        def lists(h):
+            return offsets[:, h * (HALF // 16) : (h + 1) * (HALF // 16)]
+
+        def settle_rows(plane):
+            for q in range(1, 4):
+                nc.scalar.dma_start(plane[q:P:32, :].bitcast(I32), plane[8 * q : P : 32, :].bitcast(I32))
+
+        picked0 = keep.tile([P, HALF], U8, name="picked0", align_bytes=64)
+        nc.vector.tensor_copy(picked0[:], tab_rows[:].indirect(lists(0)))
+        plane0 = keep.tile([P, HALF + 2 * H], U8, name="plane0", align_bytes=64)
+        nc.vector.tensor_copy(plane0[:, 0:HALF].bitcast(I32), picked0[:].bitcast(I32))
+        nc.vector.tensor_copy(
+            plane0[:, HALF:].bitcast(I32).rearrange("p (b t i u) -> p b t i u", b=4, t=4, i=16),
+            w_rows[:].rearrange("p w c -> p (w c)").bitcast(I32).rearrange("p (b i t u) -> p b t i u", b=4, t=4, i=16),
+        )
+        settle_rows(plane0)
+        picked1 = keep.tile([P, HALF], U8, name="picked1", align_bytes=64)
+        nc.vector.tensor_copy(picked1[:], tab_rows[:].indirect(lists(1)))
+        plane1 = keep.tile([P, HALF], U8, name="plane1", align_bytes=64)
+        nc.vector.tensor_copy(plane1[:].bitcast(I32), picked1[:].bitcast(I32))
+        settle_rows(plane1)
+        v_scales = [plane0[:, 0:HALF], plane1[:]]
+        w2_plane = plane0[:, HALF : HALF + H]
+        w3_plane = plane0[:, HALF + H :]
+
+        w1_raw.append(load_w1(1, "share_a"))
+
+        v_words = []
+
+        def gather_words(h):
+            words = keep.tile([P, HALF], I32, name="v_words%d" % h, align_bytes=64)
+            nc.vector.tensor_copy(words[:].bitcast(U32), table[:].bitcast(U32).indirect(lists(h)))
+            v_words.append(words)
+
+        gather_words(0)
+
+        w2_codes = []
+        w3_codes = []
+        for b in range(2):
+            c2 = keep.tile([P, HALF // 2], I32, name="w2_codes%d" % b, align_bytes=64)
+            nc.vector.tensor_copy(
+                c2[:].rearrange("p (t i u) -> p t i u", t=4, i=16),
+                w2_raw[:, b * HALF // 2 : (b + 1) * HALF // 2].rearrange("p (i t u) -> p t i u", t=4, i=16),
+            )
+            c3 = keep.tile([P, HALF], I32, name="w3_codes%d" % b, align_bytes=64)
+            nc.vector.tensor_copy(
+                c3[:].rearrange("p (t i u) -> p t i u", t=4, i=16),
+                w3_raw[:, b * HALF : (b + 1) * HALF].rearrange("p (i t u) -> p t i u", t=4, i=16),
+            )
+            w2_codes.append(c2)
+            w3_codes.append(c3)
+
+        cand_view = cand.rearrange("(b i t u) n -> b t i u n", b=2, i=16, t=4, u=8)
+        cand_raw = []
+        for b, tag in enumerate(("share_b", "share_c")):
+            raw = keep.tile([P, 4, N], F32, name="cand_raw%d" % b, tag=tag, align_bytes=64)
+            for t in range(4):
+                nc.sync.dma_start(raw[:, t, :], cand_view[b, t])
+            cand_raw.append(raw)
+
+        w1_codes = [keep.tile([P, HALF], U32, name="w1_codes%d" % b, align_bytes=64) for b in range(2)]
+        w1_planes = [keep.tile([P, HALF], U8, name="w1_plane%d" % b, align_bytes=64) for b in range(2)]
+        cand_codes = [keep.tile([P, N], U32, name="cand_codes%d" % b, align_bytes=64) for b in range(2)]
+        cand_planes = [keep.tile([P, N], U8, name="cand_plane%d" % b, align_bytes=64) for b in range(2)]
+        w1_round = [keep.tile([P, 4 * HALF], BF16, name="w1_round%d" % b, align_bytes=64) for b in range(2)]
+        cand_round = [keep.tile([P, 4 * N], BF16, name="cand_round%d" % b, align_bytes=64) for b in range(2)]
+
+        def round_w1(b):
+            src = w1_raw[b][:].rearrange("p j (i t u e) -> p t i u j e", i=16, t=4, u=4, e=2)
+            for t in range(4):
+                dst = w1_round[b][:, t * HALF : (t + 1) * HALF].rearrange("p (i u e j) -> p i u j e", i=16, u=4, e=2)
+                nc.scalar.copy(dst, src[:, t])
+
+        def quantise_w1(b):
+            nc.vector.quantize_mx(out=w1_codes[b][:].bitcast(FP8X4), scales=w1_planes[b][:], in_=w1_round[b][:])
+
+        def round_cand(b):
+            for lo in range(0, N, 256):
+                dst = cand_round[b][:, 4 * lo : 4 * (lo + 256)].rearrange("p (c e t) -> p c t e", e=2, t=4)
+                src = cand_raw[b][:, :, lo : lo + 256].rearrange("p t (c e) -> p c t e", e=2)
+                nc.scalar.copy(dst, src)
+
+        def quantise_cand(b):
+            for lo, hi in ((0, 512), (512, N)):
+                nc.vector.quantize_mx(
+                    out=cand_codes[b][:, lo:hi].bitcast(FP8X4),
+                    scales=cand_planes[b][:, lo:hi],
+                    in_=cand_round[b][:, 4 * lo : 4 * hi],
+                )
+
+        def pair_product(h, b):
+            pair = work.tile([P, 4, HALF], F32, name="pair", bufs=3)
+            for t in range(4):
+                cols = slice(t * P, (t + 1) * P)
+                wide = slice(b * HALF + t * P, b * HALF + (t + 1) * P)
+                x2 = psum.tile([P, HALF], F32, name="x2")
+                nc.tensor.matmul_mx(
+                    out=x2[:],
+                    lhsT=w2_codes[b][:, t * P // 2 : (t + 1) * P // 2].bitcast(FP4X4),
+                    lhsT_scale=w2_plane[:, wide],
+                    rhs=v_words[h][:].bitcast(FP8X4),
+                    rhs_scale=v_scales[h],
+                    start=True,
+                    stop=True,
+                )
+                x3 = psum.tile([P, HALF], F32, name="x3")
+                nc.tensor.matmul_mx(
+                    out=x3[:],
+                    lhsT=w3_codes[b][:, cols].bitcast(FP8X4),
+                    lhsT_scale=w3_plane[:, wide],
+                    rhs=v_words[h][:].bitcast(FP8X4),
+                    rhs_scale=v_scales[h],
+                    start=True,
+                    stop=True,
+                )
+                scaled = work.tile([P, HALF], F32, name="scaled", bufs=6)
+                nc.scalar.activation(scaled[:], x2[:], ACT.Copy, scale=rel_cols[:, b, t : t + 1])
+                nc.vector.tensor_tensor(pair[:, t, :], x3[:], scaled[:], MULT)
+            return pair
+
+        def triple_product(h, b, pair, h_round, q):
+            cols = slice(q * P, (q + 1) * P)
+            x1 = psum.tile([P, 4, P], F32, name="x1")
+            for t in range(4):
+                nc.tensor.matmul_mx(
+                    out=x1[:, t, :],
+                    lhsT=w1_codes[b][:, t * P : (t + 1) * P].bitcast(FP8X4),
+                    lhsT_scale=w1_planes[b][:, t * P : (t + 1) * P],
+                    rhs=v_words[h][:, cols].bitcast(FP8X4),
+                    rhs_scale=v_scales[h][:, cols],
+                    start=True,
+                    stop=True,
+                )
+            nc.vector.tensor_tensor(
+                h_round[:, 4 * q * P : 4 * (q + 1) * P].rearrange("p (n e t) -> p n t e", e=2, t=4),
+                x1[:].rearrange("p t (n e) -> p n t e", e=2),
+                pair[:, :, cols].rearrange("p t (n e) -> p n t e", e=2),
+                MULT,
+            )
+
+        h_codes = {}
+        h_planes = {}
+        h_rounds = {}
+        for h in range(2):
+            for b in range(2):
+                h_codes[h, b] = keep.tile([P, HALF], U32, name="h_codes%d%d" % (h, b), align_bytes=64)
+                h_planes[h, b] = keep.tile([P, HALF], U8, name="h_plane%d%d" % (h, b), align_bytes=64)
+                h_rounds[h, b] = keep.tile([P, 4 * HALF], BF16, name="h_round%d%d" % (h, b), align_bytes=64)
+
+        def quantise_h(h, b, lo, hi):
+            nc.vector.quantize_mx(
+                out=h_codes[h, b][:, lo:hi].bitcast(FP8X4),
+                scales=h_planes[h, b][:, lo:hi],
+                in_=h_rounds[h, b][:, 4 * lo : 4 * hi],
+            )
+
+        out_view = out.rearrange("(c p) j -> p c j", p=P)
+
+        def score(h, lo, hi, per_store, vector_banks):
+            width = hi - lo
+            per_bank = min(HALF // width, 3)
+            for s0 in range(0, NT, per_store):
+                staged = work.tile([P, per_store, width], F32, name="staged", bufs=4)
+                for c0 in range(s0, s0 + per_store, per_bank):
+                    bank = psum.tile([P, per_bank, width], F32, name="scores")
+                    for g in range(per_bank):
+                        c = c0 + g
+                        for b in range(2):
+                            nc.tensor.matmul_mx(
+                                out=bank[:, g, :],
+                                lhsT=cand_codes[b][:, c * P : (c + 1) * P].bitcast(FP8X4),
+                                lhsT_scale=cand_planes[b][:, c * P : (c + 1) * P],
+                                rhs=h_codes[h, b][:, lo:hi].bitcast(FP8X4),
+                                rhs_scale=h_planes[h, b][:, lo:hi],
+                                start=(b == 0),
+                                stop=(b == 1),
+                            )
+                    if c0 in vector_banks:
+                        nc.vector.tensor_tensor(
+                            staged[:, c0 - s0 : c0 - s0 + per_bank, :],
+                            bank[:],
+                            prior_cols[:, c0 : c0 + per_bank].unsqueeze(2).to_broadcast([P, per_bank, width]),
+                            ADD,
+                        )
+                    else:
+                        for g in range(per_bank):
+                            c = c0 + g
+                            nc.scalar.activation(
+                                staged[:, c - s0, :], bank[:, g, :], ACT.Identity, bias=prior_cols[:, c : c + 1]
+                            )
+                nc.sync.dma_start(out_view[:, s0 : s0 + per_store, h * HALF + lo : h * HALF + hi], staged[:])
+
+        pair = pair_product(0, 0)
+        round_w1(0)
+        gather_words(1)
+        quantise_w1(0)
+        for q in range(4):
+            triple_product(0, 0, pair, h_rounds[0, 0], q)
+        pair = pair_product(0, 1)
+        quantise_h(0, 0, 0, HALF)
+        round_w1(1)
+        quantise_w1(1)
+        for q in range(4):
+            triple_product(0, 1, pair, h_rounds[0, 1], q)
+        turn_prior()
+        round_cand(0)
+        pair = pair_product(1, 0)
+        quantise_h(0, 1, 0, HALF)
+        quantise_cand(0)
+        round_cand(1)
+        for q in range(4):
+            triple_product(1, 0, pair, h_rounds[1, 0], q)
+        quantise_cand(1)
+        pair = pair_product(1, 1)
+        quantise_h(1, 0, 0, HALF)
+        score(0, 0, HALF, 2, ())
+        for q in range(2):
+            triple_product(1, 1, pair, h_rounds[1, 1], q)
+        triple_product(1, 1, pair, h_rounds[1, 1], 2)
+        quantise_h(1, 1, 0, 2 * P)
+        triple_product(1, 1, pair, h_rounds[1, 1], 3)
+        quantise_h(1, 1, 2 * P, 3 * P)
+        score(1, 0, 2 * P, 6, ())
+        quantise_h(1, 1, 3 * P, 4 * P)
+        score(1, 2 * P, 3 * P, 3, (3,))
+        score(1, 3 * P, 4 * P, 3, (3,))

@@ -37,13 +37,16 @@ def tile_list_hyper_relational_scoring_kernel(
 
         tab_rows = keep.tile([P, T], U8, name="tab_rows", tag="share_a", align_bytes=64)
         w_rows = keep.tile([P, 2, H], U8, name="w_rows", align_bytes=64)
-        nc.vector.memset(tab_rows[:].bitcast(I32), 0)
-        nc.vector.memset(w_rows[:].rearrange("p w c -> p (w c)").bitcast(I32), 0)
-        nc.scalar.dma_start(tab_rows[0:P:8, :].bitcast(I32), tab_scales[0].bitcast(I32))
-        nc.scalar.dma_start(w_rows[0:P:8, 0, :].bitcast(I32), w2_scales[0].bitcast(I32))
-        nc.scalar.dma_start(w_rows[0:P:8, 1, :].bitcast(I32), w3_scales[0].bitcast(I32))
 
-        table = keep.tile([P, T], I32, name="table", align_bytes=64)
+        def eightfold(scales):
+            words = scales[0].bitcast(I32)
+            return words.unsqueeze(1).to_broadcast([16, 8, words.shape[1]])
+
+        nc.sync.dma_start(tab_rows[:].bitcast(I32), eightfold(tab_scales))
+        nc.sync.dma_start(w_rows[:, 0, :].bitcast(I32), eightfold(w2_scales))
+        nc.sync.dma_start(w_rows[:, 1, :].bitcast(I32), eightfold(w3_scales))
+
+        table = keep.tile([P, T], I32, name="table", tag="share_e", align_bytes=64)
         nc.sync.dma_start(table[:], tab_words[0].rearrange("p n t -> p (n t)").bitcast(I32))
         w2_raw = keep.tile([P, H // 2], I32, name="w2_raw", tag="share_c", align_bytes=64)
         nc.sync.dma_start(w2_raw[:], w2_words[0].bitcast(I32))
@@ -55,13 +58,13 @@ def tile_list_hyper_relational_scoring_kernel(
             nc.sync.dma_start(raw[:], w1[:, b * HALF : (b + 1) * HALF].rearrange("(p j) c -> p j c", j=4))
             return raw
 
-        w1_raw = [load_w1(0, "w1_first")]
 
         vec_rows = keep.tile([P, 3 * P], F32, name="vec_rows", align_bytes=64)
-        nc.gpsimd.memset(vec_rows[:], 0.0)
-        nc.gpsimd.dma_start(vec_rows[0:4, 0 : 2 * P], rel.rearrange("(i t u) -> t i u", t=4, u=8))
+        nc.vector.memset(vec_rows[:], 0.0)
+        nc.scalar.dma_start(vec_rows[0:4, 0 : 2 * P], rel.rearrange("(i t u) -> t i u", t=4, u=8))
         identity = keep.tile([P, P], F32, name="identity", align_bytes=64)
-        make_identity(nc, identity[:])
+        nc.vector.memset(identity[:], 0.0)
+        make_identity(nc, identity[:], nomemset=True)
         nc.gpsimd.dma_start(vec_rows[0:NT, 2 * P :], prior.rearrange("(c p) -> c p", p=P))
         rel_bank = psum.tile([P, 2, P], F32, name="scores")
         for b in range(2):
@@ -80,7 +83,7 @@ def tile_list_hyper_relational_scoring_kernel(
 
         def settle_rows(plane):
             for q in range(1, 4):
-                nc.scalar.dma_start(plane[q:P:32, :].bitcast(I32), plane[8 * q : P : 32, :].bitcast(I32))
+                nc.sync.dma_start(plane[q:P:32, :].bitcast(I32), plane[8 * q : P : 32, :].bitcast(I32))
 
         picked0 = keep.tile([P, HALF], U8, name="picked0", align_bytes=64)
         nc.vector.tensor_copy(picked0[:], tab_rows[:].indirect(lists(0)))
@@ -91,7 +94,7 @@ def tile_list_hyper_relational_scoring_kernel(
             w_rows[:].rearrange("p w c -> p (w c)").bitcast(I32).rearrange("p (b i t u) -> p b t i u", b=4, t=4, i=16),
         )
         settle_rows(plane0)
-        picked1 = keep.tile([P, HALF], U8, name="picked1", align_bytes=64)
+        picked1 = keep.tile([P, HALF], U8, name="picked1", tag="share_d", align_bytes=64)
         nc.vector.tensor_copy(picked1[:], tab_rows[:].indirect(lists(1)))
         plane1 = keep.tile([P, HALF], U8, name="plane1", align_bytes=64)
         nc.vector.tensor_copy(plane1[:].bitcast(I32), picked1[:].bitcast(I32))
@@ -100,36 +103,36 @@ def tile_list_hyper_relational_scoring_kernel(
         w2_plane = plane0[:, HALF : HALF + H]
         w3_plane = plane0[:, HALF + H :]
 
-        w1_raw.append(load_w1(1, "share_a"))
+        w1_raw = [load_w1(0, "share_a"), load_w1(1, "share_d")]
 
         v_words = []
 
-        def gather_words(h):
-            words = keep.tile([P, HALF], I32, name="v_words%d" % h, align_bytes=64)
+        def gather_words(h, tag):
+            words = keep.tile([P, HALF], I32, name="v_words%d" % h, tag=tag, align_bytes=64)
             nc.vector.tensor_copy(words[:].bitcast(U32), table[:].bitcast(U32).indirect(lists(h)))
             v_words.append(words)
 
-        gather_words(0)
+        gather_words(0, "v_first")
 
-        w2_codes = []
+        w2_all = keep.tile([P, H // 2], I32, name="w2_codes", align_bytes=64)
+        nc.vector.tensor_copy(
+            w2_all[:].rearrange("p (b t i u) -> p b t i u", b=2, t=4, i=16),
+            w2_raw[:].rearrange("p (b i t u) -> p b t i u", b=2, t=4, i=16),
+        )
+        w2_codes = [w2_all[:, b * HALF // 2 : (b + 1) * HALF // 2] for b in range(2)]
         w3_codes = []
         for b in range(2):
-            c2 = keep.tile([P, HALF // 2], I32, name="w2_codes%d" % b, align_bytes=64)
-            nc.vector.tensor_copy(
-                c2[:].rearrange("p (t i u) -> p t i u", t=4, i=16),
-                w2_raw[:, b * HALF // 2 : (b + 1) * HALF // 2].rearrange("p (i t u) -> p t i u", t=4, i=16),
-            )
             c3 = keep.tile([P, HALF], I32, name="w3_codes%d" % b, align_bytes=64)
             nc.vector.tensor_copy(
                 c3[:].rearrange("p (t i u) -> p t i u", t=4, i=16),
                 w3_raw[:, b * HALF : (b + 1) * HALF].rearrange("p (i t u) -> p t i u", t=4, i=16),
             )
-            w2_codes.append(c2)
             w3_codes.append(c3)
+        gather_words(1, "share_c")
 
         cand_view = cand.rearrange("(b i t u) n -> b t i u n", b=2, i=16, t=4, u=8)
         cand_raw = []
-        for b, tag in enumerate(("share_b", "share_c")):
+        for b, tag in enumerate(("share_b", "share_e")):
             raw = keep.tile([P, 4, N], F32, name="cand_raw%d" % b, tag=tag, align_bytes=64)
             for t in range(4):
                 nc.sync.dma_start(raw[:, t, :], cand_view[b, t])
@@ -143,18 +146,21 @@ def tile_list_hyper_relational_scoring_kernel(
         cand_round = [keep.tile([P, 4 * N], BF16, name="cand_round%d" % b, align_bytes=64) for b in range(2)]
 
         def round_w1(b):
-            src = w1_raw[b][:].rearrange("p j (i t u e) -> p t i u j e", i=16, t=4, u=4, e=2)
-            for t in range(4):
-                dst = w1_round[b][:, t * HALF : (t + 1) * HALF].rearrange("p (i u e j) -> p i u j e", i=16, u=4, e=2)
-                nc.scalar.copy(dst, src[:, t])
+            src = w1_raw[b][:].rearrange("p j (i t u) -> p t i j u", i=16, t=4)
+            dst = w1_round[b][:].rearrange("p (t i u j) -> p t i j u", i=16, t=4, j=4)
+            if b == 0:
+                nc.vector.tensor_copy(dst, src)
+            else:
+                for t in (0, 2):
+                    nc.scalar.copy(dst[:, t : t + 2], src[:, t : t + 2])
 
         def quantise_w1(b):
             nc.vector.quantize_mx(out=w1_codes[b][:].bitcast(FP8X4), scales=w1_planes[b][:], in_=w1_round[b][:])
 
         def round_cand(b):
-            for lo in range(0, N, 256):
-                dst = cand_round[b][:, 4 * lo : 4 * (lo + 256)].rearrange("p (c e t) -> p c t e", e=2, t=4)
-                src = cand_raw[b][:, :, lo : lo + 256].rearrange("p t (c e) -> p c t e", e=2)
+            for lo in range(0, N, 384):
+                dst = cand_round[b][:, 4 * lo : 4 * (lo + 384)].rearrange("p (c e t) -> p c t e", e=2, t=4)
+                src = cand_raw[b][:, :, lo : lo + 384].rearrange("p t (c e) -> p c t e", e=2)
                 nc.scalar.copy(dst, src)
 
         def quantise_cand(b):
@@ -165,8 +171,9 @@ def tile_list_hyper_relational_scoring_kernel(
                     in_=cand_round[b][:, 4 * lo : 4 * hi],
                 )
 
-        def pair_product(h, b):
-            pair = work.tile([P, 4, HALF], F32, name="pair", bufs=3)
+        def pair_product(h, b, tag, between=None):
+            pair = work.tile([P, 4, HALF], F32, name="pair", bufs=4)
+            scaled = keep.tile([P, 4, HALF], F32, name="scaled%d%d" % (h, b), tag=tag, align_bytes=64)
             for t in range(4):
                 cols = slice(t * P, (t + 1) * P)
                 wide = slice(b * HALF + t * P, b * HALF + (t + 1) * P)
@@ -190,9 +197,10 @@ def tile_list_hyper_relational_scoring_kernel(
                     start=True,
                     stop=True,
                 )
-                scaled = work.tile([P, HALF], F32, name="scaled", bufs=6)
-                nc.scalar.activation(scaled[:], x2[:], ACT.Copy, scale=rel_cols[:, b, t : t + 1])
-                nc.vector.tensor_tensor(pair[:, t, :], x3[:], scaled[:], MULT)
+                nc.scalar.activation(scaled[:, t, :], x2[:], ACT.Copy, scale=rel_cols[:, b, t : t + 1])
+                nc.vector.tensor_tensor(pair[:, t, :], x3[:], scaled[:, t, :], MULT)
+                if between is not None:
+                    between(t)
             return pair
 
         def triple_product(h, b, pair, h_round, q):
@@ -233,13 +241,13 @@ def tile_list_hyper_relational_scoring_kernel(
 
         out_view = out.rearrange("(c p) j -> p c j", p=P)
 
-        def score(h, lo, hi, per_store, vector_banks):
+        def score(h, lo, hi, per_store, vector_banks, tags, first=0, last=NT):
             width = hi - lo
             per_bank = min(HALF // width, 3)
-            for s0 in range(0, NT, per_store):
-                staged = work.tile([P, per_store, width], F32, name="staged", bufs=4)
+            for s0 in range(first, last, per_store):
+                staged = keep.tile([P, per_store, width], F32, name="staged_%d_%d_%d" % (h, lo, s0))
                 for c0 in range(s0, s0 + per_store, per_bank):
-                    bank = psum.tile([P, per_bank, width], F32, name="scores")
+                    bank = psum.tile([P, per_bank, width], F32, name="scores", tag=tags[c0 // per_bank % len(tags)])
                     for g in range(per_bank):
                         c = c0 + g
                         for b in range(2):
@@ -267,37 +275,36 @@ def tile_list_hyper_relational_scoring_kernel(
                             )
                 nc.sync.dma_start(out_view[:, s0 : s0 + per_store, h * HALF + lo : h * HALF + hi], staged[:])
 
-        pair = pair_product(0, 0)
+        pair = pair_product(0, 0, "scaled_a")
         round_w1(0)
-        gather_words(1)
         quantise_w1(0)
+        round_w1(1)
         for q in range(4):
             triple_product(0, 0, pair, h_rounds[0, 0], q)
-        pair = pair_product(0, 1)
+        pair = pair_product(0, 1, "scaled_b")
         quantise_h(0, 0, 0, HALF)
-        round_w1(1)
         quantise_w1(1)
         for q in range(4):
             triple_product(0, 1, pair, h_rounds[0, 1], q)
         turn_prior()
+        pair = pair_product(1, 0, "scaled_c")
         round_cand(0)
-        pair = pair_product(1, 0)
         quantise_h(0, 1, 0, HALF)
         quantise_cand(0)
         round_cand(1)
+        quantise_cand(1)
         for q in range(4):
             triple_product(1, 0, pair, h_rounds[1, 0], q)
-        quantise_cand(1)
-        pair = pair_product(1, 1)
+        marks = (0, 2, 3, 4, 6)
+        pair = pair_product(1, 1, "share_e", lambda t: score(0, 0, HALF, 1, (), ("scores",), marks[t], marks[t + 1]))
         quantise_h(1, 0, 0, HALF)
-        score(0, 0, HALF, 2, ())
         for q in range(2):
             triple_product(1, 1, pair, h_rounds[1, 1], q)
         triple_product(1, 1, pair, h_rounds[1, 1], 2)
         quantise_h(1, 1, 0, 2 * P)
         triple_product(1, 1, pair, h_rounds[1, 1], 3)
         quantise_h(1, 1, 2 * P, 3 * P)
-        score(1, 0, 2 * P, 6, ())
+        score(1, 0, 2 * P, 6, (), ("x2", "x3"))
         quantise_h(1, 1, 3 * P, 4 * P)
-        score(1, 2 * P, 3 * P, 3, (3,))
-        score(1, 3 * P, 4 * P, 3, (3,))
+        score(1, 2 * P, 3 * P, 3, (3,), ("scores",))
+        score(1, 3 * P, 4 * P, 3, (3,), ("x3", "x1"))

@@ -20,6 +20,7 @@ ACT = mybir.ActivationFunctionType
 
 P = 128
 HALF = 512
+BANKS = 8
 NT = N // P
 
 
@@ -29,54 +30,45 @@ def tile_list_hyper_relational_scoring_kernel(
     nc = tc.nc
     with ExitStack() as ctx:
         keep = ctx.enter_context(tc.tile_pool(name="keep", bufs=1))
-        work = ctx.enter_context(tc.tile_pool(name="work", bufs=2))
-        psum = ctx.enter_context(tc.psum_pool(name="psum", bufs=2))
+        psum = ctx.enter_context(tc.psum_pool(name="psum", bufs=1))
+        taken = []
+
+        def next_bank(groups):
+            tile = psum.tile([P, groups, HALF // groups], F32, name="ps%d" % len(taken), tag="bank%d" % (len(taken) % BANKS))
+            taken.append(tile)
+            return tile
 
         offsets = keep.tile([P, S // 16], U16, name="offsets")
         nc.sync.dma_start(offsets[:], offs)
 
-        tab_rows = keep.tile([P, T], U8, name="tab_rows", tag="share_a", align_bytes=64)
-        w_rows = keep.tile([P, 2, H], U8, name="w_rows", align_bytes=64)
+        tab_rows = keep.tile([P, T], U8, name="tab_rows", align_bytes=64)
+        scale_words = tab_scales[0].bitcast(I32)
+        nc.sync.dma_start(tab_rows[:].bitcast(I32), scale_words.unsqueeze(1).to_broadcast([16, 8, T // 4]))
+        w_rows = keep.tile([16, 2, H // 4], I32, name="w_rows", align_bytes=64)
+        nc.sync.dma_start(w_rows[:, 0, :], w2_scales[0].bitcast(I32))
+        nc.sync.dma_start(w_rows[:, 1, :], w3_scales[0].bitcast(I32))
+        w_plane = keep.tile([P, 2 * H], U8, name="w_plane", align_bytes=64)
+        nc.vector.memset(w_plane[:].bitcast(I32), 0)
 
-        def eightfold(scales):
-            words = scales[0].bitcast(I32)
-            return words.unsqueeze(1).to_broadcast([16, 8, words.shape[1]])
-
-        nc.sync.dma_start(tab_rows[:].bitcast(I32), eightfold(tab_scales))
-        nc.sync.dma_start(w_rows[:, 0, :].bitcast(I32), eightfold(w2_scales))
-        nc.sync.dma_start(w_rows[:, 1, :].bitcast(I32), eightfold(w3_scales))
-
-        table = keep.tile([P, T], I32, name="table", tag="share_e", align_bytes=64)
+        table = keep.tile([P, T], I32, name="table", tag="then_cand_1", align_bytes=64)
         nc.sync.dma_start(table[:], tab_words[0].rearrange("p n t -> p (n t)").bitcast(I32))
-        w2_raw = keep.tile([P, H // 2], I32, name="w2_raw", tag="share_c", align_bytes=64)
+        w2_raw = keep.tile([P, H // 2], I32, name="w2_raw", tag="then_w1_1", align_bytes=64)
         nc.sync.dma_start(w2_raw[:], w2_words[0].bitcast(I32))
-        w3_raw = keep.tile([P, H], I32, name="w3_raw", tag="share_b", align_bytes=64)
+        w3_raw = keep.tile([P, H], I32, name="w3_raw", tag="then_cand_0", align_bytes=64)
         nc.sync.dma_start(w3_raw[:], w3_words[0].rearrange("p n t -> p (n t)").bitcast(I32))
 
-        def load_w1(b, tag):
-            raw = keep.tile([P, 4, HALF], F32, name="w1_raw%d" % b, tag=tag, align_bytes=64)
-            nc.sync.dma_start(raw[:], w1[:, b * HALF : (b + 1) * HALF].rearrange("(p j) c -> p j c", j=4))
-            return raw
-
-
-        vec_rows = keep.tile([P, 3 * P], F32, name="vec_rows", align_bytes=64)
-        nc.vector.memset(vec_rows[:], 0.0)
-        nc.scalar.dma_start(vec_rows[0:4, 0 : 2 * P], rel.rearrange("(i t u) -> t i u", t=4, u=8))
+        vec_rows = keep.tile([P, 2 * P], F32, name="vec_rows", align_bytes=64)
+        nc.gpsimd.memset(vec_rows[:], 0.0)
+        nc.gpsimd.dma_start(vec_rows[0:4, :], rel.rearrange("(i t u) -> t i u", t=4, u=8))
+        nc.gpsimd.dma_start(vec_rows[4 : 4 + NT, 0:P], prior.rearrange("(c p) -> c p", p=P))
         identity = keep.tile([P, P], F32, name="identity", align_bytes=64)
-        nc.vector.memset(identity[:], 0.0)
-        make_identity(nc, identity[:], nomemset=True)
-        nc.gpsimd.dma_start(vec_rows[0:NT, 2 * P :], prior.rearrange("(c p) -> c p", p=P))
-        rel_bank = psum.tile([P, 2, P], F32, name="scores")
+        make_identity(nc, identity[:])
+        turned = next_bank(4)
         for b in range(2):
-            nc.tensor.transpose(rel_bank[:, b, :], vec_rows[:, b * P : (b + 1) * P], identity[:])
-        rel_cols = keep.tile([P, 2, 4], F32, name="rel_cols", align_bytes=64)
-        nc.scalar.copy(rel_cols[:], rel_bank[:, :, 0:4])
-        prior_cols = keep.tile([P, NT], F32, name="prior_cols", align_bytes=64)
-
-        def turn_prior():
-            prior_bank = psum.tile([P, P], F32, name="scores")
-            nc.tensor.transpose(prior_bank[:], vec_rows[:, 2 * P :], identity[:])
-            nc.scalar.copy(prior_cols[:], prior_bank[:, 0:NT])
+            nc.tensor.transpose(turned[:, b, :], vec_rows[:, b * P : (b + 1) * P], identity[:])
+        vec_cols = keep.tile([P, 2, 4 + NT], F32, name="vec_cols", align_bytes=64)
+        nc.scalar.copy(vec_cols[:], turned[:, 0:2, 0 : 4 + NT])
+        prior_cols = vec_cols[:, 0, 4:]
 
         def lists(h):
             return offsets[:, h * (HALF // 16) : (h + 1) * (HALF // 16)]
@@ -85,58 +77,65 @@ def tile_list_hyper_relational_scoring_kernel(
             for q in range(1, 4):
                 nc.sync.dma_start(plane[q:P:32, :].bitcast(I32), plane[8 * q : P : 32, :].bitcast(I32))
 
-        picked0 = keep.tile([P, HALF], U8, name="picked0", align_bytes=64)
-        nc.vector.tensor_copy(picked0[:], tab_rows[:].indirect(lists(0)))
-        plane0 = keep.tile([P, HALF + 2 * H], U8, name="plane0", align_bytes=64)
-        nc.vector.tensor_copy(plane0[:, 0:HALF].bitcast(I32), picked0[:].bitcast(I32))
-        nc.vector.tensor_copy(
-            plane0[:, HALF:].bitcast(I32).rearrange("p (b t i u) -> p b t i u", b=4, t=4, i=16),
-            w_rows[:].rearrange("p w c -> p (w c)").bitcast(I32).rearrange("p (b i t u) -> p b t i u", b=4, t=4, i=16),
-        )
-        settle_rows(plane0)
-        picked1 = keep.tile([P, HALF], U8, name="picked1", tag="share_d", align_bytes=64)
-        nc.vector.tensor_copy(picked1[:], tab_rows[:].indirect(lists(1)))
-        plane1 = keep.tile([P, HALF], U8, name="plane1", align_bytes=64)
-        nc.vector.tensor_copy(plane1[:].bitcast(I32), picked1[:].bitcast(I32))
-        settle_rows(plane1)
-        v_scales = [plane0[:, 0:HALF], plane1[:]]
-        w2_plane = plane0[:, HALF : HALF + H]
-        w3_plane = plane0[:, HALF + H :]
+        def gather_scales(h, plane, tag):
+            picked = keep.tile([P, HALF], U8, name="picked%d" % h, tag=tag, align_bytes=64)
+            nc.vector.tensor_copy(picked[:], tab_rows[:].indirect(lists(h)))
+            nc.vector.tensor_copy(plane[:].bitcast(I32), picked[:].bitcast(I32))
 
-        w1_raw = [load_w1(0, "share_a"), load_w1(1, "share_d")]
-
-        v_words = []
-
-        def gather_words(h, tag):
-            words = keep.tile([P, HALF], I32, name="v_words%d" % h, tag=tag, align_bytes=64)
+        def gather_words(h):
+            words = keep.tile([P, HALF], I32, name="v_words%d" % h, align_bytes=64)
             nc.vector.tensor_copy(words[:].bitcast(U32), table[:].bitcast(U32).indirect(lists(h)))
-            v_words.append(words)
+            return words
 
-        gather_words(0, "v_first")
+        def load_w1(b):
+            raw = keep.tile([P, 4, HALF], F32, name="w1_raw%d" % b, tag="then_w1_%d" % b, align_bytes=64)
+            nc.sync.dma_start(raw[:], w1[:, b * HALF : (b + 1) * HALF].rearrange("(p j) c -> p j c", j=4))
+            return raw
 
+        cand_view = cand.rearrange("(b i t u) n -> b t i u n", b=2, i=16, t=4, u=8)
+
+        def load_cand(b):
+            raw = keep.tile([P, 4, N], F32, name="cand_raw%d" % b, tag="then_cand_%d" % b, align_bytes=64)
+            for t in range(4):
+                nc.sync.dma_start(raw[:, t, :], cand_view[b, t])
+            return raw
+
+        def permute_w3(b):
+            codes = keep.tile([P, HALF], I32, name="w3_codes%d" % b, align_bytes=64)
+            nc.vector.tensor_copy(
+                codes[:].rearrange("p (t i u) -> p t i u", t=4, i=16),
+                w3_raw[:, b * HALF : (b + 1) * HALF].rearrange("p (i t u) -> p t i u", t=4, i=16),
+            )
+            return codes
+
+        w_dealt = keep.tile([16, 2 * H // 4], I32, name="w_dealt", align_bytes=64)
+        nc.vector.tensor_copy(
+            w_dealt[:].rearrange("p (b t i u) -> p b t i u", b=4, t=4, i=16),
+            w_rows[:].rearrange("p w c -> p (w c)").rearrange("p (b i t u) -> p b t i u", b=4, t=4, i=16),
+        )
+        for q in range(4):
+            nc.sync.dma_start(w_plane[q:P:32, :].bitcast(I32), w_dealt[q:16:4, :])
+        w2_plane = w_plane[:, 0:H]
+        w3_plane = w_plane[:, H:]
+        plane0 = keep.tile([P, HALF], U8, name="plane0", align_bytes=64)
+        gather_scales(0, plane0, "then_w1_0")
+        settle_rows(plane0)
+        w1_raw = [load_w1(0)]
+        v_words = [gather_words(0)]
         w2_all = keep.tile([P, H // 2], I32, name="w2_codes", align_bytes=64)
         nc.vector.tensor_copy(
             w2_all[:].rearrange("p (b t i u) -> p b t i u", b=2, t=4, i=16),
             w2_raw[:].rearrange("p (b i t u) -> p b t i u", b=2, t=4, i=16),
         )
-        w2_codes = [w2_all[:, b * HALF // 2 : (b + 1) * HALF // 2] for b in range(2)]
-        w3_codes = []
-        for b in range(2):
-            c3 = keep.tile([P, HALF], I32, name="w3_codes%d" % b, align_bytes=64)
-            nc.vector.tensor_copy(
-                c3[:].rearrange("p (t i u) -> p t i u", t=4, i=16),
-                w3_raw[:, b * HALF : (b + 1) * HALF].rearrange("p (i t u) -> p t i u", t=4, i=16),
-            )
-            w3_codes.append(c3)
-        gather_words(1, "share_c")
-
-        cand_view = cand.rearrange("(b i t u) n -> b t i u n", b=2, i=16, t=4, u=8)
-        cand_raw = []
-        for b, tag in enumerate(("share_b", "share_e")):
-            raw = keep.tile([P, 4, N], F32, name="cand_raw%d" % b, tag=tag, align_bytes=64)
-            for t in range(4):
-                nc.sync.dma_start(raw[:, t, :], cand_view[b, t])
-            cand_raw.append(raw)
+        w1_raw.append(load_w1(1))
+        w3_codes = [permute_w3(b) for b in range(2)]
+        cand_raw = [load_cand(0)]
+        plane1 = keep.tile([P, HALF], U8, name="plane1", align_bytes=64)
+        gather_scales(1, plane1, "picked_last")
+        settle_rows(plane1)
+        v_scales = [plane0[:], plane1[:]]
+        v_words.append(gather_words(1))
+        cand_raw.append(load_cand(1))
 
         w1_codes = [keep.tile([P, HALF], U32, name="w1_codes%d" % b, align_bytes=64) for b in range(2)]
         w1_planes = [keep.tile([P, HALF], U8, name="w1_plane%d" % b, align_bytes=64) for b in range(2)]
@@ -144,68 +143,89 @@ def tile_list_hyper_relational_scoring_kernel(
         cand_planes = [keep.tile([P, N], U8, name="cand_plane%d" % b, align_bytes=64) for b in range(2)]
         w1_round = [keep.tile([P, 4 * HALF], BF16, name="w1_round%d" % b, align_bytes=64) for b in range(2)]
         cand_round = [keep.tile([P, 4 * N], BF16, name="cand_round%d" % b, align_bytes=64) for b in range(2)]
+        scaled, pair, h_codes, h_planes, h_rounds = {}, {}, {}, {}, {}
+        for h in range(2):
+            for b in range(2):
+                h_codes[h, b] = keep.tile([P, HALF], U32, name="h_codes%d%d" % (h, b), align_bytes=64)
+                h_planes[h, b] = keep.tile([P, HALF], U8, name="h_plane%d%d" % (h, b), align_bytes=64)
+                h_rounds[h, b] = keep.tile([P, 4 * HALF], BF16, name="h_round%d%d" % (h, b), align_bytes=64)
 
-        def round_w1(b):
+        def round_w1_vector(b):
             src = w1_raw[b][:].rearrange("p j (i t u) -> p t i j u", i=16, t=4)
             dst = w1_round[b][:].rearrange("p (t i u j) -> p t i j u", i=16, t=4, j=4)
-            if b == 0:
-                nc.vector.tensor_copy(dst, src)
-            else:
-                for t in (0, 2):
-                    nc.scalar.copy(dst[:, t : t + 2], src[:, t : t + 2])
+            nc.vector.tensor_copy(dst, src)
+
+        def round_w1_scalar(b, t):
+            src = w1_raw[b][:].rearrange("p j (i t v e) -> p t i v j e", i=16, t=4, e=2)
+            dst = w1_round[b][:].rearrange("p (t i v e j) -> p t i v j e", i=16, t=4, e=2, j=4)
+            nc.scalar.copy(dst[:, t], src[:, t])
+
+        def round_w1_gpsimd(b, t):
+            src = w1_raw[b][:].rearrange("p j (i t u) -> p t i u j", i=16, t=4)
+            dst = w1_round[b][:].rearrange("p (t i u j) -> p t i u j", i=16, t=4, j=4)
+            nc.gpsimd.tensor_scalar(dst[:, t], src[:, t], 1.0, 0.0, MULT, ADD)
 
         def quantise_w1(b):
             nc.vector.quantize_mx(out=w1_codes[b][:].bitcast(FP8X4), scales=w1_planes[b][:], in_=w1_round[b][:])
 
-        def round_cand(b):
-            for lo in range(0, N, 384):
-                dst = cand_round[b][:, 4 * lo : 4 * (lo + 384)].rearrange("p (c e t) -> p c t e", e=2, t=4)
-                src = cand_raw[b][:, :, lo : lo + 384].rearrange("p t (c e) -> p c t e", e=2)
-                nc.scalar.copy(dst, src)
+        def round_cand_scalar(b, lo, hi):
+            dst = cand_round[b][:, 4 * lo : 4 * hi].rearrange("p (c e t) -> p c t e", e=2, t=4)
+            src = cand_raw[b][:, :, lo:hi].rearrange("p t (c e) -> p c t e", e=2)
+            nc.scalar.copy(dst, src)
 
-        def quantise_cand(b):
-            for lo, hi in ((0, 512), (512, N)):
-                nc.vector.quantize_mx(
-                    out=cand_codes[b][:, lo:hi].bitcast(FP8X4),
-                    scales=cand_planes[b][:, lo:hi],
-                    in_=cand_round[b][:, 4 * lo : 4 * hi],
-                )
+        def round_cand_gpsimd(b, lo, hi):
+            dst = cand_round[b][:, 4 * lo : 4 * hi].rearrange("p (c t) -> p c t", t=4)
+            src = cand_raw[b][:, :, lo:hi].rearrange("p t c -> p c t")
+            nc.gpsimd.tensor_scalar(dst, src, 1.0, 0.0, MULT, ADD)
 
-        def pair_product(h, b, tag, between=None):
-            pair = work.tile([P, 4, HALF], F32, name="pair", bufs=4)
-            scaled = keep.tile([P, 4, HALF], F32, name="scaled%d%d" % (h, b), tag=tag, align_bytes=64)
-            for t in range(4):
-                cols = slice(t * P, (t + 1) * P)
-                wide = slice(b * HALF + t * P, b * HALF + (t + 1) * P)
-                x2 = psum.tile([P, HALF], F32, name="x2")
+        def quantise_cand(b, lo, hi):
+            nc.vector.quantize_mx(
+                out=cand_codes[b][:, lo:hi].bitcast(FP8X4),
+                scales=cand_planes[b][:, lo:hi],
+                in_=cand_round[b][:, 4 * lo : 4 * hi],
+            )
+
+        steps = [(0, 0, HALF, b, t) for b in range(2) for t in range(4)]
+        steps = steps + [(1, lo, 2 * P, b, t) for lo in (0, 2 * P) for b in range(2) for t in (0, 2)]
+
+        def projection(step, codes, plane, fmt):
+            h, lo, width, b, t0 = step
+            bank = next_bank(HALF // width)
+            for g in range(HALF // width):
+                t = t0 + g
                 nc.tensor.matmul_mx(
-                    out=x2[:],
-                    lhsT=w2_codes[b][:, t * P // 2 : (t + 1) * P // 2].bitcast(FP4X4),
-                    lhsT_scale=w2_plane[:, wide],
-                    rhs=v_words[h][:].bitcast(FP8X4),
-                    rhs_scale=v_scales[h],
+                    out=bank[:, g, :],
+                    lhsT=codes(b, t).bitcast(fmt),
+                    lhsT_scale=plane[:, b * HALF + t * P : b * HALF + (t + 1) * P],
+                    rhs=v_words[h][:, lo : lo + width].bitcast(FP8X4),
+                    rhs_scale=v_scales[h][:, lo : lo + width],
                     start=True,
                     stop=True,
                 )
-                x3 = psum.tile([P, HALF], F32, name="x3")
-                nc.tensor.matmul_mx(
-                    out=x3[:],
-                    lhsT=w3_codes[b][:, cols].bitcast(FP8X4),
-                    lhsT_scale=w3_plane[:, wide],
-                    rhs=v_words[h][:].bitcast(FP8X4),
-                    rhs_scale=v_scales[h],
-                    start=True,
-                    stop=True,
-                )
-                nc.scalar.activation(scaled[:, t, :], x2[:], ACT.Copy, scale=rel_cols[:, b, t : t + 1])
-                nc.vector.tensor_tensor(pair[:, t, :], x3[:], scaled[:, t, :], MULT)
-                if between is not None:
-                    between(t)
-            return pair
+            return bank
 
-        def triple_product(h, b, pair, h_round, q):
+        def scale_x2(k):
+            h, lo, width, b, t0 = steps[k]
+            bank = projection(
+                steps[k], lambda b, t: w2_all[:, (4 * b + t) * P // 2 : (4 * b + t + 1) * P // 2], w2_plane, FP4X4
+            )
+            scaled[k] = keep.tile([P, HALF // width, width], F32, name="scaled%d" % k, align_bytes=64)
+            for g in range(HALF // width):
+                nc.scalar.activation(
+                    scaled[k][:, g, :], bank[:, g, :], ACT.Copy, scale=vec_cols[:, b, t0 + g : t0 + g + 1]
+                )
+
+        def pair_product(k):
+            h, lo, width, b, t0 = steps[k]
+            bank = projection(steps[k], lambda b, t: w3_codes[b][:, t * P : (t + 1) * P], w3_plane, FP8X4)
+            if (h, lo, b) not in pair:
+                pair[h, lo, b] = keep.tile([P, 4, width], F32, name="pair%d_%d_%d" % (h, lo, b), align_bytes=64)
+            nc.vector.tensor_tensor(pair[h, lo, b][:, t0 : t0 + HALF // width, :], bank[:], scaled[k][:], MULT)
+
+        def triple_product(h, b, q):
             cols = slice(q * P, (q + 1) * P)
-            x1 = psum.tile([P, 4, P], F32, name="x1")
+            lo = 0 if h == 0 else q // 2 * 2 * P
+            x1 = next_bank(4)
             for t in range(4):
                 nc.tensor.matmul_mx(
                     out=x1[:, t, :],
@@ -217,20 +237,11 @@ def tile_list_hyper_relational_scoring_kernel(
                     stop=True,
                 )
             nc.vector.tensor_tensor(
-                h_round[:, 4 * q * P : 4 * (q + 1) * P].rearrange("p (n e t) -> p n t e", e=2, t=4),
+                h_rounds[h, b][:, 4 * q * P : 4 * (q + 1) * P].rearrange("p (n e t) -> p n t e", e=2, t=4),
                 x1[:].rearrange("p t (n e) -> p n t e", e=2),
-                pair[:, :, cols].rearrange("p t (n e) -> p n t e", e=2),
+                pair[h, lo, b][:, :, q * P - lo : (q + 1) * P - lo].rearrange("p t (n e) -> p n t e", e=2),
                 MULT,
             )
-
-        h_codes = {}
-        h_planes = {}
-        h_rounds = {}
-        for h in range(2):
-            for b in range(2):
-                h_codes[h, b] = keep.tile([P, HALF], U32, name="h_codes%d%d" % (h, b), align_bytes=64)
-                h_planes[h, b] = keep.tile([P, HALF], U8, name="h_plane%d%d" % (h, b), align_bytes=64)
-                h_rounds[h, b] = keep.tile([P, 4 * HALF], BF16, name="h_round%d%d" % (h, b), align_bytes=64)
 
         def quantise_h(h, b, lo, hi):
             nc.vector.quantize_mx(
@@ -241,70 +252,115 @@ def tile_list_hyper_relational_scoring_kernel(
 
         out_view = out.rearrange("(c p) j -> p c j", p=P)
 
-        def score(h, lo, hi, per_store, vector_banks, tags, first=0, last=NT):
-            width = hi - lo
-            per_bank = min(HALF // width, 3)
-            for s0 in range(first, last, per_store):
-                staged = keep.tile([P, per_store, width], F32, name="staged_%d_%d_%d" % (h, lo, s0))
-                for c0 in range(s0, s0 + per_store, per_bank):
-                    bank = psum.tile([P, per_bank, width], F32, name="scores", tag=tags[c0 // per_bank % len(tags)])
-                    for g in range(per_bank):
-                        c = c0 + g
-                        for b in range(2):
-                            nc.tensor.matmul_mx(
-                                out=bank[:, g, :],
-                                lhsT=cand_codes[b][:, c * P : (c + 1) * P].bitcast(FP8X4),
-                                lhsT_scale=cand_planes[b][:, c * P : (c + 1) * P],
-                                rhs=h_codes[h, b][:, lo:hi].bitcast(FP8X4),
-                                rhs_scale=h_planes[h, b][:, lo:hi],
-                                start=(b == 0),
-                                stop=(b == 1),
-                            )
-                    if c0 in vector_banks:
-                        nc.vector.tensor_tensor(
-                            staged[:, c0 - s0 : c0 - s0 + per_bank, :],
-                            bank[:],
-                            prior_cols[:, c0 : c0 + per_bank].unsqueeze(2).to_broadcast([P, per_bank, width]),
-                            ADD,
-                        )
-                    else:
-                        for g in range(per_bank):
-                            c = c0 + g
-                            nc.scalar.activation(
-                                staged[:, c - s0, :], bank[:, g, :], ACT.Identity, bias=prior_cols[:, c : c + 1]
-                            )
-                nc.sync.dma_start(out_view[:, s0 : s0 + per_store, h * HALF + lo : h * HALF + hi], staged[:])
+        def score_passes(bank, h, lo, width, c0, count, b):
+            for g in range(count):
+                c = c0 + g
+                nc.tensor.matmul_mx(
+                    out=bank[:, g, :],
+                    lhsT=cand_codes[b][:, c * P : (c + 1) * P].bitcast(FP8X4),
+                    lhsT_scale=cand_planes[b][:, c * P : (c + 1) * P],
+                    rhs=h_codes[h, b][:, lo : lo + width].bitcast(FP8X4),
+                    rhs_scale=h_planes[h, b][:, lo : lo + width],
+                    start=(b == 0 and g == 0),
+                    stop=(b == 1 and g == count - 1),
+                )
 
-        pair = pair_product(0, 0, "scaled_a")
-        round_w1(0)
+        def add_prior(staged, bank, width, c0, count, on_vector):
+            if on_vector:
+                nc.vector.tensor_tensor(
+                    staged,
+                    bank[:, 0:count, :],
+                    prior_cols[:, c0 : c0 + count].unsqueeze(2).to_broadcast([P, count, width]),
+                    ADD,
+                )
+            else:
+                for g in range(count):
+                    nc.scalar.activation(
+                        staged[:, g, :], bank[:, g, :], ACT.Identity, bias=prior_cols[:, c0 + g : c0 + g + 1]
+                    )
+
+        def score(h, lo, width, c0, count, per_bank, on_vector=False):
+            staged = keep.tile([P, count, width], F32, name="staged_%d_%d_%d" % (h, lo, c0))
+            for g in range(0, count, per_bank):
+                bank = next_bank(HALF // width)
+                for b in range(2):
+                    score_passes(bank, h, lo, width, c0 + g, per_bank, b)
+                add_prior(staged[:, g : g + per_bank, :], bank, width, c0 + g, per_bank, on_vector)
+            nc.sync.dma_start(out_view[:, c0 : c0 + count, h * HALF + lo : h * HALF + lo + width], staged[:])
+
+        scale_x2(0)
+        scale_x2(1)
+        for k in range(4):
+            scale_x2(k + 2)
+            pair_product(k)
+        round_w1_vector(0)
+        scale_x2(6)
+        pair_product(4)
         quantise_w1(0)
-        round_w1(1)
-        for q in range(4):
-            triple_product(0, 0, pair, h_rounds[0, 0], q)
-        pair = pair_product(0, 1, "scaled_b")
-        quantise_h(0, 0, 0, HALF)
+        round_w1_scalar(1, 0)
+        pair_product(5)
+        round_w1_scalar(1, 1)
+        scale_x2(7)
+        triple_product(0, 0, 0)
+        round_w1_scalar(1, 2)
+        pair_product(6)
+        round_w1_scalar(1, 3)
+        triple_product(0, 0, 1)
+        scale_x2(8)
+        triple_product(0, 0, 2)
+        pair_product(7)
+        round_cand_scalar(0, 0, 256)
+        triple_product(0, 0, 3)
         quantise_w1(1)
-        for q in range(4):
-            triple_product(0, 1, pair, h_rounds[0, 1], q)
-        turn_prior()
-        pair = pair_product(1, 0, "scaled_c")
-        round_cand(0)
+        scale_x2(9)
+        pair_product(8)
+        round_cand_scalar(0, 256, 512)
+        triple_product(0, 1, 0)
+        quantise_h(0, 0, 0, HALF)
+        scale_x2(10)
+        triple_product(0, 1, 1)
+        round_cand_scalar(1, 0, 256)
+        pair_product(9)
+        scale_x2(11)
+        triple_product(0, 1, 2)
+        round_cand_scalar(1, 256, 512)
+        triple_product(0, 1, 3)
+        quantise_cand(0, 0, HALF)
+        scale_x2(12)
+        pair_product(10)
+        round_cand_scalar(0, 512, N)
         quantise_h(0, 1, 0, HALF)
-        quantise_cand(0)
-        round_cand(1)
-        quantise_cand(1)
-        for q in range(4):
-            triple_product(1, 0, pair, h_rounds[1, 0], q)
-        marks = (0, 2, 3, 4, 6)
-        pair = pair_product(1, 1, "share_e", lambda t: score(0, 0, HALF, 1, (), ("scores",), marks[t], marks[t + 1]))
-        quantise_h(1, 0, 0, HALF)
-        for q in range(2):
-            triple_product(1, 1, pair, h_rounds[1, 1], q)
-        triple_product(1, 1, pair, h_rounds[1, 1], 2)
+        triple_product(1, 0, 0)
+        quantise_cand(1, 0, HALF)
+        scale_x2(13)
+        pair_product(11)
+        round_cand_scalar(1, 512, N)
+        triple_product(1, 0, 1)
+        quantise_cand(0, HALF, N)
+        scale_x2(14)
+        pair_product(12)
+        score(0, 0, HALF, 0, 2, 1)
+        triple_product(1, 1, 0)
+        quantise_cand(1, HALF, N)
+        scale_x2(15)
+        pair_product(13)
+        score(0, 0, HALF, 2, 2, 1)
+        triple_product(1, 1, 1)
+        quantise_h(1, 0, 0, 2 * P)
+        pair_product(14)
+        score(0, 0, HALF, 4, 2, 1)
+        pair_product(15)
         quantise_h(1, 1, 0, 2 * P)
-        triple_product(1, 1, pair, h_rounds[1, 1], 3)
+        triple_product(1, 0, 2)
+        score(1, 0, 2 * P, 0, 2, 2)
+        triple_product(1, 1, 2)
+        quantise_h(1, 0, 2 * P, 3 * P)
+        score(1, 0, 2 * P, 2, 4, 2)
+        triple_product(1, 0, 3)
         quantise_h(1, 1, 2 * P, 3 * P)
-        score(1, 0, 2 * P, 6, (), ("x2", "x3"))
+        triple_product(1, 1, 3)
+        quantise_h(1, 0, 3 * P, 4 * P)
+        score(1, 2 * P, P, 0, NT, 3)
         quantise_h(1, 1, 3 * P, 4 * P)
-        score(1, 2 * P, 3 * P, 3, (3,), ("scores",))
-        score(1, 3 * P, 4 * P, 3, (3,), ("x3", "x1"))
+        score(1, 3 * P, P, 0, 3, 3)
+        score(1, 3 * P, P, 3, 3, 3, on_vector=True)

@@ -1,7 +1,6 @@
 from contextlib import ExitStack
 
 import concourse.mybir as mybir
-from concourse.masks import make_identity
 
 K, T, S, H, N = 512, 2048, 1024, 1024, 768
 FLOPS = 2 * K * H * S * 3 + 2 * H * N * S
@@ -41,9 +40,12 @@ def tile_list_hyper_relational_scoring_kernel(
         offsets = keep.tile([P, S // 16], U16, name="offsets")
         nc.sync.dma_start(offsets[:], offs)
 
-        tab_rows = keep.tile([P, T], U8, name="tab_rows", align_bytes=64)
+        tab_rows = keep.tile([P, T], U8, name="tab_rows", tag="then_cand_0", align_bytes=64)
         scale_words = tab_scales[0].bitcast(I32)
-        nc.sync.dma_start(tab_rows[:].bitcast(I32), scale_words.unsqueeze(1).to_broadcast([16, 8, T // 4]))
+        for e in range(2):
+            nc.sync.dma_start(
+                tab_rows[e:P:2, :].bitcast(I32), scale_words[e:16:2, :].unsqueeze(1).to_broadcast([8, 8, T // 4])
+            )
         w_rows = keep.tile([16, 2, H // 4], I32, name="w_rows", align_bytes=64)
         nc.sync.dma_start(w_rows[:, 0, :], w2_scales[0].bitcast(I32))
         nc.sync.dma_start(w_rows[:, 1, :], w3_scales[0].bitcast(I32))
@@ -52,43 +54,55 @@ def tile_list_hyper_relational_scoring_kernel(
 
         table = keep.tile([P, T], I32, name="table", tag="then_cand_1", align_bytes=64)
         nc.sync.dma_start(table[:], tab_words[0].rearrange("p n t -> p (n t)").bitcast(I32))
-        w2_raw = keep.tile([P, H // 2], I32, name="w2_raw", tag="then_w1_1", align_bytes=64)
+        w2_raw = keep.tile([P, H // 2], I32, name="w2_raw", tag="then_rel", align_bytes=64)
         nc.sync.dma_start(w2_raw[:], w2_words[0].bitcast(I32))
-        w3_raw = keep.tile([P, H], I32, name="w3_raw", tag="then_cand_0", align_bytes=64)
+        w3_raw = keep.tile([P, H], I32, name="w3_raw", tag="then_second_half", align_bytes=64)
         nc.sync.dma_start(w3_raw[:], w3_words[0].rearrange("p n t -> p (n t)").bitcast(I32))
 
-        vec_rows = keep.tile([P, 2 * P], F32, name="vec_rows", align_bytes=64)
-        nc.gpsimd.memset(vec_rows[:], 0.0)
-        nc.gpsimd.dma_start(vec_rows[0:4, :], rel.rearrange("(i t u) -> t i u", t=4, u=8))
-        nc.gpsimd.dma_start(vec_rows[4 : 4 + NT, 0:P], prior.rearrange("(c p) -> c p", p=P))
-        identity = keep.tile([P, P], F32, name="identity", align_bytes=64)
-        make_identity(nc, identity[:])
-        turned = next_bank(4)
-        for b in range(2):
-            nc.tensor.transpose(turned[:, b, :], vec_rows[:, b * P : (b + 1) * P], identity[:])
-        vec_cols = keep.tile([P, 2, 4 + NT], F32, name="vec_cols", align_bytes=64)
-        nc.scalar.copy(vec_cols[:], turned[:, 0:2, 0 : 4 + NT])
-        prior_cols = vec_cols[:, 0, 4:]
+        rel_rows = keep.tile([P, P], F32, name="rel_rows", align_bytes=64)
+        prior_rows = keep.tile([P, 2 * P], F32, name="prior_rows", align_bytes=64)
+        nc.gpsimd.memset(prior_rows[:], 0.0)
+        nc.scalar.copy(rel_rows[:], prior_rows[:, 0:P])
+        nc.scalar.dma_start(rel_rows[0:P:16, :], rel.rearrange("(b d c) -> d b c", b=2, d=4))
+        nc.gpsimd.dma_start(
+            prior_rows[0:P:32, 0 : 32 * NT].rearrange("d (c a) -> d c a", a=32),
+            prior.rearrange("(c d a) -> d c a", d=4, a=32),
+        )
+
+        def turn_rel():
+            dealt = keep.tile([P, P], F32, name="rel_dealt", tag="then_rel", align_bytes=64)
+            nc.vector.tensor_copy(
+                dealt[:].rearrange("p (t i u) -> p t i u", t=4, i=4),
+                rel_rows[:].rearrange("p (i t u) -> p t i u", t=4, i=4),
+            )
+            turned = keep.tile([P, P], F32, name="rel_turned", align_bytes=64)
+            nc.vector.transpose(turned[:], dealt[:])
+            return turned
+
+        def turn_prior():
+            turned = keep.tile([P, 2 * P], F32, name="prior_turned", tag="then_w1_0", align_bytes=64)
+            nc.vector.transpose(turned[:], prior_rows[:])
+            return turned[:, 0 : 32 * NT : 32]
 
         def lists(h):
             return offsets[:, h * (HALF // 16) : (h + 1) * (HALF // 16)]
 
         def settle_rows(plane):
-            for q in range(1, 4):
-                nc.sync.dma_start(plane[q:P:32, :].bitcast(I32), plane[8 * q : P : 32, :].bitcast(I32))
+            for e in range(2):
+                nc.sync.dma_start(plane[2 + e : P : 32, :].bitcast(I32), plane[16 + e : P : 32, :].bitcast(I32))
 
         def gather_scales(h, plane, tag):
             picked = keep.tile([P, HALF], U8, name="picked%d" % h, tag=tag, align_bytes=64)
             nc.vector.tensor_copy(picked[:], tab_rows[:].indirect(lists(h)))
             nc.vector.tensor_copy(plane[:].bitcast(I32), picked[:].bitcast(I32))
 
-        def gather_words(h):
-            words = keep.tile([P, HALF], I32, name="v_words%d" % h, align_bytes=64)
+        def gather_words(h, tag):
+            words = keep.tile([P, HALF], I32, name="v_words%d" % h, tag=tag, align_bytes=64)
             nc.vector.tensor_copy(words[:].bitcast(U32), table[:].bitcast(U32).indirect(lists(h)))
             return words
 
-        def load_w1(b):
-            raw = keep.tile([P, 4, HALF], F32, name="w1_raw%d" % b, tag="then_w1_%d" % b, align_bytes=64)
+        def load_w1(b, tag):
+            raw = keep.tile([P, 4, HALF], F32, name="w1_raw%d" % b, tag=tag, align_bytes=64)
             nc.sync.dma_start(raw[:], w1[:, b * HALF : (b + 1) * HALF].rearrange("(p j) c -> p j c", j=4))
             return raw
 
@@ -108,7 +122,7 @@ def tile_list_hyper_relational_scoring_kernel(
             )
             return codes
 
-        w_dealt = keep.tile([16, 2 * H // 4], I32, name="w_dealt", align_bytes=64)
+        w_dealt = keep.tile([16, 2 * H // 4], I32, name="w_dealt", tag="then_w1_1", align_bytes=64)
         nc.vector.tensor_copy(
             w_dealt[:].rearrange("p (b t i u) -> p b t i u", b=4, t=4, i=16),
             w_rows[:].rearrange("p w c -> p (w c)").rearrange("p (b i t u) -> p b t i u", b=4, t=4, i=16),
@@ -120,21 +134,22 @@ def tile_list_hyper_relational_scoring_kernel(
         plane0 = keep.tile([P, HALF], U8, name="plane0", align_bytes=64)
         gather_scales(0, plane0, "then_w1_0")
         settle_rows(plane0)
-        w1_raw = [load_w1(0)]
-        v_words = [gather_words(0)]
+        w1_raw = [load_w1(0, "then_w1_0")]
+        v_words = [gather_words(0, "first_half")]
         w2_all = keep.tile([P, H // 2], I32, name="w2_codes", align_bytes=64)
         nc.vector.tensor_copy(
             w2_all[:].rearrange("p (b t i u) -> p b t i u", b=2, t=4, i=16),
             w2_raw[:].rearrange("p (b i t u) -> p b t i u", b=2, t=4, i=16),
         )
-        w1_raw.append(load_w1(1))
+        rel_cols = turn_rel()
+        w1_raw.append(load_w1(1, "then_w1_1"))
         w3_codes = [permute_w3(b) for b in range(2)]
-        cand_raw = [load_cand(0)]
         plane1 = keep.tile([P, HALF], U8, name="plane1", align_bytes=64)
-        gather_scales(1, plane1, "picked_last")
+        gather_scales(1, plane1, "then_second_half")
         settle_rows(plane1)
+        cand_raw = [load_cand(0)]
         v_scales = [plane0[:], plane1[:]]
-        v_words.append(gather_words(1))
+        v_words.append(gather_words(1, "then_second_half"))
         cand_raw.append(load_cand(1))
 
         w1_codes = [keep.tile([P, HALF], U32, name="w1_codes%d" % b, align_bytes=64) for b in range(2)]
@@ -211,9 +226,8 @@ def tile_list_hyper_relational_scoring_kernel(
             )
             scaled[k] = keep.tile([P, HALF // width, width], F32, name="scaled%d" % k, align_bytes=64)
             for g in range(HALF // width):
-                nc.scalar.activation(
-                    scaled[k][:, g, :], bank[:, g, :], ACT.Copy, scale=vec_cols[:, b, t0 + g : t0 + g + 1]
-                )
+                col = 32 * (t0 + g) + 16 * b
+                nc.scalar.activation(scaled[k][:, g, :], bank[:, g, :], ACT.Copy, scale=rel_cols[:, col : col + 1])
 
         def pair_product(k):
             h, lo, width, b, t0 = steps[k]
@@ -288,17 +302,21 @@ def tile_list_hyper_relational_scoring_kernel(
                 add_prior(staged[:, g : g + per_bank, :], bank, width, c0 + g, per_bank, on_vector)
             nc.sync.dma_start(out_view[:, c0 : c0 + count, h * HALF + lo : h * HALF + lo + width], staged[:])
 
+        for t in range(4):
+            round_w1_gpsimd(0, t)
+        for lo in range(0, N, P):
+            round_cand_gpsimd(0, lo, lo + P)
+        for lo in range(HALF, N, P):
+            round_cand_gpsimd(1, lo, lo + P)
         scale_x2(0)
         scale_x2(1)
-        for k in range(4):
+        for k in range(5):
             scale_x2(k + 2)
             pair_product(k)
-        round_w1_vector(0)
-        scale_x2(6)
-        pair_product(4)
         quantise_w1(0)
         round_w1_scalar(1, 0)
         pair_product(5)
+        prior_cols = turn_prior()
         round_w1_scalar(1, 1)
         scale_x2(7)
         triple_product(0, 0, 0)
@@ -309,14 +327,11 @@ def tile_list_hyper_relational_scoring_kernel(
         scale_x2(8)
         triple_product(0, 0, 2)
         pair_product(7)
-        round_cand_scalar(0, 0, 256)
         triple_product(0, 0, 3)
         quantise_w1(1)
         scale_x2(9)
         pair_product(8)
-        round_cand_scalar(0, 256, 512)
         triple_product(0, 1, 0)
-        quantise_h(0, 0, 0, HALF)
         scale_x2(10)
         triple_product(0, 1, 1)
         round_cand_scalar(1, 0, 256)
@@ -325,30 +340,29 @@ def tile_list_hyper_relational_scoring_kernel(
         triple_product(0, 1, 2)
         round_cand_scalar(1, 256, 512)
         triple_product(0, 1, 3)
-        quantise_cand(0, 0, HALF)
         scale_x2(12)
         pair_product(10)
-        round_cand_scalar(0, 512, N)
-        quantise_h(0, 1, 0, HALF)
-        triple_product(1, 0, 0)
-        quantise_cand(1, 0, HALF)
+        quantise_h(0, 0, 0, HALF)
+        quantise_cand(0, 0, HALF)
         scale_x2(13)
+        triple_product(1, 0, 0)
+        quantise_h(0, 1, 0, HALF)
+        quantise_cand(1, 0, HALF)
         pair_product(11)
-        round_cand_scalar(1, 512, N)
+        score(0, 0, HALF, 0, 2, 1)
         triple_product(1, 0, 1)
         quantise_cand(0, HALF, N)
         scale_x2(14)
         pair_product(12)
-        score(0, 0, HALF, 0, 2, 1)
-        triple_product(1, 1, 0)
         quantise_cand(1, HALF, N)
+        score(0, 0, HALF, 2, 2, 1)
+        triple_product(1, 1, 0)
         scale_x2(15)
         pair_product(13)
-        score(0, 0, HALF, 2, 2, 1)
+        score(0, 0, HALF, 4, 2, 1)
         triple_product(1, 1, 1)
         quantise_h(1, 0, 0, 2 * P)
         pair_product(14)
-        score(0, 0, HALF, 4, 2, 1)
         pair_product(15)
         quantise_h(1, 1, 0, 2 * P)
         triple_product(1, 0, 2)

@@ -40,17 +40,15 @@ def tile_list_hyper_relational_scoring_kernel(
         offsets = keep.tile([P, S // 16], U16, name="offsets")
         nc.sync.dma_start(offsets[:], offs)
 
-        tab_rows = keep.tile([P, T], U8, name="tab_rows", tag="then_cand_0", align_bytes=64)
+        tab_rows = keep.tile([P, T], U8, name="tab_rows", align_bytes=64)
         scale_words = tab_scales[0].bitcast(I32)
         for e in range(2):
             nc.sync.dma_start(
                 tab_rows[e:P:2, :].bitcast(I32), scale_words[e:16:2, :].unsqueeze(1).to_broadcast([8, 8, T // 4])
             )
-        w_rows = keep.tile([16, 2, H // 4], I32, name="w_rows", align_bytes=64)
+        w_rows = keep.tile([16, 2, H // 4], I32, name="w_rows", tag="then_w1_0", align_bytes=64)
         nc.sync.dma_start(w_rows[:, 0, :], w2_scales[0].bitcast(I32))
         nc.sync.dma_start(w_rows[:, 1, :], w3_scales[0].bitcast(I32))
-        w_plane = keep.tile([P, 2 * H], U8, name="w_plane", align_bytes=64)
-        nc.vector.memset(w_plane[:].bitcast(I32), 0)
 
         table = keep.tile([P, T], I32, name="table", tag="then_cand_1", align_bytes=64)
         nc.sync.dma_start(table[:], tab_words[0].rearrange("p n t -> p (n t)").bitcast(I32))
@@ -60,41 +58,41 @@ def tile_list_hyper_relational_scoring_kernel(
         nc.sync.dma_start(w3_raw[:], w3_words[0].rearrange("p n t -> p (n t)").bitcast(I32))
 
         rel_rows = keep.tile([P, P], F32, name="rel_rows", align_bytes=64)
-        prior_rows = keep.tile([P, 2 * P], F32, name="prior_rows", align_bytes=64)
-        nc.gpsimd.memset(prior_rows[:], 0.0)
-        nc.scalar.copy(rel_rows[:], prior_rows[:, 0:P])
-        nc.scalar.dma_start(rel_rows[0:P:16, :], rel.rearrange("(b d c) -> d b c", b=2, d=4))
-        nc.gpsimd.dma_start(
-            prior_rows[0:P:32, 0 : 32 * NT].rearrange("d (c a) -> d c a", a=32),
-            prior.rearrange("(c d a) -> d c a", d=4, a=32),
-        )
+        w_plane = keep.tile([P, 2 * H], U8, name="w_plane", align_bytes=64)
+        nc.gpsimd.memset(w_plane[:].bitcast(I32), 0)
+        nc.scalar.copy(rel_rows[:].bitcast(U32), w_plane[:, 0 : 4 * P].bitcast(U32))
+        nc.gpsimd.dma_start(rel_rows[0:P:16, :], rel.rearrange("(b d c) -> d b c", b=2, d=4))
 
         def turn_rel():
-            dealt = keep.tile([P, P], F32, name="rel_dealt", tag="then_rel", align_bytes=64)
-            nc.vector.tensor_copy(
+            dealt = keep.tile([P, P], F32, name="rel_dealt", align_bytes=64)
+            nc.scalar.copy(
                 dealt[:].rearrange("p (t i u) -> p t i u", t=4, i=4),
                 rel_rows[:].rearrange("p (i t u) -> p t i u", t=4, i=4),
             )
-            turned = keep.tile([P, P], F32, name="rel_turned", align_bytes=64)
+            turned = keep.tile([P, P], F32, name="rel_turned", tag="then_rel", align_bytes=64)
             nc.vector.transpose(turned[:], dealt[:])
             return turned
 
-        def turn_prior():
-            turned = keep.tile([P, 2 * P], F32, name="prior_turned", tag="then_w1_0", align_bytes=64)
-            nc.vector.transpose(turned[:], prior_rows[:])
-            return turned[:, 0 : 32 * NT : 32]
+        def load_prior():
+            cols = keep.tile([P, NT], F32, name="prior_cols", tag="then_w1_1", align_bytes=64)
+            with nc.allow_non_contiguous_dma(reason="one prior for each partition and tile of candidates"):
+                nc.sync.dma_start(cols[:], prior.rearrange("(c p) -> p c", p=P))
+            return cols
 
         def lists(h):
             return offsets[:, h * (HALF // 16) : (h + 1) * (HALF // 16)]
 
-        def settle_rows(plane):
-            for e in range(2):
-                nc.sync.dma_start(plane[2 + e : P : 32, :].bitcast(I32), plane[16 + e : P : 32, :].bitcast(I32))
-
-        def gather_scales(h, plane, tag):
+        def gather_scales(h, tag):
             picked = keep.tile([P, HALF], U8, name="picked%d" % h, tag=tag, align_bytes=64)
             nc.vector.tensor_copy(picked[:], tab_rows[:].indirect(lists(h)))
+            return picked
+
+        def settle_scales(h, picked):
+            plane = keep.tile([P, HALF], U8, name="plane%d" % h, align_bytes=64)
             nc.vector.tensor_copy(plane[:].bitcast(I32), picked[:].bitcast(I32))
+            for e in range(2):
+                nc.sync.dma_start(plane[2 + e : P : 32, :].bitcast(I32), picked[16 + e : P : 32, :].bitcast(I32))
+            return plane
 
         def gather_words(h, tag):
             words = keep.tile([P, HALF], I32, name="v_words%d" % h, tag=tag, align_bytes=64)
@@ -122,18 +120,17 @@ def tile_list_hyper_relational_scoring_kernel(
             )
             return codes
 
+        picked0 = gather_scales(0, "then_cand_0")
         w_dealt = keep.tile([16, 2 * H // 4], I32, name="w_dealt", tag="then_w1_1", align_bytes=64)
         nc.vector.tensor_copy(
             w_dealt[:].rearrange("p (b t i u) -> p b t i u", b=4, t=4, i=16),
             w_rows[:].rearrange("p w c -> p (w c)").rearrange("p (b i t u) -> p b t i u", b=4, t=4, i=16),
         )
+        plane0 = settle_scales(0, picked0)
         for q in range(4):
             nc.sync.dma_start(w_plane[q:P:32, :].bitcast(I32), w_dealt[q:16:4, :])
         w2_plane = w_plane[:, 0:H]
         w3_plane = w_plane[:, H:]
-        plane0 = keep.tile([P, HALF], U8, name="plane0", align_bytes=64)
-        gather_scales(0, plane0, "then_w1_0")
-        settle_rows(plane0)
         w1_raw = [load_w1(0, "then_w1_0")]
         v_words = [gather_words(0, "first_half")]
         w2_all = keep.tile([P, H // 2], I32, name="w2_codes", align_bytes=64)
@@ -144,13 +141,9 @@ def tile_list_hyper_relational_scoring_kernel(
         rel_cols = turn_rel()
         w1_raw.append(load_w1(1, "then_w1_1"))
         w3_codes = [permute_w3(b) for b in range(2)]
-        plane1 = keep.tile([P, HALF], U8, name="plane1", align_bytes=64)
-        gather_scales(1, plane1, "then_second_half")
-        settle_rows(plane1)
         cand_raw = [load_cand(0)]
-        v_scales = [plane0[:], plane1[:]]
-        v_words.append(gather_words(1, "then_second_half"))
-        cand_raw.append(load_cand(1))
+        picked1 = gather_scales(1, "then_second_half")
+        v_scales = [plane0[:]]
 
         w1_codes = [keep.tile([P, HALF], U32, name="w1_codes%d" % b, align_bytes=64) for b in range(2)]
         w1_planes = [keep.tile([P, HALF], U8, name="w1_plane%d" % b, align_bytes=64) for b in range(2)]
@@ -236,6 +229,15 @@ def tile_list_hyper_relational_scoring_kernel(
                 pair[h, lo, b] = keep.tile([P, 4, width], F32, name="pair%d_%d_%d" % (h, lo, b), align_bytes=64)
             nc.vector.tensor_tensor(pair[h, lo, b][:, t0 : t0 + HALF // width, :], bank[:], scaled[k][:], MULT)
 
+        def pair_product_gpsimd(k):
+            h, lo, width, b, t0 = steps[k]
+            bank = projection(steps[k], lambda b, t: w3_codes[b][:, t * P : (t + 1) * P], w3_plane, FP8X4)
+            x3 = keep.tile([P, HALF // width, width], F32, name="x3_%d" % k, align_bytes=64)
+            nc.scalar.copy(x3[:], bank[:])
+            if (h, lo, b) not in pair:
+                pair[h, lo, b] = keep.tile([P, 4, width], F32, name="pair%d_%d_%d" % (h, lo, b), align_bytes=64)
+            nc.gpsimd.tensor_tensor(pair[h, lo, b][:, t0 : t0 + HALF // width, :], x3[:], scaled[k][:], MULT)
+
         def triple_product(h, b, q):
             cols = slice(q * P, (q + 1) * P)
             lo = 0 if h == 0 else q // 2 * 2 * P
@@ -293,42 +295,66 @@ def tile_list_hyper_relational_scoring_kernel(
                         staged[:, g, :], bank[:, g, :], ACT.Identity, bias=prior_cols[:, c0 + g : c0 + g + 1]
                     )
 
-        def score(h, lo, width, c0, count, per_bank, on_vector=False):
+        def store(staged, h, lo, width, c0, count):
+            nc.sync.dma_start(out_view[:, c0 : c0 + count, h * HALF + lo : h * HALF + lo + width], staged[:])
+
+        def score(h, lo, width, c0, count, per_bank):
             staged = keep.tile([P, count, width], F32, name="staged_%d_%d_%d" % (h, lo, c0))
             for g in range(0, count, per_bank):
                 bank = next_bank(HALF // width)
                 for b in range(2):
                     score_passes(bank, h, lo, width, c0 + g, per_bank, b)
-                add_prior(staged[:, g : g + per_bank, :], bank, width, c0 + g, per_bank, on_vector)
-            nc.sync.dma_start(out_view[:, c0 : c0 + count, h * HALF + lo : h * HALF + lo + width], staged[:])
+                add_prior(staged[:, g : g + per_bank, :], bank, width, c0 + g, per_bank, False)
+            store(staged, h, lo, width, c0, count)
+
+        def open_scores(q):
+            banks = [next_bank(4) for c0 in (0, 3)]
+            for c0, bank in zip((0, 3), banks):
+                score_passes(bank, 1, q * P, P, c0, 3, 0)
+            return banks
+
+        def close_scores(q, banks):
+            for c0, bank in zip((0, 3), banks):
+                score_passes(bank, 1, q * P, P, c0, 3, 1)
+
+        def finish_scores(q, bank, c0, on_vector):
+            staged = keep.tile([P, 3, P], F32, name="staged_end_%d_%d" % (q, c0))
+            add_prior(staged[:], bank, P, c0, 3, on_vector)
+            store(staged, 1, q * P, P, c0, 3)
 
         for t in range(4):
             round_w1_gpsimd(0, t)
+        scale_x2(0)
+        scale_x2(1)
+        scale_x2(2)
+        pair_product(0)
+        v_scales.append(settle_scales(1, picked1)[:])
+        scale_x2(3)
+        pair_product(1)
+        v_words.append(gather_words(1, "scaled1"))
+        cand_raw.append(load_cand(1))
+        for k in range(2, 4):
+            scale_x2(k + 2)
+            pair_product(k)
+            pair_product_gpsimd(k + 2)
         for lo in range(0, N, P):
             round_cand_gpsimd(0, lo, lo + P)
         for lo in range(HALF, N, P):
             round_cand_gpsimd(1, lo, lo + P)
-        scale_x2(0)
-        scale_x2(1)
-        for k in range(5):
-            scale_x2(k + 2)
-            pair_product(k)
         quantise_w1(0)
-        round_w1_scalar(1, 0)
-        pair_product(5)
-        prior_cols = turn_prior()
-        round_w1_scalar(1, 1)
-        scale_x2(7)
+        for t in range(4):
+            round_w1_scalar(1, t)
+        prior_cols = load_prior()
         triple_product(0, 0, 0)
-        round_w1_scalar(1, 2)
-        pair_product(6)
-        round_w1_scalar(1, 3)
+        scale_x2(6)
         triple_product(0, 0, 1)
-        scale_x2(8)
+        scale_x2(7)
         triple_product(0, 0, 2)
-        pair_product(7)
-        triple_product(0, 0, 3)
         quantise_w1(1)
+        pair_product(6)
+        scale_x2(8)
+        triple_product(0, 0, 3)
+        pair_product(7)
         scale_x2(9)
         pair_product(8)
         triple_product(0, 1, 0)
@@ -375,6 +401,8 @@ def tile_list_hyper_relational_scoring_kernel(
         triple_product(1, 1, 3)
         quantise_h(1, 0, 3 * P, 4 * P)
         score(1, 2 * P, P, 0, NT, 3)
+        last = open_scores(3)
         quantise_h(1, 1, 3 * P, 4 * P)
-        score(1, 3 * P, P, 0, 3, 3)
-        score(1, 3 * P, P, 3, 3, 3, on_vector=True)
+        close_scores(3, last)
+        finish_scores(3, last[0], 0, False)
+        finish_scores(3, last[1], 3, True)

@@ -40,63 +40,45 @@ def tile_list_hyper_relational_scoring_kernel(
         offsets = keep.tile([P, S // 16], U16, name="offsets")
         nc.sync.dma_start(offsets[:], offs)
 
+        w_rows = keep.tile([P, H], U8, name="w_rows", align_bytes=64)
+        for w, scales in enumerate((w2_scales, w3_scales)):
+            nc.sync.dma_start(
+                w_rows[w:32:2, :].bitcast(I32), scales[0].bitcast(I32).rearrange("(d q) c -> q d c", q=4)
+            )
         tab_rows = keep.tile([P, T], U8, name="tab_rows", align_bytes=64)
         scale_words = tab_scales[0].bitcast(I32)
         for e in range(2):
             nc.sync.dma_start(
                 tab_rows[e:P:2, :].bitcast(I32), scale_words[e:16:2, :].unsqueeze(1).to_broadcast([8, 8, T // 4])
             )
-        w_rows = keep.tile([16, 2, H // 4], I32, name="w_rows", tag="then_w1_0", align_bytes=64)
-        nc.sync.dma_start(w_rows[:, 0, :], w2_scales[0].bitcast(I32))
-        nc.sync.dma_start(w_rows[:, 1, :], w3_scales[0].bitcast(I32))
-
-        table = keep.tile([P, T], I32, name="table", tag="then_cand_1", align_bytes=64)
+        table = keep.tile([P, T], I32, name="table", tag="then_prior", align_bytes=64)
         nc.sync.dma_start(table[:], tab_words[0].rearrange("p n t -> p (n t)").bitcast(I32))
-        w2_raw = keep.tile([P, H // 2], I32, name="w2_raw", tag="then_rel", align_bytes=64)
+        w2_raw = keep.tile([P, H // 2], I32, name="w2_raw", align_bytes=64)
         nc.sync.dma_start(w2_raw[:], w2_words[0].bitcast(I32))
-        w3_raw = keep.tile([P, H], I32, name="w3_raw", tag="then_second_half", align_bytes=64)
-        nc.sync.dma_start(w3_raw[:], w3_words[0].rearrange("p n t -> p (n t)").bitcast(I32))
+        w3_view = w3_words[0].rearrange("p n t -> p (n t)").bitcast(I32)
+        w3_raw = []
+        for b, tag in enumerate(("then_second_half", "then_cand_1")):
+            raw = keep.tile([P, HALF], I32, name="w3_raw%d" % b, tag=tag, align_bytes=64)
+            nc.sync.dma_start(raw[:], w3_view[:, b * HALF : (b + 1) * HALF])
+            w3_raw.append(raw)
 
-        rel_rows = keep.tile([P, P], F32, name="rel_rows", align_bytes=64)
+        rel_cols = keep.tile([P, 2, 4], F32, name="rel_cols", align_bytes=64)
+        nc.gpsimd.dma_start(rel_cols[:], rel.rearrange("(b p t) -> p b t", b=2, t=4))
         w_plane = keep.tile([P, 2 * H], U8, name="w_plane", align_bytes=64)
         nc.gpsimd.memset(w_plane[:].bitcast(I32), 0)
-        nc.scalar.copy(rel_rows[:].bitcast(U32), w_plane[:, 0 : 4 * P].bitcast(U32))
-        nc.gpsimd.dma_start(rel_rows[0:P:16, :], rel.rearrange("(b d c) -> d b c", b=2, d=4))
-
-        def turn_rel():
-            dealt = keep.tile([P, P], F32, name="rel_dealt", align_bytes=64)
-            nc.scalar.copy(
-                dealt[:].rearrange("p (t i u) -> p t i u", t=4, i=4),
-                rel_rows[:].rearrange("p (i t u) -> p t i u", t=4, i=4),
-            )
-            turned = keep.tile([P, P], F32, name="rel_turned", tag="then_rel", align_bytes=64)
-            nc.vector.transpose(turned[:], dealt[:])
-            return turned
+        nc.gpsimd.memset(w_rows[32:64, :].bitcast(I32), 0)
+        nc.scalar.copy(w_rows[64:P, :].bitcast(U32), w_plane[64:P, 0:H].bitcast(U32))
 
         def load_prior():
-            cols = keep.tile([P, NT], F32, name="prior_cols", tag="then_w1_1", align_bytes=64)
+            cols = keep.tile([P, NT], F32, name="prior_cols", tag="then_prior", align_bytes=64)
             with nc.allow_non_contiguous_dma(reason="one prior for each partition and tile of candidates"):
                 nc.sync.dma_start(cols[:], prior.rearrange("(c p) -> p c", p=P))
             return cols
 
-        def lists(h):
-            return offsets[:, h * (HALF // 16) : (h + 1) * (HALF // 16)]
-
-        def gather_scales(h, tag):
-            picked = keep.tile([P, HALF], U8, name="picked%d" % h, tag=tag, align_bytes=64)
-            nc.vector.tensor_copy(picked[:], tab_rows[:].indirect(lists(h)))
-            return picked
-
-        def settle_scales(h, picked):
-            plane = keep.tile([P, HALF], U8, name="plane%d" % h, align_bytes=64)
-            nc.vector.tensor_copy(plane[:].bitcast(I32), picked[:].bitcast(I32))
-            for e in range(2):
-                nc.sync.dma_start(plane[2 + e : P : 32, :].bitcast(I32), picked[16 + e : P : 32, :].bitcast(I32))
-            return plane
-
         def gather_words(h, tag):
             words = keep.tile([P, HALF], I32, name="v_words%d" % h, tag=tag, align_bytes=64)
-            nc.vector.tensor_copy(words[:].bitcast(U32), table[:].bitcast(U32).indirect(lists(h)))
+            lists = offsets[:, h * (HALF // 16) : (h + 1) * (HALF // 16)]
+            nc.vector.tensor_copy(words[:].bitcast(U32), table[:].bitcast(U32).indirect(lists))
             return words
 
         def load_w1(b, tag):
@@ -104,46 +86,47 @@ def tile_list_hyper_relational_scoring_kernel(
             nc.sync.dma_start(raw[:], w1[:, b * HALF : (b + 1) * HALF].rearrange("(p j) c -> p j c", j=4))
             return raw
 
-        cand_view = cand.rearrange("(b i t u) n -> b t i u n", b=2, i=16, t=4, u=8)
-
         def load_cand(b):
             raw = keep.tile([P, 4, N], F32, name="cand_raw%d" % b, tag="then_cand_%d" % b, align_bytes=64)
-            for t in range(4):
-                nc.sync.dma_start(raw[:, t, :], cand_view[b, t])
+            nc.sync.dma_start(raw[:], cand[b * HALF : (b + 1) * HALF, :].rearrange("(p j) n -> p j n", j=4))
             return raw
 
         def permute_w3(b):
             codes = keep.tile([P, HALF], I32, name="w3_codes%d" % b, align_bytes=64)
             nc.vector.tensor_copy(
-                codes[:].rearrange("p (t i u) -> p t i u", t=4, i=16),
-                w3_raw[:, b * HALF : (b + 1) * HALF].rearrange("p (i t u) -> p t i u", t=4, i=16),
+                codes[:].rearrange("p (t m) -> p m t", t=4), w3_raw[b][:].rearrange("p (m t) -> p m t", t=4)
             )
             return codes
 
-        picked0 = gather_scales(0, "then_cand_0")
-        w_dealt = keep.tile([16, 2 * H // 4], I32, name="w_dealt", tag="then_w1_1", align_bytes=64)
+        w1_raw = [load_w1(0, "w1_first")]
+        w_dealt = keep.tile([P, H], U8, name="w_dealt", tag="then_w1_1", align_bytes=64)
         nc.vector.tensor_copy(
-            w_dealt[:].rearrange("p (b t i u) -> p b t i u", b=4, t=4, i=16),
-            w_rows[:].rearrange("p w c -> p (w c)").rearrange("p (b i t u) -> p b t i u", b=4, t=4, i=16),
+            w_dealt[:].rearrange("p (b t m) -> p b t m", b=2, t=4),
+            w_rows[:].rearrange("p (b m t) -> p b t m", b=2, t=4),
         )
-        plane0 = settle_scales(0, picked0)
+        w_planes = w_plane[:].bitcast(I32).rearrange("p (w c) -> p w c", w=2)
         for q in range(4):
-            nc.sync.dma_start(w_plane[q:P:32, :].bitcast(I32), w_dealt[q:16:4, :])
+            nc.scalar.dma_start(w_planes[q:P:32], w_dealt[8 * q : 8 * q + 8, :].bitcast(I32))
         w2_plane = w_plane[:, 0:H]
         w3_plane = w_plane[:, H:]
-        w1_raw = [load_w1(0, "then_w1_0")]
+        picked = keep.tile([P, S], U8, name="picked", tag="then_cand_0", align_bytes=64)
+        nc.vector.tensor_copy(picked[:], tab_rows[:].indirect(offsets[:]))
+        v_plane = keep.tile([P, S], U8, name="v_plane", align_bytes=64)
+        nc.vector.tensor_copy(v_plane[:].bitcast(I32), picked[:].bitcast(I32))
+        for e in range(2):
+            nc.scalar.dma_start(v_plane[2 + e : P : 32, :].bitcast(I32), picked[16 + e : P : 32, :].bitcast(I32))
+        v_scales = [v_plane[:, 0:HALF], v_plane[:, HALF:]]
         v_words = [gather_words(0, "first_half")]
         w2_all = keep.tile([P, H // 2], I32, name="w2_codes", align_bytes=64)
         nc.vector.tensor_copy(
-            w2_all[:].rearrange("p (b t i u) -> p b t i u", b=2, t=4, i=16),
-            w2_raw[:].rearrange("p (b i t u) -> p b t i u", b=2, t=4, i=16),
+            w2_all[:].bitcast(U16).rearrange("p (b t m) -> p b t m", b=2, t=4),
+            w2_raw[:].bitcast(U16).rearrange("p (b m t) -> p b t m", b=2, t=4),
         )
-        rel_cols = turn_rel()
         w1_raw.append(load_w1(1, "then_w1_1"))
-        w3_codes = [permute_w3(b) for b in range(2)]
-        cand_raw = [load_cand(0)]
-        picked1 = gather_scales(1, "then_second_half")
-        v_scales = [plane0[:]]
+        w3_codes = [permute_w3(0)]
+        v_words.append(gather_words(1, "then_second_half"))
+        w3_codes.append(permute_w3(1))
+        cand_raw = [load_cand(b) for b in range(2)]
 
         w1_codes = [keep.tile([P, HALF], U32, name="w1_codes%d" % b, align_bytes=64) for b in range(2)]
         w1_planes = [keep.tile([P, HALF], U8, name="w1_plane%d" % b, align_bytes=64) for b in range(2)]
@@ -158,19 +141,15 @@ def tile_list_hyper_relational_scoring_kernel(
                 h_planes[h, b] = keep.tile([P, HALF], U8, name="h_plane%d%d" % (h, b), align_bytes=64)
                 h_rounds[h, b] = keep.tile([P, 4 * HALF], BF16, name="h_round%d%d" % (h, b), align_bytes=64)
 
-        def round_w1_vector(b):
-            src = w1_raw[b][:].rearrange("p j (i t u) -> p t i j u", i=16, t=4)
-            dst = w1_round[b][:].rearrange("p (t i u j) -> p t i j u", i=16, t=4, j=4)
-            nc.vector.tensor_copy(dst, src)
-
-        def round_w1_scalar(b, t):
-            src = w1_raw[b][:].rearrange("p j (i t v e) -> p t i v j e", i=16, t=4, e=2)
-            dst = w1_round[b][:].rearrange("p (t i v e j) -> p t i v j e", i=16, t=4, e=2, j=4)
-            nc.scalar.copy(dst[:, t], src[:, t])
+        def round_w1_scalar(b, quarter):
+            src = w1_raw[b][:].rearrange("p j (m t) -> p m j t", t=4)
+            dst = w1_round[b][:].rearrange("p (t m j) -> p m j t", t=4, j=4)
+            rows = slice(32 * quarter, 32 * quarter + 32)
+            nc.scalar.copy(dst[:, rows], src[:, rows])
 
         def round_w1_gpsimd(b, t):
-            src = w1_raw[b][:].rearrange("p j (i t u) -> p t i u j", i=16, t=4)
-            dst = w1_round[b][:].rearrange("p (t i u j) -> p t i u j", i=16, t=4, j=4)
+            src = w1_raw[b][:].rearrange("p j (m t) -> p t m j", t=4)
+            dst = w1_round[b][:].rearrange("p (t m j) -> p t m j", t=4, j=4)
             nc.gpsimd.tensor_scalar(dst[:, t], src[:, t], 1.0, 0.0, MULT, ADD)
 
         def quantise_w1(b):
@@ -219,8 +198,8 @@ def tile_list_hyper_relational_scoring_kernel(
             )
             scaled[k] = keep.tile([P, HALF // width, width], F32, name="scaled%d" % k, align_bytes=64)
             for g in range(HALF // width):
-                col = 32 * (t0 + g) + 16 * b
-                nc.scalar.activation(scaled[k][:, g, :], bank[:, g, :], ACT.Copy, scale=rel_cols[:, col : col + 1])
+                t = t0 + g
+                nc.scalar.activation(scaled[k][:, g, :], bank[:, g, :], ACT.Copy, scale=rel_cols[:, b, t : t + 1])
 
         def pair_product(k):
             h, lo, width, b, t0 = steps[k]
@@ -328,11 +307,8 @@ def tile_list_hyper_relational_scoring_kernel(
         scale_x2(1)
         scale_x2(2)
         pair_product(0)
-        v_scales.append(settle_scales(1, picked1)[:])
         scale_x2(3)
         pair_product(1)
-        v_words.append(gather_words(1, "scaled1"))
-        cand_raw.append(load_cand(1))
         for k in range(2, 4):
             scale_x2(k + 2)
             pair_product(k)

@@ -40,7 +40,7 @@ def tile_list_hyper_relational_scoring_kernel(
         offsets = keep.tile([P, S // 16], U16, name="offsets")
         nc.sync.dma_start(offsets[:], offs)
 
-        w_rows = keep.tile([P, H], U8, name="w_rows", align_bytes=64)
+        w_rows = keep.tile([P, H], U8, name="w_rows", tag="then_w3", align_bytes=64)
         for w, scales in enumerate((w2_scales, w3_scales)):
             nc.sync.dma_start(
                 w_rows[w:32:2, :].bitcast(I32), scales[0].bitcast(I32).rearrange("(d q) c -> q d c", q=4)
@@ -51,26 +51,20 @@ def tile_list_hyper_relational_scoring_kernel(
             nc.sync.dma_start(
                 tab_rows[e:P:2, :].bitcast(I32), scale_words[e:16:2, :].unsqueeze(1).to_broadcast([8, 8, T // 4])
             )
-        table = keep.tile([P, T], I32, name="table", tag="then_prior", align_bytes=64)
-        nc.sync.dma_start(table[:], tab_words[0].rearrange("p n t -> p (n t)").bitcast(I32))
-        w2_raw = keep.tile([P, H // 2], I32, name="w2_raw", align_bytes=64)
+        w2_raw = keep.tile([P, H // 2], I32, name="w2_raw", tag="then_w1_0", align_bytes=64)
         nc.sync.dma_start(w2_raw[:], w2_words[0].bitcast(I32))
-        w3_view = w3_words[0].rearrange("p n t -> p (n t)").bitcast(I32)
-        w3_raw = []
-        for b, tag in enumerate(("then_second_half", "then_cand_1")):
-            raw = keep.tile([P, HALF], I32, name="w3_raw%d" % b, tag=tag, align_bytes=64)
-            nc.sync.dma_start(raw[:], w3_view[:, b * HALF : (b + 1) * HALF])
-            w3_raw.append(raw)
-
+        table = keep.tile([P, T], I32, name="table", tag="then_cand_1", align_bytes=64)
+        nc.sync.dma_start(table[:], tab_words[0].rearrange("p n t -> p (n t)").bitcast(I32))
         rel_cols = keep.tile([P, 2, 4], F32, name="rel_cols", align_bytes=64)
-        nc.gpsimd.dma_start(rel_cols[:], rel.rearrange("(b p t) -> p b t", b=2, t=4))
+        nc.sync.dma_start(rel_cols[:], rel.rearrange("(b p t) -> p b t", b=2, t=4))
+
         w_plane = keep.tile([P, 2 * H], U8, name="w_plane", align_bytes=64)
-        nc.gpsimd.memset(w_plane[:].bitcast(I32), 0)
-        nc.gpsimd.memset(w_rows[32:64, :].bitcast(I32), 0)
+        nc.vector.memset(w_plane[:].bitcast(I32), 0)
+        nc.vector.memset(w_rows[32:64, :].bitcast(I32), 0)
         nc.scalar.copy(w_rows[64:P, :].bitcast(U32), w_plane[64:P, 0:H].bitcast(U32))
 
         def load_prior():
-            cols = keep.tile([P, NT], F32, name="prior_cols", tag="then_prior", align_bytes=64)
+            cols = keep.tile([P, NT], F32, name="prior_cols", tag="then_w1_0", align_bytes=64)
             with nc.allow_non_contiguous_dma(reason="one prior for each partition and tile of candidates"):
                 nc.sync.dma_start(cols[:], prior.rearrange("(c p) -> p c", p=P))
             return cols
@@ -81,8 +75,8 @@ def tile_list_hyper_relational_scoring_kernel(
             nc.vector.tensor_copy(words[:].bitcast(U32), table[:].bitcast(U32).indirect(lists))
             return words
 
-        def load_w1(b, tag):
-            raw = keep.tile([P, 4, HALF], F32, name="w1_raw%d" % b, tag=tag, align_bytes=64)
+        def load_w1(b):
+            raw = keep.tile([P, 4, HALF], F32, name="w1_raw%d" % b, tag="then_w1_%d" % b, align_bytes=64)
             nc.sync.dma_start(raw[:], w1[:, b * HALF : (b + 1) * HALF].rearrange("(p j) c -> p j c", j=4))
             return raw
 
@@ -91,14 +85,6 @@ def tile_list_hyper_relational_scoring_kernel(
             nc.sync.dma_start(raw[:], cand[b * HALF : (b + 1) * HALF, :].rearrange("(p j) n -> p j n", j=4))
             return raw
 
-        def permute_w3(b):
-            codes = keep.tile([P, HALF], I32, name="w3_codes%d" % b, align_bytes=64)
-            nc.vector.tensor_copy(
-                codes[:].rearrange("p (t m) -> p m t", t=4), w3_raw[b][:].rearrange("p (m t) -> p m t", t=4)
-            )
-            return codes
-
-        w1_raw = [load_w1(0, "w1_first")]
         w_dealt = keep.tile([P, H], U8, name="w_dealt", tag="then_w1_1", align_bytes=64)
         nc.vector.tensor_copy(
             w_dealt[:].rearrange("p (b t m) -> p b t m", b=2, t=4),
@@ -106,26 +92,32 @@ def tile_list_hyper_relational_scoring_kernel(
         )
         w_planes = w_plane[:].bitcast(I32).rearrange("p (w c) -> p w c", w=2)
         for q in range(4):
-            nc.scalar.dma_start(w_planes[q:P:32], w_dealt[8 * q : 8 * q + 8, :].bitcast(I32))
+            nc.sync.dma_start(w_planes[q:P:32], w_dealt[8 * q : 8 * q + 8, :].bitcast(I32))
         w2_plane = w_plane[:, 0:H]
         w3_plane = w_plane[:, H:]
+        w3_raw = keep.tile([P, H], I32, name="w3_raw", tag="then_w3", align_bytes=64)
+        nc.sync.dma_start(w3_raw[:], w3_words[0].rearrange("p n t -> p (n t)").bitcast(I32))
         picked = keep.tile([P, S], U8, name="picked", tag="then_cand_0", align_bytes=64)
         nc.vector.tensor_copy(picked[:], tab_rows[:].indirect(offsets[:]))
         v_plane = keep.tile([P, S], U8, name="v_plane", align_bytes=64)
         nc.vector.tensor_copy(v_plane[:].bitcast(I32), picked[:].bitcast(I32))
         for e in range(2):
-            nc.scalar.dma_start(v_plane[2 + e : P : 32, :].bitcast(I32), picked[16 + e : P : 32, :].bitcast(I32))
+            nc.sync.dma_start(v_plane[2 + e : P : 32, :].bitcast(I32), picked[16 + e : P : 32, :].bitcast(I32))
         v_scales = [v_plane[:, 0:HALF], v_plane[:, HALF:]]
-        v_words = [gather_words(0, "first_half")]
         w2_all = keep.tile([P, H // 2], I32, name="w2_codes", align_bytes=64)
         nc.vector.tensor_copy(
             w2_all[:].bitcast(U16).rearrange("p (b t m) -> p b t m", b=2, t=4),
             w2_raw[:].bitcast(U16).rearrange("p (b m t) -> p b t m", b=2, t=4),
         )
-        w1_raw.append(load_w1(1, "then_w1_1"))
-        w3_codes = [permute_w3(0)]
-        v_words.append(gather_words(1, "then_second_half"))
-        w3_codes.append(permute_w3(1))
+        w1_raw = [load_w1(b) for b in range(2)]
+        v_words = [gather_words(0, "first_half")]
+        w3_all = keep.tile([P, H], I32, name="w3_codes", align_bytes=64)
+        nc.vector.tensor_copy(
+            w3_all[:].rearrange("p (b t m) -> p b m t", b=2, t=4),
+            w3_raw[:].rearrange("p (b m t) -> p b m t", b=2, t=4),
+        )
+        w3_codes = [w3_all[:, 0:HALF], w3_all[:, HALF:]]
+        v_words.append(gather_words(1, "then_w3"))
         cand_raw = [load_cand(b) for b in range(2)]
 
         w1_codes = [keep.tile([P, HALF], U32, name="w1_codes%d" % b, align_bytes=64) for b in range(2)]
@@ -141,29 +133,18 @@ def tile_list_hyper_relational_scoring_kernel(
                 h_planes[h, b] = keep.tile([P, HALF], U8, name="h_plane%d%d" % (h, b), align_bytes=64)
                 h_rounds[h, b] = keep.tile([P, 4 * HALF], BF16, name="h_round%d%d" % (h, b), align_bytes=64)
 
-        def round_w1_scalar(b, quarter):
+        def round_w1(engine, b, lo, hi):
             src = w1_raw[b][:].rearrange("p j (m t) -> p m j t", t=4)
             dst = w1_round[b][:].rearrange("p (t m j) -> p m j t", t=4, j=4)
-            rows = slice(32 * quarter, 32 * quarter + 32)
-            nc.scalar.copy(dst[:, rows], src[:, rows])
-
-        def round_w1_gpsimd(b, t):
-            src = w1_raw[b][:].rearrange("p j (m t) -> p t m j", t=4)
-            dst = w1_round[b][:].rearrange("p (t m j) -> p t m j", t=4, j=4)
-            nc.gpsimd.tensor_scalar(dst[:, t], src[:, t], 1.0, 0.0, MULT, ADD)
+            engine(dst[:, lo:hi], src[:, lo:hi])
 
         def quantise_w1(b):
             nc.vector.quantize_mx(out=w1_codes[b][:].bitcast(FP8X4), scales=w1_planes[b][:], in_=w1_round[b][:])
 
-        def round_cand_scalar(b, lo, hi):
-            dst = cand_round[b][:, 4 * lo : 4 * hi].rearrange("p (c e t) -> p c t e", e=2, t=4)
-            src = cand_raw[b][:, :, lo:hi].rearrange("p t (c e) -> p c t e", e=2)
-            nc.scalar.copy(dst, src)
-
-        def round_cand_gpsimd(b, lo, hi):
-            dst = cand_round[b][:, 4 * lo : 4 * hi].rearrange("p (c t) -> p c t", t=4)
-            src = cand_raw[b][:, :, lo:hi].rearrange("p t c -> p c t")
-            nc.gpsimd.tensor_scalar(dst, src, 1.0, 0.0, MULT, ADD)
+        def round_cand(engine, b, lo, hi):
+            dst = cand_round[b][:, 4 * lo : 4 * hi].rearrange("p (c e t) -> p c t e", e=4, t=4)
+            src = cand_raw[b][:, :, lo:hi].rearrange("p t (c e) -> p c t e", e=4)
+            engine(dst, src)
 
         def quantise_cand(b, lo, hi):
             nc.vector.quantize_mx(
@@ -207,15 +188,6 @@ def tile_list_hyper_relational_scoring_kernel(
             if (h, lo, b) not in pair:
                 pair[h, lo, b] = keep.tile([P, 4, width], F32, name="pair%d_%d_%d" % (h, lo, b), align_bytes=64)
             nc.vector.tensor_tensor(pair[h, lo, b][:, t0 : t0 + HALF // width, :], bank[:], scaled[k][:], MULT)
-
-        def pair_product_gpsimd(k):
-            h, lo, width, b, t0 = steps[k]
-            bank = projection(steps[k], lambda b, t: w3_codes[b][:, t * P : (t + 1) * P], w3_plane, FP8X4)
-            x3 = keep.tile([P, HALF // width, width], F32, name="x3_%d" % k, align_bytes=64)
-            nc.scalar.copy(x3[:], bank[:])
-            if (h, lo, b) not in pair:
-                pair[h, lo, b] = keep.tile([P, 4, width], F32, name="pair%d_%d_%d" % (h, lo, b), align_bytes=64)
-            nc.gpsimd.tensor_tensor(pair[h, lo, b][:, t0 : t0 + HALF // width, :], x3[:], scaled[k][:], MULT)
 
         def triple_product(h, b, q):
             cols = slice(q * P, (q + 1) * P)
@@ -301,72 +273,68 @@ def tile_list_hyper_relational_scoring_kernel(
             add_prior(staged[:], bank, P, c0, 3, on_vector)
             store(staged, 1, q * P, P, c0, 3)
 
-        for t in range(4):
-            round_w1_gpsimd(0, t)
+        on_scalar, on_vector = nc.scalar.copy, nc.vector.tensor_copy
         scale_x2(0)
         scale_x2(1)
         scale_x2(2)
         pair_product(0)
         scale_x2(3)
         pair_product(1)
-        for k in range(2, 4):
-            scale_x2(k + 2)
-            pair_product(k)
-            pair_product_gpsimd(k + 2)
-        for lo in range(0, N, P):
-            round_cand_gpsimd(0, lo, lo + P)
-        for lo in range(HALF, N, P):
-            round_cand_gpsimd(1, lo, lo + P)
+        round_w1(on_scalar, 0, 0, 64)
+        pair_product(2)
+        pair_product(3)
+        round_w1(on_vector, 0, 64, P)
+        scale_x2(4)
         quantise_w1(0)
-        for t in range(4):
-            round_w1_scalar(1, t)
         prior_cols = load_prior()
-        triple_product(0, 0, 0)
-        scale_x2(6)
-        triple_product(0, 0, 1)
-        scale_x2(7)
-        triple_product(0, 0, 2)
+        for q in range(4):
+            if q < 3:
+                scale_x2(5 + q)
+            triple_product(0, 0, q)
+        round_w1(on_scalar, 1, 0, 64)
+        round_w1(on_scalar, 1, 64, P)
+        for k in range(4, 8):
+            pair_product(k)
         quantise_w1(1)
-        pair_product(6)
-        scale_x2(8)
-        triple_product(0, 0, 3)
-        pair_product(7)
-        scale_x2(9)
-        pair_product(8)
+        for lo in range(0, N, 2 * P):
+            round_cand(on_scalar, 0, lo, lo + 2 * P)
         triple_product(0, 1, 0)
-        scale_x2(10)
-        triple_product(0, 1, 1)
-        round_cand_scalar(1, 0, 256)
-        pair_product(9)
-        scale_x2(11)
-        triple_product(0, 1, 2)
-        round_cand_scalar(1, 256, 512)
-        triple_product(0, 1, 3)
-        scale_x2(12)
-        pair_product(10)
         quantise_h(0, 0, 0, HALF)
-        quantise_cand(0, 0, HALF)
-        scale_x2(13)
-        triple_product(1, 0, 0)
+        for q in range(1, 4):
+            triple_product(0, 1, q)
+        scale_x2(8)
+        scale_x2(9)
+        round_cand(on_vector, 1, HALF, N)
         quantise_h(0, 1, 0, HALF)
-        quantise_cand(1, 0, HALF)
-        pair_product(11)
-        score(0, 0, HALF, 0, 2, 1)
-        triple_product(1, 0, 1)
+        quantise_cand(0, 0, HALF)
+        round_cand(on_scalar, 1, 0, 256)
+        round_cand(on_scalar, 1, 256, HALF)
+        pair_product(8)
         quantise_cand(0, HALF, N)
+        pair_product(9)
+        quantise_cand(1, HALF, N)
+        scale_x2(10)
+        scale_x2(11)
+        triple_product(1, 0, 0)
+        quantise_cand(1, 0, HALF)
+        triple_product(1, 0, 1)
+        score(0, 0, HALF, 0, 2, 1)
+        pair_product(10)
+        scale_x2(12)
+        pair_product(11)
+        scale_x2(13)
+        triple_product(1, 1, 0)
+        score(0, 0, HALF, 2, 2, 1)
+        triple_product(1, 1, 1)
+        quantise_h(1, 0, 0, 2 * P)
         scale_x2(14)
         pair_product(12)
-        quantise_cand(1, HALF, N)
-        score(0, 0, HALF, 2, 2, 1)
-        triple_product(1, 1, 0)
+        quantise_h(1, 1, 0, 2 * P)
         scale_x2(15)
         pair_product(13)
         score(0, 0, HALF, 4, 2, 1)
-        triple_product(1, 1, 1)
-        quantise_h(1, 0, 0, 2 * P)
         pair_product(14)
         pair_product(15)
-        quantise_h(1, 1, 0, 2 * P)
         triple_product(1, 0, 2)
         score(1, 0, 2 * P, 0, 2, 2)
         triple_product(1, 1, 2)

@@ -39,25 +39,26 @@ def tile_list_hyper_relational_scoring_kernel(
 
         offsets = keep.tile([P, S // 16], U16, name="offsets")
         nc.sync.dma_start(offsets[:], offs)
-
-        w_rows = keep.tile([P, H], U8, name="w_rows", tag="then_w3", align_bytes=64)
-        for w, scales in enumerate((w2_scales, w3_scales)):
-            nc.sync.dma_start(
-                w_rows[w:32:2, :].bitcast(I32), scales[0].bitcast(I32).rearrange("(d q) c -> q d c", q=4)
-            )
-        tab_rows = keep.tile([P, T], U8, name="tab_rows", align_bytes=64)
+        tab_rows = keep.tile([P, T], U8, name="tab_rows", tag="then_second_words", align_bytes=64)
         scale_words = tab_scales[0].bitcast(I32)
         for e in range(2):
             nc.sync.dma_start(
                 tab_rows[e:P:2, :].bitcast(I32), scale_words[e:16:2, :].unsqueeze(1).to_broadcast([8, 8, T // 4])
             )
+        w_rows = keep.tile([P, H], U8, name="w_rows", align_bytes=64)
+        for w, scales in enumerate((w2_scales, w3_scales)):
+            nc.sync.dma_start(
+                w_rows[w:32:2, :].bitcast(I32), scales[0].bitcast(I32).rearrange("(d q) c -> q d c", q=4)
+            )
         w2_raw = keep.tile([P, H // 2], I32, name="w2_raw", tag="then_w1_0", align_bytes=64)
         nc.sync.dma_start(w2_raw[:], w2_words[0].bitcast(I32))
-        table = keep.tile([P, T], I32, name="table", tag="then_cand_1", align_bytes=64)
+        table = keep.tile([P, T], I32, name="table", tag="gpsimd_turn", align_bytes=64)
         nc.sync.dma_start(table[:], tab_words[0].rearrange("p n t -> p (n t)").bitcast(I32))
-        rel_cols = keep.tile([P, 2, 4], F32, name="rel_cols", align_bytes=64)
-        nc.sync.dma_start(rel_cols[:], rel.rearrange("(b p t) -> p b t", b=2, t=4))
+        w3_raw = keep.tile([P, H], I32, name="w3_raw", tag="then_second_half", align_bytes=64)
+        nc.sync.dma_start(w3_raw[:], w3_words[0].rearrange("p n t -> p (n t)").bitcast(I32))
 
+        rel_cols = keep.tile([P, 2, 4], F32, name="rel_cols", align_bytes=64)
+        nc.gpsimd.dma_start(rel_cols[:], rel.rearrange("(b p t) -> p b t", b=2, t=4))
         w_plane = keep.tile([P, 2 * H], U8, name="w_plane", align_bytes=64)
         nc.vector.memset(w_plane[:].bitcast(I32), 0)
         nc.vector.memset(w_rows[32:64, :].bitcast(I32), 0)
@@ -69,10 +70,21 @@ def tile_list_hyper_relational_scoring_kernel(
                 nc.sync.dma_start(cols[:], prior.rearrange("(c p) -> p c", p=P))
             return cols
 
+        def lists(h):
+            return offsets[:, h * (HALF // 16) : (h + 1) * (HALF // 16)]
+
+        def gather_scales(h, tag, queue):
+            picked = keep.tile([P, HALF], U8, name="picked%d" % h, tag=tag, align_bytes=64)
+            nc.vector.tensor_copy(picked[:], tab_rows[:].indirect(lists(h)))
+            plane = keep.tile([P, HALF], U8, name="v_plane%d" % h, align_bytes=64)
+            nc.vector.tensor_copy(plane[:].bitcast(I32), picked[:].bitcast(I32))
+            for e in range(2):
+                queue.dma_start(plane[2 + e : P : 32, :].bitcast(I32), picked[16 + e : P : 32, :].bitcast(I32))
+            return plane
+
         def gather_words(h, tag):
             words = keep.tile([P, HALF], I32, name="v_words%d" % h, tag=tag, align_bytes=64)
-            lists = offsets[:, h * (HALF // 16) : (h + 1) * (HALF // 16)]
-            nc.vector.tensor_copy(words[:].bitcast(U32), table[:].bitcast(U32).indirect(lists))
+            nc.vector.tensor_copy(words[:].bitcast(U32), table[:].bitcast(U32).indirect(lists(h)))
             return words
 
         def load_w1(b):
@@ -80,30 +92,22 @@ def tile_list_hyper_relational_scoring_kernel(
             nc.sync.dma_start(raw[:], w1[:, b * HALF : (b + 1) * HALF].rearrange("(p j) c -> p j c", j=4))
             return raw
 
-        def load_cand(b):
-            raw = keep.tile([P, 4, N], F32, name="cand_raw%d" % b, tag="then_cand_%d" % b, align_bytes=64)
+        def load_cand(b, tag):
+            raw = keep.tile([P, 4, N], F32, name="cand_raw%d" % b, tag=tag, align_bytes=64)
             nc.sync.dma_start(raw[:], cand[b * HALF : (b + 1) * HALF, :].rearrange("(p j) n -> p j n", j=4))
             return raw
 
-        w_dealt = keep.tile([P, H], U8, name="w_dealt", tag="then_w1_1", align_bytes=64)
+        v_scales = [gather_scales(0, "then_w1_1", nc.scalar)]
+        w_dealt = keep.tile([P, H], U8, name="w_dealt", tag="then_cand_0", align_bytes=64)
         nc.vector.tensor_copy(
             w_dealt[:].rearrange("p (b t m) -> p b t m", b=2, t=4),
             w_rows[:].rearrange("p (b m t) -> p b t m", b=2, t=4),
         )
         w_planes = w_plane[:].bitcast(I32).rearrange("p (w c) -> p w c", w=2)
         for q in range(4):
-            nc.sync.dma_start(w_planes[q:P:32], w_dealt[8 * q : 8 * q + 8, :].bitcast(I32))
+            nc.scalar.dma_start(w_planes[q:P:32], w_dealt[8 * q : 8 * q + 8, :].bitcast(I32))
         w2_plane = w_plane[:, 0:H]
         w3_plane = w_plane[:, H:]
-        w3_raw = keep.tile([P, H], I32, name="w3_raw", tag="then_w3", align_bytes=64)
-        nc.sync.dma_start(w3_raw[:], w3_words[0].rearrange("p n t -> p (n t)").bitcast(I32))
-        picked = keep.tile([P, S], U8, name="picked", tag="then_cand_0", align_bytes=64)
-        nc.vector.tensor_copy(picked[:], tab_rows[:].indirect(offsets[:]))
-        v_plane = keep.tile([P, S], U8, name="v_plane", align_bytes=64)
-        nc.vector.tensor_copy(v_plane[:].bitcast(I32), picked[:].bitcast(I32))
-        for e in range(2):
-            nc.sync.dma_start(v_plane[2 + e : P : 32, :].bitcast(I32), picked[16 + e : P : 32, :].bitcast(I32))
-        v_scales = [v_plane[:, 0:HALF], v_plane[:, HALF:]]
         w2_all = keep.tile([P, H // 2], I32, name="w2_codes", align_bytes=64)
         nc.vector.tensor_copy(
             w2_all[:].bitcast(U16).rearrange("p (b t m) -> p b t m", b=2, t=4),
@@ -117,15 +121,15 @@ def tile_list_hyper_relational_scoring_kernel(
             w3_raw[:].rearrange("p (b m t) -> p b m t", b=2, t=4),
         )
         w3_codes = [w3_all[:, 0:HALF], w3_all[:, HALF:]]
-        v_words.append(gather_words(1, "then_w3"))
-        cand_raw = [load_cand(b) for b in range(2)]
+        v_scales.append(gather_scales(1, "then_second_half", nc.sync))
+        v_words.append(gather_words(1, "then_second_words"))
+        cand_raw = [load_cand(0, "then_cand_0"), load_cand(1, "then_second_half")]
 
         w1_codes = [keep.tile([P, HALF], U32, name="w1_codes%d" % b, align_bytes=64) for b in range(2)]
         w1_planes = [keep.tile([P, HALF], U8, name="w1_plane%d" % b, align_bytes=64) for b in range(2)]
         cand_codes = [keep.tile([P, N], U32, name="cand_codes%d" % b, align_bytes=64) for b in range(2)]
         cand_planes = [keep.tile([P, N], U8, name="cand_plane%d" % b, align_bytes=64) for b in range(2)]
-        w1_round = [keep.tile([P, 4 * HALF], BF16, name="w1_round%d" % b, align_bytes=64) for b in range(2)]
-        cand_round = [keep.tile([P, 4 * N], BF16, name="cand_round%d" % b, align_bytes=64) for b in range(2)]
+        w1_round, cand_round = {}, {}
         scaled, pair, h_codes, h_planes, h_rounds = {}, {}, {}, {}, {}
         for h in range(2):
             for b in range(2):
@@ -133,24 +137,41 @@ def tile_list_hyper_relational_scoring_kernel(
                 h_planes[h, b] = keep.tile([P, HALF], U8, name="h_plane%d%d" % (h, b), align_bytes=64)
                 h_rounds[h, b] = keep.tile([P, 4 * HALF], BF16, name="h_round%d%d" % (h, b), align_bytes=64)
 
-        def round_w1(engine, b, lo, hi):
+        def round_w1_scalar(b):
+            w1_round[b] = keep.tile([P, 4 * HALF], BF16, name="w1_round%d" % b, align_bytes=64)
             src = w1_raw[b][:].rearrange("p j (m t) -> p m j t", t=4)
             dst = w1_round[b][:].rearrange("p (t m j) -> p m j t", t=4, j=4)
-            engine(dst[:, lo:hi], src[:, lo:hi])
+            for lo in (0, 64):
+                nc.scalar.copy(dst[:, lo : lo + 64], src[:, lo : lo + 64])
+
+        def round_w1_gpsimd(b):
+            w1_round[b] = keep.tile([P, 4 * HALF], BF16, name="w1_round%d" % b, tag="gpsimd_turn", align_bytes=64)
+            src = w1_raw[b][:].rearrange("p j (m t) -> p t m j", t=4)
+            dst = w1_round[b][:].rearrange("p (t m j) -> p t m j", t=4, j=4)
+            for lo in (0, 2):
+                nc.gpsimd.tensor_scalar(dst[:, lo : lo + 2], src[:, lo : lo + 2], 1.0, 0.0, MULT, ADD)
 
         def quantise_w1(b):
             nc.vector.quantize_mx(out=w1_codes[b][:].bitcast(FP8X4), scales=w1_planes[b][:], in_=w1_round[b][:])
 
-        def round_cand(engine, b, lo, hi):
-            dst = cand_round[b][:, 4 * lo : 4 * hi].rearrange("p (c e t) -> p c t e", e=4, t=4)
+        def round_cand_scalar(b, lo, hi):
+            cand_round[b, lo] = keep.tile([P, 4 * (hi - lo)], BF16, name="cand_round%d_%d" % (b, lo), align_bytes=64)
+            dst = cand_round[b, lo][:].rearrange("p (c e t) -> p c t e", e=4, t=4)
             src = cand_raw[b][:, :, lo:hi].rearrange("p t (c e) -> p c t e", e=4)
-            engine(dst, src)
+            nc.scalar.copy(dst, src)
+
+        def round_cand_gpsimd(b, lo, hi):
+            cand_round[b, lo] = keep.tile(
+                [P, 4 * (hi - lo)], BF16, name="cand_round%d_%d" % (b, lo), tag="gpsimd_turn", align_bytes=64
+            )
+            dst = cand_round[b, lo][:].rearrange("p (c t) -> p c t", t=4)
+            src = cand_raw[b][:, :, lo:hi].rearrange("p t c -> p c t")
+            for c in range(0, hi - lo, 2 * P):
+                nc.gpsimd.tensor_scalar(dst[:, c : c + 2 * P], src[:, c : c + 2 * P], 1.0, 0.0, MULT, ADD)
 
         def quantise_cand(b, lo, hi):
             nc.vector.quantize_mx(
-                out=cand_codes[b][:, lo:hi].bitcast(FP8X4),
-                scales=cand_planes[b][:, lo:hi],
-                in_=cand_round[b][:, 4 * lo : 4 * hi],
+                out=cand_codes[b][:, lo:hi].bitcast(FP8X4), scales=cand_planes[b][:, lo:hi], in_=cand_round[b, lo][:]
             )
 
         steps = [(0, 0, HALF, b, t) for b in range(2) for t in range(4)]
@@ -188,6 +209,22 @@ def tile_list_hyper_relational_scoring_kernel(
             if (h, lo, b) not in pair:
                 pair[h, lo, b] = keep.tile([P, 4, width], F32, name="pair%d_%d_%d" % (h, lo, b), align_bytes=64)
             nc.vector.tensor_tensor(pair[h, lo, b][:, t0 : t0 + HALF // width, :], bank[:], scaled[k][:], MULT)
+
+        x3_rows = {}
+
+        def copy_x3(k):
+            h, lo, width, b, t0 = steps[k]
+            bank = projection(steps[k], lambda b, t: w3_codes[b][:, t * P : (t + 1) * P], w3_plane, FP8X4)
+            x3_rows[k] = keep.tile([P, HALF // width, width], F32, name="x3_%d" % k, align_bytes=64)
+            nc.scalar.copy(x3_rows[k][:], bank[:])
+
+        def pair_product_gpsimd(k):
+            h, lo, width, b, t0 = steps[k]
+            if (h, lo, b) not in pair:
+                pair[h, lo, b] = keep.tile(
+                    [P, 4, width], F32, name="pair%d_%d_%d" % (h, lo, b), tag="gpsimd_turn", align_bytes=64
+                )
+            nc.gpsimd.tensor_tensor(pair[h, lo, b][:, t0 : t0 + HALF // width, :], x3_rows[k][:], scaled[k][:], MULT)
 
         def triple_product(h, b, q):
             cols = slice(q * P, (q + 1) * P)
@@ -273,68 +310,62 @@ def tile_list_hyper_relational_scoring_kernel(
             add_prior(staged[:], bank, P, c0, 3, on_vector)
             store(staged, 1, q * P, P, c0, 3)
 
-        on_scalar, on_vector = nc.scalar.copy, nc.vector.tensor_copy
-        scale_x2(0)
-        scale_x2(1)
-        scale_x2(2)
-        pair_product(0)
-        scale_x2(3)
-        pair_product(1)
-        round_w1(on_scalar, 0, 0, 64)
-        pair_product(2)
-        pair_product(3)
-        round_w1(on_vector, 0, 64, P)
-        scale_x2(4)
+        for k in range(3):
+            scale_x2(k)
+        round_w1_gpsimd(0)
+        for k in range(8):
+            pair_product(k)
+            if k + 3 < 8:
+                scale_x2(k + 3)
+        round_w1_scalar(1)
         quantise_w1(0)
         prior_cols = load_prior()
-        for q in range(4):
-            if q < 3:
-                scale_x2(5 + q)
-            triple_product(0, 0, q)
-        round_w1(on_scalar, 1, 0, 64)
-        round_w1(on_scalar, 1, 64, P)
-        for k in range(4, 8):
-            pair_product(k)
-        quantise_w1(1)
-        for lo in range(0, N, 2 * P):
-            round_cand(on_scalar, 0, lo, lo + 2 * P)
-        triple_product(0, 1, 0)
-        quantise_h(0, 0, 0, HALF)
-        for q in range(1, 4):
-            triple_product(0, 1, q)
+        round_cand_gpsimd(0, 0, HALF)
+        triple_product(0, 0, 0)
         scale_x2(8)
+        triple_product(0, 0, 1)
+        round_cand_scalar(0, HALF, N)
+        triple_product(0, 0, 2)
         scale_x2(9)
-        round_cand(on_vector, 1, HALF, N)
-        quantise_h(0, 1, 0, HALF)
-        quantise_cand(0, 0, HALF)
-        round_cand(on_scalar, 1, 0, 256)
-        round_cand(on_scalar, 1, 256, HALF)
+        triple_product(0, 0, 3)
         pair_product(8)
-        quantise_cand(0, HALF, N)
-        pair_product(9)
-        quantise_cand(1, HALF, N)
+        quantise_w1(1)
         scale_x2(10)
         scale_x2(11)
-        triple_product(1, 0, 0)
+        quantise_h(0, 0, 0, HALF)
+        quantise_cand(0, HALF, N)
+        round_cand_scalar(1, HALF, N)
+        quantise_cand(0, 0, HALF)
+        round_cand_gpsimd(1, 0, HALF)
+        triple_product(0, 1, 0)
+        scale_x2(14)
+        triple_product(0, 1, 1)
+        copy_x3(14)
+        triple_product(0, 1, 2)
+        scale_x2(15)
+        triple_product(0, 1, 3)
+        copy_x3(15)
+        pair_product(9)
+        scale_x2(12)
+        quantise_h(0, 1, 0, HALF)
+        scale_x2(13)
+        quantise_cand(1, HALF, N)
         quantise_cand(1, 0, HALF)
+        pair_product_gpsimd(14)
+        pair_product_gpsimd(15)
+        triple_product(1, 0, 0)
         triple_product(1, 0, 1)
         score(0, 0, HALF, 0, 2, 1)
         pair_product(10)
-        scale_x2(12)
         pair_product(11)
-        scale_x2(13)
-        triple_product(1, 1, 0)
         score(0, 0, HALF, 2, 2, 1)
+        triple_product(1, 1, 0)
         triple_product(1, 1, 1)
-        quantise_h(1, 0, 0, 2 * P)
-        scale_x2(14)
-        pair_product(12)
-        quantise_h(1, 1, 0, 2 * P)
-        scale_x2(15)
-        pair_product(13)
         score(0, 0, HALF, 4, 2, 1)
-        pair_product(14)
-        pair_product(15)
+        pair_product(12)
+        quantise_h(1, 0, 0, 2 * P)
+        pair_product(13)
+        quantise_h(1, 1, 0, 2 * P)
         triple_product(1, 0, 2)
         score(1, 0, 2 * P, 0, 2, 2)
         triple_product(1, 1, 2)

@@ -52,7 +52,7 @@ def tile_list_hyper_relational_scoring_kernel(
             )
         w2_raw = keep.tile([P, H // 2], I32, name="w2_raw", tag="then_w1_0", align_bytes=64)
         nc.sync.dma_start(w2_raw[:], w2_words[0].bitcast(I32))
-        table = keep.tile([P, T], I32, name="table", tag="gpsimd_turn", align_bytes=64)
+        table = keep.tile([P, T], I32, name="table", align_bytes=64)
         nc.sync.dma_start(table[:], tab_words[0].rearrange("p n t -> p (n t)").bitcast(I32))
         w3_raw = keep.tile([P, H], I32, name="w3_raw", tag="then_second_half", align_bytes=64)
         nc.sync.dma_start(w3_raw[:], w3_words[0].rearrange("p n t -> p (n t)").bitcast(I32))
@@ -129,7 +129,8 @@ def tile_list_hyper_relational_scoring_kernel(
         w1_planes = [keep.tile([P, HALF], U8, name="w1_plane%d" % b, align_bytes=64) for b in range(2)]
         cand_codes = [keep.tile([P, N], U32, name="cand_codes%d" % b, align_bytes=64) for b in range(2)]
         cand_planes = [keep.tile([P, N], U8, name="cand_plane%d" % b, align_bytes=64) for b in range(2)]
-        w1_round, cand_round = {}, {}
+        w1_round = [keep.tile([P, 4 * HALF], BF16, name="w1_round%d" % b, tag=tag, align_bytes=64) for b, tag in enumerate(("gpsimd_turn", "w1_round1"))]
+        cand_round = {}
         scaled, pair, h_codes, h_planes, h_rounds = {}, {}, {}, {}, {}
         for h in range(2):
             for b in range(2):
@@ -137,19 +138,10 @@ def tile_list_hyper_relational_scoring_kernel(
                 h_planes[h, b] = keep.tile([P, HALF], U8, name="h_plane%d%d" % (h, b), align_bytes=64)
                 h_rounds[h, b] = keep.tile([P, 4 * HALF], BF16, name="h_round%d%d" % (h, b), align_bytes=64)
 
-        def round_w1_scalar(b):
-            w1_round[b] = keep.tile([P, 4 * HALF], BF16, name="w1_round%d" % b, align_bytes=64)
+        def round_w1(engine, b, lo, hi):
             src = w1_raw[b][:].rearrange("p j (m t) -> p m j t", t=4)
             dst = w1_round[b][:].rearrange("p (t m j) -> p m j t", t=4, j=4)
-            for lo in (0, 64):
-                nc.scalar.copy(dst[:, lo : lo + 64], src[:, lo : lo + 64])
-
-        def round_w1_gpsimd(b):
-            w1_round[b] = keep.tile([P, 4 * HALF], BF16, name="w1_round%d" % b, tag="gpsimd_turn", align_bytes=64)
-            src = w1_raw[b][:].rearrange("p j (m t) -> p t m j", t=4)
-            dst = w1_round[b][:].rearrange("p (t m j) -> p t m j", t=4, j=4)
-            for lo in (0, 2):
-                nc.gpsimd.tensor_scalar(dst[:, lo : lo + 2], src[:, lo : lo + 2], 1.0, 0.0, MULT, ADD)
+            engine(dst[:, lo:hi], src[:, lo:hi])
 
         def quantise_w1(b):
             nc.vector.quantize_mx(out=w1_codes[b][:].bitcast(FP8X4), scales=w1_planes[b][:], in_=w1_round[b][:])
@@ -166,16 +158,14 @@ def tile_list_hyper_relational_scoring_kernel(
             )
             dst = cand_round[b, lo][:].rearrange("p (c t) -> p c t", t=4)
             src = cand_raw[b][:, :, lo:hi].rearrange("p t c -> p c t")
-            for c in range(0, hi - lo, 2 * P):
-                nc.gpsimd.tensor_scalar(dst[:, c : c + 2 * P], src[:, c : c + 2 * P], 1.0, 0.0, MULT, ADD)
+            nc.gpsimd.tensor_scalar(dst, src, 1.0, 0.0, MULT, ADD)
 
         def quantise_cand(b, lo, hi):
             nc.vector.quantize_mx(
                 out=cand_codes[b][:, lo:hi].bitcast(FP8X4), scales=cand_planes[b][:, lo:hi], in_=cand_round[b, lo][:]
             )
 
-        steps = [(0, 0, HALF, b, t) for b in range(2) for t in range(4)]
-        steps = steps + [(1, lo, 2 * P, b, t) for lo in (0, 2 * P) for b in range(2) for t in (0, 2)]
+        steps = [(h, 0, HALF, b, t) for h in range(2) for b in range(2) for t in range(4)]
 
         def projection(step, codes, plane, fmt):
             h, lo, width, b, t0 = step
@@ -218,17 +208,17 @@ def tile_list_hyper_relational_scoring_kernel(
             x3_rows[k] = keep.tile([P, HALF // width, width], F32, name="x3_%d" % k, align_bytes=64)
             nc.scalar.copy(x3_rows[k][:], bank[:])
 
-        def pair_product_gpsimd(k):
+        def pair_product_gpsimd(k, tag):
             h, lo, width, b, t0 = steps[k]
             if (h, lo, b) not in pair:
                 pair[h, lo, b] = keep.tile(
-                    [P, 4, width], F32, name="pair%d_%d_%d" % (h, lo, b), tag="gpsimd_turn", align_bytes=64
+                    [P, 4, width], F32, name="pair%d_%d_%d" % (h, lo, b), tag=tag, align_bytes=64
                 )
             nc.gpsimd.tensor_tensor(pair[h, lo, b][:, t0 : t0 + HALF // width, :], x3_rows[k][:], scaled[k][:], MULT)
 
         def triple_product(h, b, q):
             cols = slice(q * P, (q + 1) * P)
-            lo = 0 if h == 0 else q // 2 * 2 * P
+            lo = 0
             x1 = next_bank(4)
             for t in range(4):
                 nc.tensor.matmul_mx(
@@ -310,63 +300,63 @@ def tile_list_hyper_relational_scoring_kernel(
             add_prior(staged[:], bank, P, c0, 3, on_vector)
             store(staged, 1, q * P, P, c0, 3)
 
-        for k in range(3):
+        on_scalar, on_vector = nc.scalar.copy, nc.vector.tensor_copy
+        for k in range(4):
             scale_x2(k)
-        round_w1_gpsimd(0)
-        for k in range(8):
+        pair_product(0)
+        round_w1(on_scalar, 0, 0, 64)
+        for k in range(1, 4):
             pair_product(k)
-            if k + 3 < 8:
-                scale_x2(k + 3)
-        round_w1_scalar(1)
-        quantise_w1(0)
+        round_w1(on_vector, 0, 64, P)
+        scale_x2(4)
         prior_cols = load_prior()
+        quantise_w1(0)
         round_cand_gpsimd(0, 0, HALF)
-        triple_product(0, 0, 0)
-        scale_x2(8)
-        triple_product(0, 0, 1)
+        for q in range(4):
+            if q < 3:
+                scale_x2(5 + q)
+            triple_product(0, 0, q)
+        round_w1(on_scalar, 1, 0, 64)
+        round_w1(on_scalar, 1, 64, P)
+        for k in range(4, 8):
+            pair_product(k)
         round_cand_scalar(0, HALF, N)
-        triple_product(0, 0, 2)
-        scale_x2(9)
-        triple_product(0, 0, 3)
-        pair_product(8)
         quantise_w1(1)
-        scale_x2(10)
-        scale_x2(11)
+        scale_x2(8)
         quantise_h(0, 0, 0, HALF)
+        scale_x2(9)
         quantise_cand(0, HALF, N)
-        round_cand_scalar(1, HALF, N)
         quantise_cand(0, 0, HALF)
         round_cand_gpsimd(1, 0, HALF)
         triple_product(0, 1, 0)
-        scale_x2(14)
+        scale_x2(10)
         triple_product(0, 1, 1)
-        copy_x3(14)
+        scale_x2(11)
         triple_product(0, 1, 2)
-        scale_x2(15)
+        round_cand_scalar(1, HALF, N)
         triple_product(0, 1, 3)
-        copy_x3(15)
-        pair_product(9)
-        scale_x2(12)
+        for k in range(8, 12):
+            pair_product(k)
+            scale_x2(k + 4)
+            if k < 10:
+                copy_x3(k + 4)
         quantise_h(0, 1, 0, HALF)
-        scale_x2(13)
         quantise_cand(1, HALF, N)
         quantise_cand(1, 0, HALF)
-        pair_product_gpsimd(14)
-        pair_product_gpsimd(15)
+        pair_product_gpsimd(12, "gpsimd_turn")
+        pair_product_gpsimd(13, "gpsimd_turn")
+        pair_product(14)
+        pair_product(15)
+        score(0, 0, HALF, 0, 2, 1)
         triple_product(1, 0, 0)
         triple_product(1, 0, 1)
-        score(0, 0, HALF, 0, 2, 1)
-        pair_product(10)
-        pair_product(11)
         score(0, 0, HALF, 2, 2, 1)
         triple_product(1, 1, 0)
         triple_product(1, 1, 1)
         score(0, 0, HALF, 4, 2, 1)
-        pair_product(12)
         quantise_h(1, 0, 0, 2 * P)
-        pair_product(13)
-        quantise_h(1, 1, 0, 2 * P)
         triple_product(1, 0, 2)
+        quantise_h(1, 1, 0, 2 * P)
         score(1, 0, 2 * P, 0, 2, 2)
         triple_product(1, 1, 2)
         quantise_h(1, 0, 2 * P, 3 * P)

@@ -52,7 +52,7 @@ def tile_list_hyper_relational_scoring_kernel(
             )
         w2_raw = keep.tile([P, H // 2], I32, name="w2_raw", tag="then_w1_0", align_bytes=64)
         nc.sync.dma_start(w2_raw[:], w2_words[0].bitcast(I32))
-        table = keep.tile([P, T], I32, name="table", align_bytes=64)
+        table = keep.tile([P, T], I32, name="table", tag="then_last_loads", align_bytes=64)
         nc.sync.dma_start(table[:], tab_words[0].rearrange("p n t -> p (n t)").bitcast(I32))
         w3_raw = keep.tile([P, H], I32, name="w3_raw", tag="then_second_half", align_bytes=64)
         nc.sync.dma_start(w3_raw[:], w3_words[0].rearrange("p n t -> p (n t)").bitcast(I32))
@@ -87,15 +87,21 @@ def tile_list_hyper_relational_scoring_kernel(
             nc.vector.tensor_copy(words[:].bitcast(U32), table[:].bitcast(U32).indirect(lists(h)))
             return words
 
-        def load_w1(b):
-            raw = keep.tile([P, 4, HALF], F32, name="w1_raw%d" % b, tag="then_w1_%d" % b, align_bytes=64)
+        def load_w1(b, tag):
+            raw = keep.tile([P, 4, HALF], F32, name="w1_raw%d" % b, tag=tag, align_bytes=64)
             nc.sync.dma_start(raw[:], w1[:, b * HALF : (b + 1) * HALF].rearrange("(p j) c -> p j c", j=4))
             return raw
 
-        def load_cand(b, tag):
-            raw = keep.tile([P, 4, N], F32, name="cand_raw%d" % b, tag=tag, align_bytes=64)
-            nc.sync.dma_start(raw[:], cand[b * HALF : (b + 1) * HALF, :].rearrange("(p j) n -> p j n", j=4))
-            return raw
+        cand_raw = {}
+
+        def load_cand(b, lo, hi, tag):
+            raw = keep.tile([P, 4, hi - lo], F32, name="cand_raw%d_%d" % (b, lo), tag=tag, align_bytes=64)
+            nc.sync.dma_start(raw[:], cand[b * HALF : (b + 1) * HALF, lo:hi].rearrange("(p j) n -> p j n", j=4))
+            cand_raw[b, lo] = raw
+
+        def cand_columns(b, lo, hi):
+            first = max(start for (pass_, start) in cand_raw if pass_ == b and start <= lo)
+            return cand_raw[b, first][:, :, lo - first : hi - first]
 
         v_scales = [gather_scales(0, "then_w1_1", nc.scalar)]
         w_dealt = keep.tile([P, H], U8, name="w_dealt", tag="then_cand_0", align_bytes=64)
@@ -113,7 +119,9 @@ def tile_list_hyper_relational_scoring_kernel(
             w2_all[:].bitcast(U16).rearrange("p (b t m) -> p b t m", b=2, t=4),
             w2_raw[:].bitcast(U16).rearrange("p (b m t) -> p b t m", b=2, t=4),
         )
-        w1_raw = [load_w1(b) for b in range(2)]
+        w1_raw = [load_w1(0, "then_w1_0")]
+        load_cand(0, 0, HALF, "then_w1_1")
+        w1_raw.append(load_w1(1, "then_cand_0"))
         v_words = [gather_words(0, "first_half")]
         w3_all = keep.tile([P, H], I32, name="w3_codes", align_bytes=64)
         nc.vector.tensor_copy(
@@ -123,7 +131,8 @@ def tile_list_hyper_relational_scoring_kernel(
         w3_codes = [w3_all[:, 0:HALF], w3_all[:, HALF:]]
         v_scales.append(gather_scales(1, "then_second_half", nc.sync))
         v_words.append(gather_words(1, "then_second_words"))
-        cand_raw = [load_cand(0, "then_cand_0"), load_cand(1, "then_second_half")]
+        load_cand(0, HALF, N, "then_last_loads")
+        load_cand(1, 0, N, "then_second_half")
 
         w1_codes = [keep.tile([P, HALF], U32, name="w1_codes%d" % b, align_bytes=64) for b in range(2)]
         w1_planes = [keep.tile([P, HALF], U8, name="w1_plane%d" % b, align_bytes=64) for b in range(2)]
@@ -149,7 +158,7 @@ def tile_list_hyper_relational_scoring_kernel(
         def round_cand_scalar(b, lo, hi):
             cand_round[b, lo] = keep.tile([P, 4 * (hi - lo)], BF16, name="cand_round%d_%d" % (b, lo), align_bytes=64)
             dst = cand_round[b, lo][:].rearrange("p (c e t) -> p c t e", e=4, t=4)
-            src = cand_raw[b][:, :, lo:hi].rearrange("p t (c e) -> p c t e", e=4)
+            src = cand_columns(b, lo, hi).rearrange("p t (c e) -> p c t e", e=4)
             nc.scalar.copy(dst, src)
 
         def round_cand_gpsimd(b, lo, hi):
@@ -157,7 +166,7 @@ def tile_list_hyper_relational_scoring_kernel(
                 [P, 4 * (hi - lo)], BF16, name="cand_round%d_%d" % (b, lo), tag="gpsimd_turn", align_bytes=64
             )
             dst = cand_round[b, lo][:].rearrange("p (c t) -> p c t", t=4)
-            src = cand_raw[b][:, :, lo:hi].rearrange("p t c -> p c t")
+            src = cand_columns(b, lo, hi).rearrange("p t c -> p c t")
             nc.gpsimd.tensor_scalar(dst, src, 1.0, 0.0, MULT, ADD)
 
         def quantise_cand(b, lo, hi):
@@ -165,7 +174,8 @@ def tile_list_hyper_relational_scoring_kernel(
                 out=cand_codes[b][:, lo:hi].bitcast(FP8X4), scales=cand_planes[b][:, lo:hi], in_=cand_round[b, lo][:]
             )
 
-        steps = [(h, 0, HALF, b, t) for h in range(2) for b in range(2) for t in range(4)]
+        steps = [(0, 0, HALF, b, t) for b in range(2) for t in range(4)]
+        steps = steps + [(1, lo, 2 * P, b, t) for lo in (0, 2 * P) for b in range(2) for t in (0, 2)]
 
         def projection(step, codes, plane, fmt):
             h, lo, width, b, t0 = step
@@ -202,23 +212,22 @@ def tile_list_hyper_relational_scoring_kernel(
 
         x3_rows = {}
 
-        def copy_x3(k):
+        def copy_x3(k, tag):
             h, lo, width, b, t0 = steps[k]
             bank = projection(steps[k], lambda b, t: w3_codes[b][:, t * P : (t + 1) * P], w3_plane, FP8X4)
-            x3_rows[k] = keep.tile([P, HALF // width, width], F32, name="x3_%d" % k, align_bytes=64)
+            x3_rows[k] = keep.tile([P, HALF // width, width], F32, name="x3_%d" % k, tag=tag, align_bytes=64)
             nc.scalar.copy(x3_rows[k][:], bank[:])
 
-        def pair_product_gpsimd(k, tag):
+        def pair_product_gpsimd(k):
             h, lo, width, b, t0 = steps[k]
             if (h, lo, b) not in pair:
-                pair[h, lo, b] = keep.tile(
-                    [P, 4, width], F32, name="pair%d_%d_%d" % (h, lo, b), tag=tag, align_bytes=64
-                )
+                both = keep.tile([P, 2, 4, width], F32, name="pair_gpsimd", tag="gpsimd_turn", align_bytes=64)
+                pair[h, lo, 0], pair[h, lo, 1] = both[:, 0], both[:, 1]
             nc.gpsimd.tensor_tensor(pair[h, lo, b][:, t0 : t0 + HALF // width, :], x3_rows[k][:], scaled[k][:], MULT)
 
         def triple_product(h, b, q):
             cols = slice(q * P, (q + 1) * P)
-            lo = 0
+            lo = 0 if h == 0 else q // 2 * 2 * P
             x1 = next_bank(4)
             for t in range(4):
                 nc.tensor.matmul_mx(
@@ -307,14 +316,15 @@ def tile_list_hyper_relational_scoring_kernel(
         round_w1(on_scalar, 0, 0, 64)
         for k in range(1, 4):
             pair_product(k)
-        round_w1(on_vector, 0, 64, P)
         scale_x2(4)
+        round_w1(on_vector, 0, 64, P)
+        scale_x2(5)
         prior_cols = load_prior()
         quantise_w1(0)
         round_cand_gpsimd(0, 0, HALF)
         for q in range(4):
-            if q < 3:
-                scale_x2(5 + q)
+            if q < 2:
+                scale_x2(6 + q)
             triple_product(0, 0, q)
         round_w1(on_scalar, 1, 0, 64)
         round_w1(on_scalar, 1, 64, P)
@@ -322,46 +332,48 @@ def tile_list_hyper_relational_scoring_kernel(
             pair_product(k)
         round_cand_scalar(0, HALF, N)
         quantise_w1(1)
-        scale_x2(8)
+        round_cand_scalar(1, 2 * P, N)
         quantise_h(0, 0, 0, HALF)
-        scale_x2(9)
-        quantise_cand(0, HALF, N)
         quantise_cand(0, 0, HALF)
-        round_cand_gpsimd(1, 0, HALF)
-        triple_product(0, 1, 0)
-        scale_x2(10)
-        triple_product(0, 1, 1)
-        scale_x2(11)
-        triple_product(0, 1, 2)
-        round_cand_scalar(1, HALF, N)
-        triple_product(0, 1, 3)
-        for k in range(8, 12):
-            pair_product(k)
-            scale_x2(k + 4)
-            if k < 10:
-                copy_x3(k + 4)
+        round_cand_gpsimd(1, 0, 2 * P)
+        for q in range(4):
+            triple_product(0, 1, q)
+            scale_x2(8 + q)
+        scale_x2(12)
         quantise_h(0, 1, 0, HALF)
-        quantise_cand(1, HALF, N)
-        quantise_cand(1, 0, HALF)
-        pair_product_gpsimd(12, "gpsimd_turn")
-        pair_product_gpsimd(13, "gpsimd_turn")
-        pair_product(14)
-        pair_product(15)
-        score(0, 0, HALF, 0, 2, 1)
+        copy_x3(12, "x3_12")
+        quantise_cand(0, HALF, N)
+        scale_x2(13)
+        quantise_cand(1, 2 * P, N)
+        copy_x3(13, "x3_13")
+        quantise_cand(1, 0, 2 * P)
+        pair_product_gpsimd(12)
+        pair_product_gpsimd(13)
+        pair_product(8)
+        scale_x2(14)
+        pair_product(9)
+        copy_x3(14, "x3_14")
+        pair_product_gpsimd(14)
+        pair_product(10)
+        score(0, 0, HALF, 0, 1, 1)
+        pair_product(11)
+        scale_x2(15)
         triple_product(1, 0, 0)
+        copy_x3(15, "x3_15")
+        pair_product_gpsimd(15)
         triple_product(1, 0, 1)
-        score(0, 0, HALF, 2, 2, 1)
+        score(0, 0, HALF, 1, 2, 1)
         triple_product(1, 1, 0)
         triple_product(1, 1, 1)
-        score(0, 0, HALF, 4, 2, 1)
-        quantise_h(1, 0, 0, 2 * P)
+        score(0, 0, HALF, 3, 3, 1)
         triple_product(1, 0, 2)
+        quantise_h(1, 0, 0, 2 * P)
         quantise_h(1, 1, 0, 2 * P)
-        score(1, 0, 2 * P, 0, 2, 2)
         triple_product(1, 1, 2)
+        score(1, 0, 2 * P, 0, 2, 2)
         quantise_h(1, 0, 2 * P, 3 * P)
-        score(1, 0, 2 * P, 2, 4, 2)
         triple_product(1, 0, 3)
+        score(1, 0, 2 * P, 2, 4, 2)
         quantise_h(1, 1, 2 * P, 3 * P)
         triple_product(1, 1, 3)
         quantise_h(1, 0, 3 * P, 4 * P)

@@ -32,29 +32,33 @@ def tile_list_hyper_relational_scoring_kernel(
         psum = ctx.enter_context(tc.psum_pool(name="psum", bufs=1))
         taken = []
 
-        def next_bank(groups):
-            tile = psum.tile([P, groups, HALF // groups], F32, name="ps%d" % len(taken), tag="bank%d" % (len(taken) % BANKS))
-            taken.append(tile)
-            return tile
+        turn = []
+
+        def next_bank(groups, bank=None):
+            if bank is None:
+                bank = len(turn) % BANKS
+                turn.append(bank)
+            taken.append(bank)
+            return psum.tile([P, groups, HALF // groups], F32, name="ps%d" % len(taken), tag="bank%d" % bank)
 
         offsets = keep.tile([P, S // 16], U16, name="offsets")
         nc.sync.dma_start(offsets[:], offs)
-        tab_rows = keep.tile([P, T], U8, name="tab_rows", tag="then_second_words", align_bytes=64)
+        tab_rows = keep.tile([P, T], U8, name="tab_rows", tag="then_w1_0", align_bytes=64)
         scale_words = tab_scales[0].bitcast(I32)
         for e in range(2):
             nc.sync.dma_start(
                 tab_rows[e:P:2, :].bitcast(I32), scale_words[e:16:2, :].unsqueeze(1).to_broadcast([8, 8, T // 4])
             )
-        w_rows = keep.tile([P, H], U8, name="w_rows", align_bytes=64)
+        w_rows = keep.tile([P, H], U8, name="w_rows", tag="then_cand_0_rest", align_bytes=64)
         for w, scales in enumerate((w2_scales, w3_scales)):
             nc.sync.dma_start(
                 w_rows[w:32:2, :].bitcast(I32), scales[0].bitcast(I32).rearrange("(d q) c -> q d c", q=4)
             )
-        w2_raw = keep.tile([P, H // 2], I32, name="w2_raw", tag="then_w1_0", align_bytes=64)
+        w2_raw = keep.tile([P, H // 2], I32, name="w2_raw", align_bytes=64)
         nc.sync.dma_start(w2_raw[:], w2_words[0].bitcast(I32))
-        table = keep.tile([P, T], I32, name="table", tag="then_last_loads", align_bytes=64)
+        table = keep.tile([P, T], I32, name="table", tag="then_cand_1", align_bytes=64)
         nc.sync.dma_start(table[:], tab_words[0].rearrange("p n t -> p (n t)").bitcast(I32))
-        w3_raw = keep.tile([P, H], I32, name="w3_raw", tag="then_second_half", align_bytes=64)
+        w3_raw = keep.tile([P, H], I32, name="w3_raw", tag="then_second_words", align_bytes=64)
         nc.sync.dma_start(w3_raw[:], w3_words[0].rearrange("p n t -> p (n t)").bitcast(I32))
 
         rel_cols = keep.tile([P, 2, 4], F32, name="rel_cols", align_bytes=64)
@@ -62,10 +66,13 @@ def tile_list_hyper_relational_scoring_kernel(
         w_plane = keep.tile([P, 2 * H], U8, name="w_plane", align_bytes=64)
         nc.vector.memset(w_plane[:].bitcast(I32), 0)
         nc.vector.memset(w_rows[32:64, :].bitcast(I32), 0)
+        v_scales = [keep.tile([P, HALF], U8, name="v_plane%d" % h, align_bytes=64) for h in range(2)]
+        for plane in v_scales:
+            nc.vector.memset(plane[96:P, :].bitcast(I32), 0)
         nc.scalar.copy(w_rows[64:P, :].bitcast(U32), w_plane[64:P, 0:H].bitcast(U32))
 
         def load_prior():
-            cols = keep.tile([P, NT], F32, name="prior_cols", tag="then_w1_0", align_bytes=64)
+            cols = keep.tile([P, NT], F32, name="prior_cols", tag="then_cand_0", align_bytes=64)
             with nc.allow_non_contiguous_dma(reason="one prior for each partition and tile of candidates"):
                 nc.sync.dma_start(cols[:], prior.rearrange("(c p) -> p c", p=P))
             return cols
@@ -76,11 +83,7 @@ def tile_list_hyper_relational_scoring_kernel(
         def gather_scales(h, tag, queue):
             picked = keep.tile([P, HALF], U8, name="picked%d" % h, tag=tag, align_bytes=64)
             nc.vector.tensor_copy(picked[:], tab_rows[:].indirect(lists(h)))
-            plane = keep.tile([P, HALF], U8, name="v_plane%d" % h, align_bytes=64)
-            nc.vector.tensor_copy(plane[:].bitcast(I32), picked[:].bitcast(I32))
-            for e in range(2):
-                queue.dma_start(plane[2 + e : P : 32, :].bitcast(I32), picked[16 + e : P : 32, :].bitcast(I32))
-            return plane
+            queue.dma_start(v_scales[h][0:112, :].bitcast(I32), picked[14:126, :].bitcast(I32))
 
         def gather_words(h, tag):
             words = keep.tile([P, HALF], I32, name="v_words%d" % h, tag=tag, align_bytes=64)
@@ -103,7 +106,7 @@ def tile_list_hyper_relational_scoring_kernel(
             first = max(start for (pass_, start) in cand_raw if pass_ == b and start <= lo)
             return cand_raw[b, first][:, :, lo - first : hi - first]
 
-        v_scales = [gather_scales(0, "then_w1_1", nc.scalar)]
+        gather_scales(0, "then_w1_1", nc.sync)
         w_dealt = keep.tile([P, H], U8, name="w_dealt", tag="then_cand_0", align_bytes=64)
         nc.vector.tensor_copy(
             w_dealt[:].rearrange("p (b t m) -> p b t m", b=2, t=4),
@@ -114,12 +117,13 @@ def tile_list_hyper_relational_scoring_kernel(
             nc.scalar.dma_start(w_planes[q:P:32], w_dealt[8 * q : 8 * q + 8, :].bitcast(I32))
         w2_plane = w_plane[:, 0:H]
         w3_plane = w_plane[:, H:]
+        gather_scales(1, "then_cand_0_rest", nc.sync)
+        w1_raw = [load_w1(0, "then_w1_0")]
         w2_all = keep.tile([P, H // 2], I32, name="w2_codes", align_bytes=64)
         nc.vector.tensor_copy(
             w2_all[:].bitcast(U16).rearrange("p (b t m) -> p b t m", b=2, t=4),
             w2_raw[:].bitcast(U16).rearrange("p (b m t) -> p b t m", b=2, t=4),
         )
-        w1_raw = [load_w1(0, "then_w1_0")]
         load_cand(0, 0, HALF, "then_w1_1")
         w1_raw.append(load_w1(1, "then_cand_0"))
         v_words = [gather_words(0, "first_half")]
@@ -129,22 +133,23 @@ def tile_list_hyper_relational_scoring_kernel(
             w3_raw[:].rearrange("p (b m t) -> p b m t", b=2, t=4),
         )
         w3_codes = [w3_all[:, 0:HALF], w3_all[:, HALF:]]
-        v_scales.append(gather_scales(1, "then_second_half", nc.sync))
         v_words.append(gather_words(1, "then_second_words"))
-        load_cand(0, HALF, N, "then_last_loads")
-        load_cand(1, 0, N, "then_second_half")
+        load_cand(0, HALF, N, "then_cand_0_rest")
+        load_cand(1, 0, 2 * P, "then_cand_1")
 
-        w1_codes = [keep.tile([P, HALF], U32, name="w1_codes%d" % b, align_bytes=64) for b in range(2)]
-        w1_planes = [keep.tile([P, HALF], U8, name="w1_plane%d" % b, align_bytes=64) for b in range(2)]
-        cand_codes = [keep.tile([P, N], U32, name="cand_codes%d" % b, align_bytes=64) for b in range(2)]
-        cand_planes = [keep.tile([P, N], U8, name="cand_plane%d" % b, align_bytes=64) for b in range(2)]
         w1_round = [keep.tile([P, 4 * HALF], BF16, name="w1_round%d" % b, tag=tag, align_bytes=64) for b, tag in enumerate(("gpsimd_turn", "w1_round1"))]
         cand_round = {}
-        scaled, pair, h_codes, h_planes, h_rounds = {}, {}, {}, {}, {}
+        scaled, pair, h_rounds = {}, {}, {}
+        w1_mx, cand_mx, h_mx = {}, {}, {}
+
+        def quantise(name, rounded, width, slot):
+            codes = keep.tile([P, width], U32, name=name + "_codes", tag=slot or name + "_codes", align_bytes=64)
+            plane = keep.tile([P, width], U8, name=name + "_plane", align_bytes=64)
+            nc.vector.quantize_mx(out=codes[:].bitcast(FP8X4), scales=plane[:], in_=rounded)
+            return codes, plane
+
         for h in range(2):
             for b in range(2):
-                h_codes[h, b] = keep.tile([P, HALF], U32, name="h_codes%d%d" % (h, b), align_bytes=64)
-                h_planes[h, b] = keep.tile([P, HALF], U8, name="h_plane%d%d" % (h, b), align_bytes=64)
                 h_rounds[h, b] = keep.tile([P, 4 * HALF], BF16, name="h_round%d%d" % (h, b), align_bytes=64)
 
         def round_w1(engine, b, lo, hi):
@@ -152,14 +157,14 @@ def tile_list_hyper_relational_scoring_kernel(
             dst = w1_round[b][:].rearrange("p (t m j) -> p m j t", t=4, j=4)
             engine(dst[:, lo:hi], src[:, lo:hi])
 
-        def quantise_w1(b):
-            nc.vector.quantize_mx(out=w1_codes[b][:].bitcast(FP8X4), scales=w1_planes[b][:], in_=w1_round[b][:])
+        def quantise_w1(b, slot):
+            w1_mx[b] = quantise("w1_%d" % b, w1_round[b][:], HALF, slot)
 
-        def round_cand_scalar(b, lo, hi):
+        def round_cand(engine, b, lo, hi):
             cand_round[b, lo] = keep.tile([P, 4 * (hi - lo)], BF16, name="cand_round%d_%d" % (b, lo), align_bytes=64)
             dst = cand_round[b, lo][:].rearrange("p (c e t) -> p c t e", e=4, t=4)
             src = cand_columns(b, lo, hi).rearrange("p t (c e) -> p c t e", e=4)
-            nc.scalar.copy(dst, src)
+            engine(dst, src)
 
         def round_cand_gpsimd(b, lo, hi):
             cand_round[b, lo] = keep.tile(
@@ -169,17 +174,18 @@ def tile_list_hyper_relational_scoring_kernel(
             src = cand_columns(b, lo, hi).rearrange("p t c -> p c t")
             nc.gpsimd.tensor_scalar(dst, src, 1.0, 0.0, MULT, ADD)
 
-        def quantise_cand(b, lo, hi):
-            nc.vector.quantize_mx(
-                out=cand_codes[b][:, lo:hi].bitcast(FP8X4), scales=cand_planes[b][:, lo:hi], in_=cand_round[b, lo][:]
-            )
+        def quantise_cand(b, lo, hi, slot):
+            codes, plane = quantise("cand%d_%d" % (b, lo), cand_round[b, lo][:], hi - lo, slot)
+            for c in range(lo // P, hi // P):
+                cols = slice(c * P - lo, (c + 1) * P - lo)
+                cand_mx[b, c] = codes[:, cols], plane[:, cols]
 
         steps = [(0, 0, HALF, b, t) for b in range(2) for t in range(4)]
         steps = steps + [(1, lo, 2 * P, b, t) for lo in (0, 2 * P) for b in range(2) for t in (0, 2)]
 
-        def projection(step, codes, plane, fmt):
+        def projection(step, codes, plane, fmt, after=None):
             h, lo, width, b, t0 = step
-            bank = next_bank(HALF // width)
+            bank = next_bank(HALF // width, after)
             for g in range(HALF // width):
                 t = t0 + g
                 nc.tensor.matmul_mx(
@@ -193,36 +199,39 @@ def tile_list_hyper_relational_scoring_kernel(
                 )
             return bank
 
-        def scale_x2(k):
+        pair_bank = {}
+
+        def scale_x2(k, after=None):
             h, lo, width, b, t0 = steps[k]
             bank = projection(
-                steps[k], lambda b, t: w2_all[:, (4 * b + t) * P // 2 : (4 * b + t + 1) * P // 2], w2_plane, FP4X4
+                steps[k], lambda b, t: w2_all[:, (4 * b + t) * P // 2 : (4 * b + t + 1) * P // 2], w2_plane, FP4X4, after
             )
             scaled[k] = keep.tile([P, HALF // width, width], F32, name="scaled%d" % k, align_bytes=64)
             for g in range(HALF // width):
                 t = t0 + g
                 nc.scalar.activation(scaled[k][:, g, :], bank[:, g, :], ACT.Copy, scale=rel_cols[:, b, t : t + 1])
 
-        def pair_product(k):
+        def pair_product(k, slot=None):
             h, lo, width, b, t0 = steps[k]
             bank = projection(steps[k], lambda b, t: w3_codes[b][:, t * P : (t + 1) * P], w3_plane, FP8X4)
+            pair_bank[k] = taken[-1]
             if (h, lo, b) not in pair:
-                pair[h, lo, b] = keep.tile([P, 4, width], F32, name="pair%d_%d_%d" % (h, lo, b), align_bytes=64)
+                name = "pair%d_%d_%d" % (h, lo, b)
+                pair[h, lo, b] = keep.tile([P, 4, width], F32, name=name, tag=slot or name, align_bytes=64)
             nc.vector.tensor_tensor(pair[h, lo, b][:, t0 : t0 + HALF // width, :], bank[:], scaled[k][:], MULT)
 
         x3_rows = {}
 
-        def copy_x3(k, tag):
+        def copy_x3(k, tag, after=None):
             h, lo, width, b, t0 = steps[k]
-            bank = projection(steps[k], lambda b, t: w3_codes[b][:, t * P : (t + 1) * P], w3_plane, FP8X4)
+            bank = projection(steps[k], lambda b, t: w3_codes[b][:, t * P : (t + 1) * P], w3_plane, FP8X4, after)
             x3_rows[k] = keep.tile([P, HALF // width, width], F32, name="x3_%d" % k, tag=tag, align_bytes=64)
             nc.scalar.copy(x3_rows[k][:], bank[:])
 
-        def pair_product_gpsimd(k):
+        def pair_product_gpsimd(k, slot):
             h, lo, width, b, t0 = steps[k]
             if (h, lo, b) not in pair:
-                both = keep.tile([P, 2, 4, width], F32, name="pair_gpsimd", tag="gpsimd_turn", align_bytes=64)
-                pair[h, lo, 0], pair[h, lo, 1] = both[:, 0], both[:, 1]
+                pair[h, lo, b] = keep.tile([P, 4, width], F32, name="pair%d_%d_%d" % (h, lo, b), tag=slot, align_bytes=64)
             nc.gpsimd.tensor_tensor(pair[h, lo, b][:, t0 : t0 + HALF // width, :], x3_rows[k][:], scaled[k][:], MULT)
 
         def triple_product(h, b, q):
@@ -232,8 +241,8 @@ def tile_list_hyper_relational_scoring_kernel(
             for t in range(4):
                 nc.tensor.matmul_mx(
                     out=x1[:, t, :],
-                    lhsT=w1_codes[b][:, t * P : (t + 1) * P].bitcast(FP8X4),
-                    lhsT_scale=w1_planes[b][:, t * P : (t + 1) * P],
+                    lhsT=w1_mx[b][0][:, t * P : (t + 1) * P].bitcast(FP8X4),
+                    lhsT_scale=w1_mx[b][1][:, t * P : (t + 1) * P],
                     rhs=v_words[h][:, cols].bitcast(FP8X4),
                     rhs_scale=v_scales[h][:, cols],
                     start=True,
@@ -246,12 +255,8 @@ def tile_list_hyper_relational_scoring_kernel(
                 MULT,
             )
 
-        def quantise_h(h, b, lo, hi):
-            nc.vector.quantize_mx(
-                out=h_codes[h, b][:, lo:hi].bitcast(FP8X4),
-                scales=h_planes[h, b][:, lo:hi],
-                in_=h_rounds[h, b][:, 4 * lo : 4 * hi],
-            )
+        def quantise_h(h, b, lo, hi, slot=None):
+            h_mx[h, b, lo] = quantise("h%d%d_%d" % (h, b, lo), h_rounds[h, b][:, 4 * lo : 4 * hi], hi - lo, slot)
 
         out_view = out.rearrange("(c p) j -> p c j", p=P)
 
@@ -260,10 +265,10 @@ def tile_list_hyper_relational_scoring_kernel(
                 c = c0 + g
                 nc.tensor.matmul_mx(
                     out=bank[:, g, :],
-                    lhsT=cand_codes[b][:, c * P : (c + 1) * P].bitcast(FP8X4),
-                    lhsT_scale=cand_planes[b][:, c * P : (c + 1) * P],
-                    rhs=h_codes[h, b][:, lo : lo + width].bitcast(FP8X4),
-                    rhs_scale=h_planes[h, b][:, lo : lo + width],
+                    lhsT=cand_mx[b, c][0].bitcast(FP8X4),
+                    lhsT_scale=cand_mx[b, c][1],
+                    rhs=h_mx[h, b, lo][0][:].bitcast(FP8X4),
+                    rhs_scale=h_mx[h, b, lo][1][:],
                     start=(b == 0 and g == 0),
                     stop=(b == 1 and g == count - 1),
                 )
@@ -319,56 +324,54 @@ def tile_list_hyper_relational_scoring_kernel(
         scale_x2(4)
         round_w1(on_vector, 0, 64, P)
         scale_x2(5)
-        prior_cols = load_prior()
-        quantise_w1(0)
+        load_cand(1, 2 * P, N, "then_w1_0")
+        quantise_w1(0, None)
         round_cand_gpsimd(0, 0, HALF)
         for q in range(4):
-            if q < 2:
-                scale_x2(6 + q)
+            scale_x2(6 + q)
             triple_product(0, 0, q)
+        for k in range(4, 6):
+            scale_x2(6 + k)
+            pair_product(k)
         round_w1(on_scalar, 1, 0, 64)
         round_w1(on_scalar, 1, 64, P)
-        for k in range(4, 8):
-            pair_product(k)
-        round_cand_scalar(0, HALF, N)
-        quantise_w1(1)
-        round_cand_scalar(1, 2 * P, N)
-        quantise_h(0, 0, 0, HALF)
-        quantise_cand(0, 0, HALF)
+        pair_product(6)
+        pair_product(7)
+        prior_cols = load_prior()
+        round_cand(on_scalar, 0, HALF, N)
+        quantise_w1(1, "scaled7")
+        quantise_h(0, 0, 0, HALF, "then_w1_1")
+        quantise_cand(0, 0, HALF, None)
         round_cand_gpsimd(1, 0, 2 * P)
+        for k in (12, 13):
+            scale_x2(k)
+            copy_x3(k, "x3_%d" % k)
+            pair_product_gpsimd(k, "then_cand_1")
         for q in range(4):
             triple_product(0, 1, q)
-            scale_x2(8 + q)
-        scale_x2(12)
-        quantise_h(0, 1, 0, HALF)
-        copy_x3(12, "x3_12")
-        quantise_cand(0, HALF, N)
-        scale_x2(13)
-        quantise_cand(1, 2 * P, N)
-        copy_x3(13, "x3_13")
-        quantise_cand(1, 0, 2 * P)
-        pair_product_gpsimd(12)
-        pair_product_gpsimd(13)
-        pair_product(8)
-        scale_x2(14)
-        pair_product(9)
-        copy_x3(14, "x3_14")
-        pair_product_gpsimd(14)
-        pair_product(10)
-        score(0, 0, HALF, 0, 1, 1)
-        pair_product(11)
-        scale_x2(15)
+        round_cand(on_scalar, 1, 2 * P, N)
+        for k, slot in zip(range(8, 12), ("w1_round1", None, "h_round00", None)):
+            pair_product(k, slot)
+        scale_x2(14, pair_bank[8])
+        quantise_h(0, 1, 0, HALF, "x3_13")
+        copy_x3(14, "x3_14", pair_bank[9])
+        quantise_cand(0, HALF, N, "scaled13")
+        scale_x2(15, pair_bank[10])
+        quantise_cand(1, 2 * P, N, "scaled11")
+        copy_x3(15, "x3_15", pair_bank[11])
+        quantise_cand(1, 0, 2 * P, "scaled10")
+        pair_product_gpsimd(14, "gpsimd_turn")
+        pair_product_gpsimd(15, "gpsimd_turn")
         triple_product(1, 0, 0)
-        copy_x3(15, "x3_15")
-        pair_product_gpsimd(15)
+        score(0, 0, HALF, 0, 2, 1)
         triple_product(1, 0, 1)
-        score(0, 0, HALF, 1, 2, 1)
         triple_product(1, 1, 0)
+        score(0, 0, HALF, 2, 2, 1)
         triple_product(1, 1, 1)
-        score(0, 0, HALF, 3, 3, 1)
         triple_product(1, 0, 2)
-        quantise_h(1, 0, 0, 2 * P)
-        quantise_h(1, 1, 0, 2 * P)
+        score(0, 0, HALF, 4, 2, 1)
+        quantise_h(1, 0, 0, 2 * P, "x3_15")
+        quantise_h(1, 1, 0, 2 * P, "scaled15")
         triple_product(1, 1, 2)
         score(1, 0, 2 * P, 0, 2, 2)
         quantise_h(1, 0, 2 * P, 3 * P)

@@ -54,7 +54,7 @@ def tile_list_hyper_relational_scoring_kernel(
             nc.sync.dma_start(
                 w_rows[w:32:2, :].bitcast(I32), scales[0].bitcast(I32).rearrange("(d q) c -> q d c", q=4)
             )
-        w2_raw = keep.tile([P, H // 2], I32, name="w2_raw", align_bytes=64)
+        w2_raw = keep.tile([P, H // 2], I32, name="w2_raw", tag="then_w1_1_rest", align_bytes=64)
         nc.sync.dma_start(w2_raw[:], w2_words[0].bitcast(I32))
         table = keep.tile([P, T], I32, name="table", tag="then_cand_1", align_bytes=64)
         nc.sync.dma_start(table[:], tab_words[0].rearrange("p n t -> p (n t)").bitcast(I32))
@@ -72,7 +72,7 @@ def tile_list_hyper_relational_scoring_kernel(
         nc.scalar.copy(w_rows[64:P, :].bitcast(U32), w_plane[64:P, 0:H].bitcast(U32))
 
         def load_prior():
-            cols = keep.tile([P, NT], F32, name="prior_cols", tag="then_cand_0", align_bytes=64)
+            cols = keep.tile([P, NT], F32, name="prior_cols", tag="scaled5", align_bytes=64)
             with nc.allow_non_contiguous_dma(reason="one prior for each partition and tile of candidates"):
                 nc.sync.dma_start(cols[:], prior.rearrange("(c p) -> p c", p=P))
             return cols
@@ -90,10 +90,14 @@ def tile_list_hyper_relational_scoring_kernel(
             nc.vector.tensor_copy(words[:].bitcast(U32), table[:].bitcast(U32).indirect(lists(h)))
             return words
 
-        def load_w1(b, tag):
-            raw = keep.tile([P, 4, HALF], F32, name="w1_raw%d" % b, tag=tag, align_bytes=64)
-            nc.sync.dma_start(raw[:], w1[:, b * HALF : (b + 1) * HALF].rearrange("(p j) c -> p j c", j=4))
-            return raw
+        w1_raw = {}
+
+        def load_w1(b, lo, hi, tag):
+            raw = keep.tile([P, 4, 4 * (hi - lo)], F32, name="w1_raw%d_%d" % (b, lo), tag=tag, align_bytes=64)
+            columns = w1[:, b * HALF + 4 * lo : b * HALF + 4 * hi]
+            nc.sync.dma_start(raw[:], columns.rearrange("(p j) c -> p j c", j=4))
+            for m in range(lo, hi, 64):
+                w1_raw[b, m] = raw[:, :, 4 * (m - lo) : 4 * (m - lo + 64)]
 
         cand_raw = {}
 
@@ -118,14 +122,15 @@ def tile_list_hyper_relational_scoring_kernel(
         w2_plane = w_plane[:, 0:H]
         w3_plane = w_plane[:, H:]
         gather_scales(1, "then_cand_0_rest", nc.sync)
-        w1_raw = [load_w1(0, "then_w1_0")]
+        load_w1(0, 0, P, "then_w1_0")
         w2_all = keep.tile([P, H // 2], I32, name="w2_codes", align_bytes=64)
         nc.vector.tensor_copy(
             w2_all[:].bitcast(U16).rearrange("p (b t m) -> p b t m", b=2, t=4),
             w2_raw[:].bitcast(U16).rearrange("p (b m t) -> p b t m", b=2, t=4),
         )
         load_cand(0, 0, HALF, "then_w1_1")
-        w1_raw.append(load_w1(1, "then_cand_0"))
+        load_w1(1, 0, 64, "then_cand_0")
+        load_w1(1, 64, P, "then_w1_1_rest")
         v_words = [gather_words(0, "first_half")]
         w3_all = keep.tile([P, H], I32, name="w3_codes", align_bytes=64)
         nc.vector.tensor_copy(
@@ -148,14 +153,21 @@ def tile_list_hyper_relational_scoring_kernel(
             nc.vector.quantize_mx(out=codes[:].bitcast(FP8X4), scales=plane[:], in_=rounded)
             return codes, plane
 
-        for h in range(2):
-            for b in range(2):
-                h_rounds[h, b] = keep.tile([P, 4 * HALF], BF16, name="h_round%d%d" % (h, b), align_bytes=64)
+        for b in range(2):
+            whole = keep.tile([P, 4 * HALF], BF16, name="h_round0%d" % b, align_bytes=64)
+            for q in range(4):
+                h_rounds[0, b, q] = whole[:, 4 * q * P : 4 * (q + 1) * P]
+            h_rounds[0, b] = whole[:]
+            for q in range(2, 4):
+                h_rounds[1, b, q] = keep.tile([P, 4 * P], BF16, name="h_round1%d%d" % (b, q), align_bytes=64)[:]
+        third = keep.tile([P, 2, 2, 4 * P], BF16, name="h_round_third", align_bytes=64)
+        for b in range(2):
+            for q in range(2):
+                h_rounds[1, b, q] = third[:, b, q, :]
 
-        def round_w1(engine, b, lo, hi):
-            src = w1_raw[b][:].rearrange("p j (m t) -> p m j t", t=4)
+        def round_w1(engine, b, lo):
             dst = w1_round[b][:].rearrange("p (t m j) -> p m j t", t=4, j=4)
-            engine(dst[:, lo:hi], src[:, lo:hi])
+            engine(dst[:, lo : lo + 64], w1_raw[b, lo].rearrange("p j (m t) -> p m j t", t=4))
 
         def quantise_w1(b, slot):
             w1_mx[b] = quantise("w1_%d" % b, w1_round[b][:], HALF, slot)
@@ -201,12 +213,12 @@ def tile_list_hyper_relational_scoring_kernel(
 
         pair_bank = {}
 
-        def scale_x2(k, after=None):
+        def scale_x2(k, after=None, slot=None):
             h, lo, width, b, t0 = steps[k]
             bank = projection(
                 steps[k], lambda b, t: w2_all[:, (4 * b + t) * P // 2 : (4 * b + t + 1) * P // 2], w2_plane, FP4X4, after
             )
-            scaled[k] = keep.tile([P, HALF // width, width], F32, name="scaled%d" % k, align_bytes=64)
+            scaled[k] = keep.tile([P, HALF // width, width], F32, name="scaled%d" % k, tag=slot or "scaled%d" % k, align_bytes=64)
             for g in range(HALF // width):
                 t = t0 + g
                 nc.scalar.activation(scaled[k][:, g, :], bank[:, g, :], ACT.Copy, scale=rel_cols[:, b, t : t + 1])
@@ -249,14 +261,25 @@ def tile_list_hyper_relational_scoring_kernel(
                     stop=True,
                 )
             nc.vector.tensor_tensor(
-                h_rounds[h, b][:, 4 * q * P : 4 * (q + 1) * P].rearrange("p (n e t) -> p n t e", e=2, t=4),
+                h_rounds[h, b, q].rearrange("p (n e t) -> p n t e", e=2, t=4),
                 x1[:].rearrange("p t (n e) -> p n t e", e=2),
                 pair[h, lo, b][:, :, q * P - lo : (q + 1) * P - lo].rearrange("p t (n e) -> p n t e", e=2),
                 MULT,
             )
 
-        def quantise_h(h, b, lo, hi, slot=None):
-            h_mx[h, b, lo] = quantise("h%d%d_%d" % (h, b, lo), h_rounds[h, b][:, 4 * lo : 4 * hi], hi - lo, slot)
+        def quantise_first_half(b, slot):
+            codes, plane = quantise("h0%d" % b, h_rounds[0, b], HALF, slot)
+            h_mx[0, b, 0] = codes[:], plane[:]
+
+        def quantise_third(slot):
+            codes, plane = quantise("h_third", third[:].rearrange("p b q n -> p (b q n)"), HALF, slot)
+            for b in range(2):
+                cols = slice(b * 2 * P, (b + 1) * 2 * P)
+                h_mx[1, b, 0] = codes[:, cols], plane[:, cols]
+
+        def quantise_eighth(b, q):
+            codes, plane = quantise("h1%d%d" % (b, q), h_rounds[1, b, q], P, None)
+            h_mx[1, b, q * P] = codes[:], plane[:]
 
         out_view = out.rearrange("(c p) j -> p c j", p=P)
 
@@ -267,8 +290,8 @@ def tile_list_hyper_relational_scoring_kernel(
                     out=bank[:, g, :],
                     lhsT=cand_mx[b, c][0].bitcast(FP8X4),
                     lhsT_scale=cand_mx[b, c][1],
-                    rhs=h_mx[h, b, lo][0][:].bitcast(FP8X4),
-                    rhs_scale=h_mx[h, b, lo][1][:],
+                    rhs=h_mx[h, b, lo][0].bitcast(FP8X4),
+                    rhs_scale=h_mx[h, b, lo][1],
                     start=(b == 0 and g == 0),
                     stop=(b == 1 and g == count - 1),
                 )
@@ -315,14 +338,16 @@ def tile_list_hyper_relational_scoring_kernel(
             store(staged, 1, q * P, P, c0, 3)
 
         on_scalar, on_vector = nc.scalar.copy, nc.vector.tensor_copy
-        for k in range(4):
+        for k in range(3):
             scale_x2(k)
         pair_product(0)
-        round_w1(on_scalar, 0, 0, 64)
-        for k in range(1, 4):
-            pair_product(k)
+        scale_x2(3)
+        pair_product(1)
+        round_w1(on_scalar, 0, 0)
+        pair_product(2)
+        pair_product(3)
         scale_x2(4)
-        round_w1(on_vector, 0, 64, P)
+        round_w1(on_vector, 0, 64)
         scale_x2(5)
         load_cand(1, 2 * P, N, "then_w1_0")
         quantise_w1(0, None)
@@ -330,59 +355,58 @@ def tile_list_hyper_relational_scoring_kernel(
         for q in range(4):
             scale_x2(6 + q)
             triple_product(0, 0, q)
-        for k in range(4, 6):
-            scale_x2(6 + k)
+        round_w1(on_scalar, 1, 0)
+        round_w1(on_scalar, 1, 64)
+        for k in range(4, 8):
             pair_product(k)
-        round_w1(on_scalar, 1, 0, 64)
-        round_w1(on_scalar, 1, 64, P)
-        pair_product(6)
-        pair_product(7)
         prior_cols = load_prior()
         round_cand(on_scalar, 0, HALF, N)
-        quantise_w1(1, "scaled7")
-        quantise_h(0, 0, 0, HALF, "then_w1_1")
+        scale_x2(10, slot="then_cand_0")
+        scale_x2(11, slot="then_w1_1_rest")
+        quantise_w1(1, "scaled6")
+        quantise_first_half(0, "then_w1_1")
         quantise_cand(0, 0, HALF, None)
         round_cand_gpsimd(1, 0, 2 * P)
-        for k in (12, 13):
-            scale_x2(k)
-            copy_x3(k, "x3_%d" % k)
+        for k, x2_slot, x3_slot in ((12, "w1_round1", "h_round00"), (13, "then_cand_0_rest", "scaled7")):
+            scale_x2(k, slot=x2_slot)
+            copy_x3(k, x3_slot)
             pair_product_gpsimd(k, "then_cand_1")
         for q in range(4):
             triple_product(0, 1, q)
         round_cand(on_scalar, 1, 2 * P, N)
-        for k, slot in zip(range(8, 12), ("w1_round1", None, "h_round00", None)):
-            pair_product(k, slot)
+        for k in range(8, 12):
+            pair_product(k)
         scale_x2(14, pair_bank[8])
-        quantise_h(0, 1, 0, HALF, "x3_13")
+        quantise_first_half(1, "scaled7")
         copy_x3(14, "x3_14", pair_bank[9])
-        quantise_cand(0, HALF, N, "scaled13")
+        quantise_cand(1, 0, 2 * P, "then_cand_0_rest")
         scale_x2(15, pair_bank[10])
-        quantise_cand(1, 2 * P, N, "scaled11")
+        quantise_cand(1, 2 * P, N, "then_w1_1_rest")
         copy_x3(15, "x3_15", pair_bank[11])
-        quantise_cand(1, 0, 2 * P, "scaled10")
-        pair_product_gpsimd(14, "gpsimd_turn")
-        pair_product_gpsimd(15, "gpsimd_turn")
+        quantise_cand(0, HALF, N, "then_cand_0")
+        pair_product_gpsimd(14, "cand_round0_512")
+        pair_product_gpsimd(15, "cand_round0_512")
+        score(0, 0, HALF, 0, 1, 1)
+        score(0, 0, HALF, 1, 1, 1)
         triple_product(1, 0, 0)
-        score(0, 0, HALF, 0, 2, 1)
         triple_product(1, 0, 1)
-        triple_product(1, 1, 0)
         score(0, 0, HALF, 2, 2, 1)
+        triple_product(1, 1, 0)
         triple_product(1, 1, 1)
-        triple_product(1, 0, 2)
         score(0, 0, HALF, 4, 2, 1)
-        quantise_h(1, 0, 0, 2 * P, "x3_15")
-        quantise_h(1, 1, 0, 2 * P, "scaled15")
+        triple_product(1, 0, 2)
+        quantise_third("x3_15")
         triple_product(1, 1, 2)
         score(1, 0, 2 * P, 0, 2, 2)
-        quantise_h(1, 0, 2 * P, 3 * P)
+        quantise_eighth(0, 2)
         triple_product(1, 0, 3)
         score(1, 0, 2 * P, 2, 4, 2)
-        quantise_h(1, 1, 2 * P, 3 * P)
+        quantise_eighth(1, 2)
         triple_product(1, 1, 3)
-        quantise_h(1, 0, 3 * P, 4 * P)
+        quantise_eighth(0, 3)
         score(1, 2 * P, P, 0, NT, 3)
         last = open_scores(3)
-        quantise_h(1, 1, 3 * P, 4 * P)
+        quantise_eighth(1, 3)
         close_scores(3, last)
         finish_scores(3, last[0], 0, False)
         finish_scores(3, last[1], 3, True)

@@ -128,7 +128,7 @@ def tile_list_hyper_relational_scoring_kernel(
             w2_all[:].bitcast(U16).rearrange("p (b t m) -> p b t m", b=2, t=4),
             w2_raw[:].bitcast(U16).rearrange("p (b m t) -> p b t m", b=2, t=4),
         )
-        load_cand(0, 0, HALF, "then_w1_1")
+        load_cand(0, 0, 384, "then_w1_1")
         load_w1(1, 0, 64, "then_cand_0")
         load_w1(1, 64, P, "then_w1_1_rest")
         v_words = [gather_words(0, "first_half")]
@@ -139,8 +139,8 @@ def tile_list_hyper_relational_scoring_kernel(
         )
         w3_codes = [w3_all[:, 0:HALF], w3_all[:, HALF:]]
         v_words.append(gather_words(1, "then_second_words"))
-        load_cand(0, HALF, N, "then_cand_0_rest")
-        load_cand(1, 0, 2 * P, "then_cand_1")
+        load_cand(0, 384, N, "then_cand_0_rest")
+        load_cand(1, 0, 160, "then_cand_1")
 
         w1_round = [keep.tile([P, 4 * HALF], BF16, name="w1_round%d" % b, tag=tag, align_bytes=64) for b, tag in enumerate(("gpsimd_turn", "w1_round1"))]
         cand_round = {}
@@ -178,13 +178,17 @@ def tile_list_hyper_relational_scoring_kernel(
             src = cand_columns(b, lo, hi).rearrange("p t (c e) -> p c t e", e=4)
             engine(dst, src)
 
-        def round_cand_gpsimd(b, lo, hi):
+        def round_cand_gpsimd(b, lo, cut, hi):
             cand_round[b, lo] = keep.tile(
                 [P, 4 * (hi - lo)], BF16, name="cand_round%d_%d" % (b, lo), tag="gpsimd_turn", align_bytes=64
             )
-            dst = cand_round[b, lo][:].rearrange("p (c t) -> p c t", t=4)
-            src = cand_columns(b, lo, hi).rearrange("p t c -> p c t")
+            dst = cand_round[b, lo][:, 0 : 4 * (cut - lo)].rearrange("p (c t) -> p c t", t=4)
+            src = cand_columns(b, lo, cut).rearrange("p t c -> p c t")
             nc.gpsimd.tensor_scalar(dst, src, 1.0, 0.0, MULT, ADD)
+
+        def round_cand_rest(b, lo, cut, hi):
+            dst = cand_round[b, lo][:, 4 * (cut - lo) :].rearrange("p (c e t) -> p c t e", e=4, t=4)
+            nc.scalar.copy(dst, cand_columns(b, cut, hi).rearrange("p t (c e) -> p c t e", e=4))
 
         def quantise_cand(b, lo, hi, slot):
             codes, plane = quantise("cand%d_%d" % (b, lo), cand_round[b, lo][:], hi - lo, slot)
@@ -349,9 +353,9 @@ def tile_list_hyper_relational_scoring_kernel(
         scale_x2(4)
         round_w1(on_vector, 0, 64)
         scale_x2(5)
-        load_cand(1, 2 * P, N, "then_w1_0")
+        load_cand(1, 160, N, "then_w1_0")
         quantise_w1(0, None)
-        round_cand_gpsimd(0, 0, HALF)
+        round_cand_gpsimd(0, 0, 384, HALF)
         for q in range(4):
             scale_x2(6 + q)
             triple_product(0, 0, q)
@@ -360,19 +364,21 @@ def tile_list_hyper_relational_scoring_kernel(
         for k in range(4, 8):
             pair_product(k)
         prior_cols = load_prior()
+        round_cand_rest(0, 0, 384, HALF)
         round_cand(on_scalar, 0, HALF, N)
         scale_x2(10, slot="then_cand_0")
         scale_x2(11, slot="then_w1_1_rest")
         quantise_w1(1, "scaled6")
         quantise_first_half(0, "then_w1_1")
         quantise_cand(0, 0, HALF, None)
-        round_cand_gpsimd(1, 0, 2 * P)
+        round_cand_gpsimd(1, 0, 160, 2 * P)
         for k, x2_slot, x3_slot in ((12, "w1_round1", "h_round00"), (13, "then_cand_0_rest", "scaled7")):
             scale_x2(k, slot=x2_slot)
             copy_x3(k, x3_slot)
             pair_product_gpsimd(k, "then_cand_1")
         for q in range(4):
             triple_product(0, 1, q)
+        round_cand_rest(1, 0, 160, 2 * P)
         round_cand(on_scalar, 1, 2 * P, N)
         for k in range(8, 12):
             pair_product(k)

@@ -84,6 +84,7 @@ def tile_list_hyper_relational_scoring_kernel(
             picked = keep.tile([P, HALF], U8, name="picked%d" % h, tag=tag, align_bytes=64)
             nc.vector.tensor_copy(picked[:], tab_rows[:].indirect(lists(h)))
             queue.dma_start(v_scales[h][0:112, :].bitcast(I32), picked[14:126, :].bitcast(I32))
+            return picked
 
         def gather_words(h, tag):
             words = keep.tile([P, HALF], I32, name="v_words%d" % h, tag=tag, align_bytes=64)
@@ -110,7 +111,7 @@ def tile_list_hyper_relational_scoring_kernel(
             first = max(start for (pass_, start) in cand_raw if pass_ == b and start <= lo)
             return cand_raw[b, first][:, :, lo - first : hi - first]
 
-        gather_scales(0, "then_w1_1", nc.sync)
+        first_picked = gather_scales(0, "then_w1_1", nc.sync)
         w_dealt = keep.tile([P, H], U8, name="w_dealt", tag="then_cand_0", align_bytes=64)
         nc.vector.tensor_copy(
             w_dealt[:].rearrange("p (b t m) -> p b t m", b=2, t=4),
@@ -128,6 +129,17 @@ def tile_list_hyper_relational_scoring_kernel(
             w2_all[:].bitcast(U16).rearrange("p (b t m) -> p b t m", b=2, t=4),
             w2_raw[:].bitcast(U16).rearrange("p (b m t) -> p b t m", b=2, t=4),
         )
+        idle_bank = next_bank(1)
+        for i in range(3):
+            nc.tensor.matmul_mx(
+                out=idle_bank[:, 0, :],
+                lhsT=w2_raw[:, 0 : P // 2].bitcast(FP4X4),
+                lhsT_scale=first_picked[:, 0:P],
+                rhs=table[:, 0:HALF].bitcast(FP8X4),
+                rhs_scale=first_picked[:],
+                start=True,
+                stop=True,
+            )
         load_cand(0, 0, 384, "then_w1_1")
         load_w1(1, 0, 64, "then_cand_0")
         load_w1(1, 64, P, "then_w1_1_rest")

@@ -20,7 +20,10 @@ ACT = mybir.ActivationFunctionType
 P = 128
 HALF = 512
 BANKS = 8
-NT = N // P
+TILES = N // P
+M_PIECE = 64
+GPSIMD_FIRST, GPSIMD_SECOND = 384, 160
+WARM_UP_PASSES = 3
 
 
 def tile_list_hyper_relational_scoring_kernel(
@@ -30,49 +33,52 @@ def tile_list_hyper_relational_scoring_kernel(
     with ExitStack() as ctx:
         keep = ctx.enter_context(tc.tile_pool(name="keep", bufs=1))
         psum = ctx.enter_context(tc.psum_pool(name="psum", bufs=1))
-        taken = []
 
-        turn = []
+        def sbuf(name, shape, dtype, after=None):
+            return keep.tile(shape, dtype, name=name, tag=after or name, align_bytes=64)
+
+        banks_taken, banks_in_turn = [], []
 
         def next_bank(groups, bank=None):
             if bank is None:
-                bank = len(turn) % BANKS
-                turn.append(bank)
-            taken.append(bank)
-            return psum.tile([P, groups, HALF // groups], F32, name="ps%d" % len(taken), tag="bank%d" % bank)
+                bank = len(banks_in_turn) % BANKS
+                banks_in_turn.append(bank)
+            banks_taken.append(bank)
+            return psum.tile([P, groups, HALF // groups], F32, name="ps%d" % len(banks_taken), tag="bank%d" % bank)
 
         offsets = keep.tile([P, S // 16], U16, name="offsets")
         nc.sync.dma_start(offsets[:], offs)
-        tab_rows = keep.tile([P, T], U8, name="tab_rows", tag="then_w1_0", align_bytes=64)
+        tab_rows = sbuf("tab_rows", [P, T], U8)
         scale_words = tab_scales[0].bitcast(I32)
         for e in range(2):
             nc.sync.dma_start(
                 tab_rows[e:P:2, :].bitcast(I32), scale_words[e:16:2, :].unsqueeze(1).to_broadcast([8, 8, T // 4])
             )
-        w_rows = keep.tile([P, H], U8, name="w_rows", tag="then_cand_0_rest", align_bytes=64)
+        w_rows = sbuf("w_rows", [P, H], U8)
         for w, scales in enumerate((w2_scales, w3_scales)):
             nc.sync.dma_start(
                 w_rows[w:32:2, :].bitcast(I32), scales[0].bitcast(I32).rearrange("(d q) c -> q d c", q=4)
             )
-        w2_raw = keep.tile([P, H // 2], I32, name="w2_raw", tag="then_w1_1_rest", align_bytes=64)
+        w2_raw = sbuf("w2_raw", [P, H // 2], I32)
         nc.sync.dma_start(w2_raw[:], w2_words[0].bitcast(I32))
-        table = keep.tile([P, T], I32, name="table", tag="then_cand_1", align_bytes=64)
+        table = sbuf("table", [P, T], I32)
         nc.sync.dma_start(table[:], tab_words[0].rearrange("p n t -> p (n t)").bitcast(I32))
-        w3_raw = keep.tile([P, H], I32, name="w3_raw", tag="then_second_words", align_bytes=64)
+        w3_raw = sbuf("w3_raw", [P, H], I32)
         nc.sync.dma_start(w3_raw[:], w3_words[0].rearrange("p n t -> p (n t)").bitcast(I32))
 
-        rel_cols = keep.tile([P, 2, 4], F32, name="rel_cols", align_bytes=64)
+        rel_cols = sbuf("rel_cols", [P, 2, 4], F32)
         nc.gpsimd.dma_start(rel_cols[:], rel.rearrange("(b p t) -> p b t", b=2, t=4))
-        w_plane = keep.tile([P, 2 * H], U8, name="w_plane", align_bytes=64)
+
+        w_plane = sbuf("w_plane", [P, 2 * H], U8)
         nc.vector.memset(w_plane[:].bitcast(I32), 0)
         nc.vector.memset(w_rows[32:64, :].bitcast(I32), 0)
-        v_scales = [keep.tile([P, HALF], U8, name="v_plane%d" % h, align_bytes=64) for h in range(2)]
-        for plane in v_scales:
+        v_planes = [sbuf("v_plane%d" % h, [P, HALF], U8) for h in range(2)]
+        for plane in v_planes:
             nc.vector.memset(plane[96:P, :].bitcast(I32), 0)
         nc.scalar.copy(w_rows[64:P, :].bitcast(U32), w_plane[64:P, 0:H].bitcast(U32))
 
-        def load_prior():
-            cols = keep.tile([P, NT], F32, name="prior_cols", tag="scaled5", align_bytes=64)
+        def load_prior(after):
+            cols = sbuf("prior_cols", [P, TILES], F32, after)
             with nc.allow_non_contiguous_dma(reason="one prior for each partition and tile of candidates"):
                 nc.sync.dma_start(cols[:], prior.rearrange("(c p) -> p c", p=P))
             return cols
@@ -80,351 +86,359 @@ def tile_list_hyper_relational_scoring_kernel(
         def lists(h):
             return offsets[:, h * (HALF // 16) : (h + 1) * (HALF // 16)]
 
-        def gather_scales(h, tag, queue):
-            picked = keep.tile([P, HALF], U8, name="picked%d" % h, tag=tag, align_bytes=64)
+        def gather_scales(h, after=None):
+            picked = sbuf("picked%d" % h, [P, HALF], U8, after)
             nc.vector.tensor_copy(picked[:], tab_rows[:].indirect(lists(h)))
-            queue.dma_start(v_scales[h][0:112, :].bitcast(I32), picked[14:126, :].bitcast(I32))
+            nc.sync.dma_start(v_planes[h][0:112, :].bitcast(I32), picked[14:126, :].bitcast(I32))
             return picked
 
-        def gather_words(h, tag):
-            words = keep.tile([P, HALF], I32, name="v_words%d" % h, tag=tag, align_bytes=64)
+        def gather_words(h, after=None):
+            words = sbuf("v_words%d" % h, [P, HALF], I32, after)
             nc.vector.tensor_copy(words[:].bitcast(U32), table[:].bitcast(U32).indirect(lists(h)))
             return words
 
-        w1_raw = {}
+        w1_raw, cand_raw = {}, {}
 
-        def load_w1(b, lo, hi, tag):
-            raw = keep.tile([P, 4, 4 * (hi - lo)], F32, name="w1_raw%d_%d" % (b, lo), tag=tag, align_bytes=64)
+        def load_w1(b, lo, hi, after):
+            raw = sbuf("w1_raw%d_%d" % (b, lo), [P, 4, 4 * (hi - lo)], F32, after)
             columns = w1[:, b * HALF + 4 * lo : b * HALF + 4 * hi]
             nc.sync.dma_start(raw[:], columns.rearrange("(p j) c -> p j c", j=4))
-            for m in range(lo, hi, 64):
-                w1_raw[b, m] = raw[:, :, 4 * (m - lo) : 4 * (m - lo + 64)]
+            for m in range(lo, hi, M_PIECE):
+                w1_raw[b, m] = raw[:, :, 4 * (m - lo) : 4 * (m - lo + M_PIECE)]
 
-        cand_raw = {}
-
-        def load_cand(b, lo, hi, tag):
-            raw = keep.tile([P, 4, hi - lo], F32, name="cand_raw%d_%d" % (b, lo), tag=tag, align_bytes=64)
-            nc.sync.dma_start(raw[:], cand[b * HALF : (b + 1) * HALF, lo:hi].rearrange("(p j) n -> p j n", j=4))
+        def load_cand(b, lo, hi, after):
+            raw = sbuf("cand_raw%d_%d" % (b, lo), [P, 4, hi - lo], F32, after)
+            nc.sync.dma_start(raw[:], cand[b * HALF : (b + 1) * HALF, lo:hi].rearrange("(p t) n -> p t n", t=4))
             cand_raw[b, lo] = raw
 
         def cand_columns(b, lo, hi):
-            first = max(start for (pass_, start) in cand_raw if pass_ == b and start <= lo)
+            first = max(start for (of_pass, start) in cand_raw if of_pass == b and start <= lo)
             return cand_raw[b, first][:, :, lo - first : hi - first]
 
-        first_picked = gather_scales(0, "then_w1_1", nc.sync)
-        w_dealt = keep.tile([P, H], U8, name="w_dealt", tag="then_cand_0", align_bytes=64)
+        picked0 = gather_scales(0)
+        w_dealt = sbuf("w_dealt", [P, H], U8)
         nc.vector.tensor_copy(
             w_dealt[:].rearrange("p (b t m) -> p b t m", b=2, t=4),
             w_rows[:].rearrange("p (b m t) -> p b t m", b=2, t=4),
         )
-        w_planes = w_plane[:].bitcast(I32).rearrange("p (w c) -> p w c", w=2)
+        w_plane_words = w_plane[:].bitcast(I32).rearrange("p (w c) -> p w c", w=2)
         for q in range(4):
-            nc.scalar.dma_start(w_planes[q:P:32], w_dealt[8 * q : 8 * q + 8, :].bitcast(I32))
+            nc.sync.dma_start(w_plane_words[q:P:32], w_dealt[8 * q : 8 * q + 8, :].bitcast(I32))
         w2_plane = w_plane[:, 0:H]
         w3_plane = w_plane[:, H:]
-        gather_scales(1, "then_cand_0_rest", nc.sync)
-        load_w1(0, 0, P, "then_w1_0")
-        w2_all = keep.tile([P, H // 2], I32, name="w2_codes", align_bytes=64)
+        load_w1(0, 0, P, after="w_rows")
+        w2_codes = sbuf("w2_codes", [P, H // 2], I32)
         nc.vector.tensor_copy(
-            w2_all[:].bitcast(U16).rearrange("p (b t m) -> p b t m", b=2, t=4),
+            w2_codes[:].bitcast(U16).rearrange("p (b t m) -> p b t m", b=2, t=4),
             w2_raw[:].bitcast(U16).rearrange("p (b m t) -> p b t m", b=2, t=4),
         )
-        idle_bank = next_bank(1)
-        for i in range(3):
+        gather_scales(1, after="w2_raw")
+        unread = next_bank(1)
+        for repeat in range(WARM_UP_PASSES):
             nc.tensor.matmul_mx(
-                out=idle_bank[:, 0, :],
-                lhsT=w2_raw[:, 0 : P // 2].bitcast(FP4X4),
-                lhsT_scale=first_picked[:, 0:P],
+                out=unread[:, 0, :],
+                lhsT=w2_codes[:, 0 : P // 2].bitcast(FP4X4),
+                lhsT_scale=picked0[:, 0:P],
                 rhs=table[:, 0:HALF].bitcast(FP8X4),
-                rhs_scale=first_picked[:],
+                rhs_scale=picked0[:],
                 start=True,
                 stop=True,
             )
-        load_cand(0, 0, 384, "then_w1_1")
-        load_w1(1, 0, 64, "then_cand_0")
-        load_w1(1, 64, P, "then_w1_1_rest")
-        v_words = [gather_words(0, "first_half")]
-        w3_all = keep.tile([P, H], I32, name="w3_codes", align_bytes=64)
+        load_cand(0, 0, GPSIMD_FIRST, after="picked0")
+        load_w1(1, 0, M_PIECE, after="w_dealt")
+        load_w1(1, M_PIECE, P, after="tab_rows")
+        v_words = [gather_words(0)]
+        w3_codes = sbuf("w3_codes", [P, H], I32)
         nc.vector.tensor_copy(
-            w3_all[:].rearrange("p (b t m) -> p b m t", b=2, t=4),
+            w3_codes[:].rearrange("p (b t m) -> p b m t", b=2, t=4),
             w3_raw[:].rearrange("p (b m t) -> p b m t", b=2, t=4),
         )
-        w3_codes = [w3_all[:, 0:HALF], w3_all[:, HALF:]]
-        v_words.append(gather_words(1, "then_second_words"))
-        load_cand(0, 384, N, "then_cand_0_rest")
-        load_cand(1, 0, 160, "then_cand_1")
+        v_words.append(gather_words(1, after="w3_raw"))
+        load_cand(0, GPSIMD_FIRST, N, after="w2_raw")
+        load_cand(1, 0, GPSIMD_SECOND, after="table")
 
-        w1_round = [keep.tile([P, 4 * HALF], BF16, name="w1_round%d" % b, tag=tag, align_bytes=64) for b, tag in enumerate(("gpsimd_turn", "w1_round1"))]
-        cand_round = {}
-        scaled, pair, h_rounds = {}, {}, {}
+        w1_round = [sbuf("w1_round%d" % b, [P, 4 * HALF], BF16) for b in range(2)]
+        cand_round, scaled, pair, h_round, h_first = {}, {}, {}, {}, {}
         w1_mx, cand_mx, h_mx = {}, {}, {}
 
-        def quantise(name, rounded, width, slot):
-            codes = keep.tile([P, width], U32, name=name + "_codes", tag=slot or name + "_codes", align_bytes=64)
-            plane = keep.tile([P, width], U8, name=name + "_plane", align_bytes=64)
+        def quantise(name, rounded, width, after):
+            codes = sbuf(name + "_codes", [P, width], U32, after)
+            plane = sbuf(name + "_plane", [P, width], U8)
             nc.vector.quantize_mx(out=codes[:].bitcast(FP8X4), scales=plane[:], in_=rounded)
             return codes, plane
 
         for b in range(2):
-            whole = keep.tile([P, 4 * HALF], BF16, name="h_round0%d" % b, align_bytes=64)
+            h_first[b] = sbuf("h_first%d" % b, [P, 4 * HALF], BF16)
             for q in range(4):
-                h_rounds[0, b, q] = whole[:, 4 * q * P : 4 * (q + 1) * P]
-            h_rounds[0, b] = whole[:]
+                h_round[0, b, q] = h_first[b][:, 4 * q * P : 4 * (q + 1) * P]
             for q in range(2, 4):
-                h_rounds[1, b, q] = keep.tile([P, 4 * P], BF16, name="h_round1%d%d" % (b, q), align_bytes=64)[:]
-        third = keep.tile([P, 2, 2, 4 * P], BF16, name="h_round_third", align_bytes=64)
+                h_round[1, b, q] = sbuf("h_last%d%d" % (b, q), [P, 4 * P], BF16)[:]
+        h_middle = sbuf("h_middle", [P, 2, 2, 4 * P], BF16)
         for b in range(2):
             for q in range(2):
-                h_rounds[1, b, q] = third[:, b, q, :]
+                h_round[1, b, q] = h_middle[:, b, q, :]
 
-        def round_w1(engine, b, lo):
+        def round_w1(copy, b, lo):
             dst = w1_round[b][:].rearrange("p (t m j) -> p m j t", t=4, j=4)
-            engine(dst[:, lo : lo + 64], w1_raw[b, lo].rearrange("p j (m t) -> p m j t", t=4))
+            copy(dst[:, lo : lo + M_PIECE], w1_raw[b, lo].rearrange("p j (m t) -> p m j t", t=4))
 
-        def quantise_w1(b, slot):
-            w1_mx[b] = quantise("w1_%d" % b, w1_round[b][:], HALF, slot)
+        def quantise_w1(b, after=None):
+            w1_mx[b] = quantise("w1_%d" % b, w1_round[b][:], HALF, after)
 
-        def round_cand(engine, b, lo, hi):
-            cand_round[b, lo] = keep.tile([P, 4 * (hi - lo)], BF16, name="cand_round%d_%d" % (b, lo), align_bytes=64)
-            dst = cand_round[b, lo][:].rearrange("p (c e t) -> p c t e", e=4, t=4)
-            src = cand_columns(b, lo, hi).rearrange("p t (c e) -> p c t e", e=4)
-            engine(dst, src)
+        def round_cand_columns(rounded, b, lo, hi):
+            dst = rounded.rearrange("p (c e t) -> p c t e", e=4, t=4)
+            nc.scalar.copy(dst, cand_columns(b, lo, hi).rearrange("p t (c e) -> p c t e", e=4))
 
-        def round_cand_gpsimd(b, lo, cut, hi):
-            cand_round[b, lo] = keep.tile(
-                [P, 4 * (hi - lo)], BF16, name="cand_round%d_%d" % (b, lo), tag="gpsimd_turn", align_bytes=64
-            )
-            dst = cand_round[b, lo][:, 0 : 4 * (cut - lo)].rearrange("p (c t) -> p c t", t=4)
-            src = cand_columns(b, lo, cut).rearrange("p t c -> p c t")
+        def round_cand_scalar(b, lo, hi):
+            cand_round[b, lo] = sbuf("cand_round%d_%d" % (b, lo), [P, 4 * (hi - lo)], BF16)
+            round_cand_columns(cand_round[b, lo][:], b, lo, hi)
+
+        def round_cand_gpsimd(b, share, hi):
+            cand_round[b, 0] = sbuf("cand_round%d_0" % b, [P, 4 * hi], BF16, after="w1_round0")
+            dst = cand_round[b, 0][:, 0 : 4 * share].rearrange("p (c t) -> p c t", t=4)
+            src = cand_columns(b, 0, share).rearrange("p t c -> p c t")
             nc.gpsimd.tensor_scalar(dst, src, 1.0, 0.0, MULT, ADD)
 
-        def round_cand_rest(b, lo, cut, hi):
-            dst = cand_round[b, lo][:, 4 * (cut - lo) :].rearrange("p (c e t) -> p c t e", e=4, t=4)
-            nc.scalar.copy(dst, cand_columns(b, cut, hi).rearrange("p t (c e) -> p c t e", e=4))
+        def round_cand_rest(b, share, hi):
+            round_cand_columns(cand_round[b, 0][:, 4 * share :], b, share, hi)
 
-        def quantise_cand(b, lo, hi, slot):
-            codes, plane = quantise("cand%d_%d" % (b, lo), cand_round[b, lo][:], hi - lo, slot)
+        def quantise_cand(b, lo, hi, after=None):
+            codes, plane = quantise("cand%d_%d" % (b, lo), cand_round[b, lo][:], hi - lo, after)
             for c in range(lo // P, hi // P):
                 cols = slice(c * P - lo, (c + 1) * P - lo)
                 cand_mx[b, c] = codes[:, cols], plane[:, cols]
 
-        steps = [(0, 0, HALF, b, t) for b in range(2) for t in range(4)]
-        steps = steps + [(1, lo, 2 * P, b, t) for lo in (0, 2 * P) for b in range(2) for t in (0, 2)]
-
-        def projection(step, codes, plane, fmt, after=None):
-            h, lo, width, b, t0 = step
-            bank = next_bank(HALF // width, after)
-            for g in range(HALF // width):
-                t = t0 + g
-                nc.tensor.matmul_mx(
-                    out=bank[:, g, :],
-                    lhsT=codes(b, t).bitcast(fmt),
-                    lhsT_scale=plane[:, b * HALF + t * P : b * HALF + (t + 1) * P],
-                    rhs=v_words[h][:, lo : lo + width].bitcast(FP8X4),
-                    rhs_scale=v_scales[h][:, lo : lo + width],
-                    start=True,
-                    stop=True,
-                )
-            return bank
-
-        pair_bank = {}
-
-        def scale_x2(k, after=None, slot=None):
-            h, lo, width, b, t0 = steps[k]
-            bank = projection(
-                steps[k], lambda b, t: w2_all[:, (4 * b + t) * P // 2 : (4 * b + t + 1) * P // 2], w2_plane, FP4X4, after
-            )
-            scaled[k] = keep.tile([P, HALF // width, width], F32, name="scaled%d" % k, tag=slot or "scaled%d" % k, align_bytes=64)
-            for g in range(HALF // width):
-                t = t0 + g
-                nc.scalar.activation(scaled[k][:, g, :], bank[:, g, :], ACT.Copy, scale=rel_cols[:, b, t : t + 1])
-
-        def pair_product(k, slot=None):
-            h, lo, width, b, t0 = steps[k]
-            bank = projection(steps[k], lambda b, t: w3_codes[b][:, t * P : (t + 1) * P], w3_plane, FP8X4)
-            pair_bank[k] = taken[-1]
-            if (h, lo, b) not in pair:
-                name = "pair%d_%d_%d" % (h, lo, b)
-                pair[h, lo, b] = keep.tile([P, 4, width], F32, name=name, tag=slot or name, align_bytes=64)
-            nc.vector.tensor_tensor(pair[h, lo, b][:, t0 : t0 + HALF // width, :], bank[:], scaled[k][:], MULT)
-
-        x3_rows = {}
-
-        def copy_x3(k, tag, after=None):
-            h, lo, width, b, t0 = steps[k]
-            bank = projection(steps[k], lambda b, t: w3_codes[b][:, t * P : (t + 1) * P], w3_plane, FP8X4, after)
-            x3_rows[k] = keep.tile([P, HALF // width, width], F32, name="x3_%d" % k, tag=tag, align_bytes=64)
-            nc.scalar.copy(x3_rows[k][:], bank[:])
-
-        def pair_product_gpsimd(k, slot):
-            h, lo, width, b, t0 = steps[k]
-            if (h, lo, b) not in pair:
-                pair[h, lo, b] = keep.tile([P, 4, width], F32, name="pair%d_%d_%d" % (h, lo, b), tag=slot, align_bytes=64)
-            nc.gpsimd.tensor_tensor(pair[h, lo, b][:, t0 : t0 + HALF // width, :], x3_rows[k][:], scaled[k][:], MULT)
-
-        def triple_product(h, b, q):
-            cols = slice(q * P, (q + 1) * P)
-            lo = 0 if h == 0 else q // 2 * 2 * P
-            x1 = next_bank(4)
-            for t in range(4):
-                nc.tensor.matmul_mx(
-                    out=x1[:, t, :],
-                    lhsT=w1_mx[b][0][:, t * P : (t + 1) * P].bitcast(FP8X4),
-                    lhsT_scale=w1_mx[b][1][:, t * P : (t + 1) * P],
-                    rhs=v_words[h][:, cols].bitcast(FP8X4),
-                    rhs_scale=v_scales[h][:, cols],
-                    start=True,
-                    stop=True,
-                )
-            nc.vector.tensor_tensor(
-                h_rounds[h, b, q].rearrange("p (n e t) -> p n t e", e=2, t=4),
-                x1[:].rearrange("p t (n e) -> p n t e", e=2),
-                pair[h, lo, b][:, :, q * P - lo : (q + 1) * P - lo].rearrange("p t (n e) -> p n t e", e=2),
-                MULT,
-            )
-
-        def quantise_first_half(b, slot):
-            codes, plane = quantise("h0%d" % b, h_rounds[0, b], HALF, slot)
+        def quantise_h_first(b, after):
+            codes, plane = quantise("h_first%d" % b, h_first[b][:], HALF, after)
             h_mx[0, b, 0] = codes[:], plane[:]
 
-        def quantise_third(slot):
-            codes, plane = quantise("h_third", third[:].rearrange("p b q n -> p (b q n)"), HALF, slot)
+        def quantise_h_middle(after):
+            codes, plane = quantise("h_middle", h_middle[:].rearrange("p b q n -> p (b q n)"), HALF, after)
             for b in range(2):
                 cols = slice(b * 2 * P, (b + 1) * 2 * P)
                 h_mx[1, b, 0] = codes[:, cols], plane[:, cols]
 
-        def quantise_eighth(b, q):
-            codes, plane = quantise("h1%d%d" % (b, q), h_rounds[1, b, q], P, None)
+        def quantise_h_last(b, q):
+            codes, plane = quantise("h_last%d%d" % (b, q), h_round[1, b, q], P, None)
             h_mx[1, b, q * P] = codes[:], plane[:]
+
+        steps = [(0, 0, HALF, b, t) for b in range(2) for t in range(4)]
+        steps = steps + [(1, lo, 2 * P, b, t) for lo in (0, 2 * P) for b in range(2) for t in (0, 2)]
+        pair_bank, x3_rows, x1_banks = {}, {}, {}
+
+        def w2_tile(b, t):
+            return w2_codes[:, (4 * b + t) * P // 2 : (4 * b + t + 1) * P // 2].bitcast(FP4X4)
+
+        def w3_tile(b, t):
+            return w3_codes[:, (4 * b + t) * P : (4 * b + t + 1) * P].bitcast(FP8X4)
+
+        def project(k, weight_tile, plane, bank=None):
+            h, lo, width, b, t0 = steps[k]
+            sums = next_bank(HALF // width, bank)
+            for g in range(HALF // width):
+                t = t0 + g
+                nc.tensor.matmul_mx(
+                    out=sums[:, g, :],
+                    lhsT=weight_tile(b, t),
+                    lhsT_scale=plane[:, (4 * b + t) * P : (4 * b + t + 1) * P],
+                    rhs=v_words[h][:, lo : lo + width].bitcast(FP8X4),
+                    rhs_scale=v_planes[h][:, lo : lo + width],
+                    start=True,
+                    stop=True,
+                )
+            return sums
+
+        def scale_x2(k, after=None, bank=None):
+            h, lo, width, b, t0 = steps[k]
+            x2 = project(k, w2_tile, w2_plane, bank)
+            scaled[k] = sbuf("scaled%d" % k, [P, HALF // width, width], F32, after)
+            for g in range(HALF // width):
+                t = t0 + g
+                nc.scalar.activation(scaled[k][:, g, :], x2[:, g, :], ACT.Copy, scale=rel_cols[:, b, t : t + 1])
+
+        def pair_rows(k, after=None):
+            h, lo, width, b, t0 = steps[k]
+            if (h, lo, b) not in pair:
+                pair[h, lo, b] = sbuf("pair%d_%d_%d" % (h, lo, b), [P, 4, width], F32, after)
+            return pair[h, lo, b][:, t0 : t0 + HALF // width, :]
+
+        def pair_product(k):
+            x3 = project(k, w3_tile, w3_plane)
+            pair_bank[k] = banks_taken[-1]
+            nc.vector.tensor_tensor(pair_rows(k), x3[:], scaled[k][:], MULT)
+
+        def copy_x3(k, after=None, bank=None):
+            h, lo, width, b, t0 = steps[k]
+            x3 = project(k, w3_tile, w3_plane, bank)
+            x3_rows[k] = sbuf("x3_%d" % k, [P, HALF // width, width], F32, after)
+            nc.scalar.copy(x3_rows[k][:], x3[:])
+
+        def pair_product_gpsimd(k, after):
+            nc.gpsimd.tensor_tensor(pair_rows(k, after), x3_rows[k][:], scaled[k][:], MULT)
+
+        def project_x1(h, b, q):
+            cols = slice(q * P, (q + 1) * P)
+            x1_banks[h, b, q] = next_bank(4)
+            codes, plane = w1_mx[b]
+            for t in range(4):
+                nc.tensor.matmul_mx(
+                    out=x1_banks[h, b, q][:, t, :],
+                    lhsT=codes[:, t * P : (t + 1) * P].bitcast(FP8X4),
+                    lhsT_scale=plane[:, t * P : (t + 1) * P],
+                    rhs=v_words[h][:, cols].bitcast(FP8X4),
+                    rhs_scale=v_planes[h][:, cols],
+                    start=True,
+                    stop=True,
+                )
+
+        def multiply_x1(h, b, q):
+            lo = 0 if h == 0 else q // 2 * 2 * P
+            nc.vector.tensor_tensor(
+                h_round[h, b, q].rearrange("p (n e t) -> p n t e", e=2, t=4),
+                x1_banks[h, b, q][:].rearrange("p t (n e) -> p n t e", e=2),
+                pair[h, lo, b][:, :, q * P - lo : (q + 1) * P - lo].rearrange("p t (n e) -> p n t e", e=2),
+                MULT,
+            )
+
+        def triple_product(h, b, q):
+            project_x1(h, b, q)
+            multiply_x1(h, b, q)
 
         out_view = out.rearrange("(c p) j -> p c j", p=P)
 
-        def score_passes(bank, h, lo, width, c0, count, b):
+        def score_passes(sums, h, lo, c0, count, b):
             for g in range(count):
-                c = c0 + g
                 nc.tensor.matmul_mx(
-                    out=bank[:, g, :],
-                    lhsT=cand_mx[b, c][0].bitcast(FP8X4),
-                    lhsT_scale=cand_mx[b, c][1],
+                    out=sums[:, g, :],
+                    lhsT=cand_mx[b, c0 + g][0].bitcast(FP8X4),
+                    lhsT_scale=cand_mx[b, c0 + g][1],
                     rhs=h_mx[h, b, lo][0].bitcast(FP8X4),
                     rhs_scale=h_mx[h, b, lo][1],
                     start=(b == 0 and g == 0),
                     stop=(b == 1 and g == count - 1),
                 )
 
-        def add_prior(staged, bank, width, c0, count, on_vector):
-            if on_vector:
-                nc.vector.tensor_tensor(
-                    staged,
-                    bank[:, 0:count, :],
-                    prior_cols[:, c0 : c0 + count].unsqueeze(2).to_broadcast([P, count, width]),
-                    ADD,
+        def add_prior_scalar(staged, sums, c0, count):
+            for g in range(count):
+                nc.scalar.activation(
+                    staged[:, g, :], sums[:, g, :], ACT.Identity, bias=prior_cols[:, c0 + g : c0 + g + 1]
                 )
-            else:
-                for g in range(count):
-                    nc.scalar.activation(
-                        staged[:, g, :], bank[:, g, :], ACT.Identity, bias=prior_cols[:, c0 + g : c0 + g + 1]
-                    )
 
-        def store(staged, h, lo, width, c0, count):
-            nc.sync.dma_start(out_view[:, c0 : c0 + count, h * HALF + lo : h * HALF + lo + width], staged[:])
+        def add_prior_vector(staged, sums, c0, count):
+            spread = prior_cols[:, c0 : c0 + count].unsqueeze(2).to_broadcast([P, count, P])
+            nc.vector.tensor_tensor(staged, sums[:, 0:count, :], spread, ADD)
 
-        def score(h, lo, width, c0, count, per_bank):
-            staged = keep.tile([P, count, width], F32, name="staged_%d_%d_%d" % (h, lo, c0))
+        def store(staged, first, width, c0, count):
+            nc.sync.dma_start(out_view[:, c0 : c0 + count, first : first + width], staged[:])
+
+        def score(h, width, c0, count):
+            per_bank = HALF // width
+            staged = keep.tile([P, count, width], F32, name="staged_%d_%d" % (h, c0))
             for g in range(0, count, per_bank):
-                bank = next_bank(HALF // width)
+                sums = next_bank(per_bank)
                 for b in range(2):
-                    score_passes(bank, h, lo, width, c0 + g, per_bank, b)
-                add_prior(staged[:, g : g + per_bank, :], bank, width, c0 + g, per_bank, False)
-            store(staged, h, lo, width, c0, count)
+                    score_passes(sums, h, 0, c0 + g, per_bank, b)
+                add_prior_scalar(staged[:, g : g + per_bank, :], sums, c0 + g, per_bank)
+            store(staged, h * HALF, width, c0, count)
 
-        def open_scores(q):
-            banks = [next_bank(4) for c0 in (0, 3)]
-            for c0, bank in zip((0, 3), banks):
-                score_passes(bank, 1, q * P, P, c0, 3, 0)
-            return banks
+        share = TILES // 2
 
-        def close_scores(q, banks):
-            for c0, bank in zip((0, 3), banks):
-                score_passes(bank, 1, q * P, P, c0, 3, 1)
+        def last_passes(q, b, sums):
+            for half_of_tiles in range(2):
+                score_passes(sums[half_of_tiles], 1, q * P, half_of_tiles * share, share, b)
 
-        def finish_scores(q, bank, c0, on_vector):
-            staged = keep.tile([P, 3, P], F32, name="staged_end_%d_%d" % (q, c0))
-            add_prior(staged[:], bank, P, c0, 3, on_vector)
-            store(staged, 1, q * P, P, c0, 3)
+        def open_last(q):
+            sums = [next_bank(4), next_bank(4)]
+            last_passes(q, 0, sums)
+            return sums
 
-        on_scalar, on_vector = nc.scalar.copy, nc.vector.tensor_copy
+        def finish_last(q, sums, half_of_tiles):
+            c0 = half_of_tiles * share
+            staged = keep.tile([P, share, P], F32, name="staged_last_%d_%d" % (q, c0))
+            (add_prior_scalar, add_prior_vector)[half_of_tiles](staged[:], sums[half_of_tiles], c0, share)
+            store(staged, HALF + q * P, P, c0, share)
+
         for k in range(3):
             scale_x2(k)
         pair_product(0)
         scale_x2(3)
         pair_product(1)
-        round_w1(on_scalar, 0, 0)
+        round_w1(nc.scalar.copy, 0, 0)
         pair_product(2)
         pair_product(3)
         scale_x2(4)
-        round_w1(on_vector, 0, 64)
+        round_w1(nc.vector.tensor_copy, 0, M_PIECE)
         scale_x2(5)
-        load_cand(1, 160, N, "then_w1_0")
-        quantise_w1(0, None)
-        round_cand_gpsimd(0, 0, 384, HALF)
+        load_cand(1, GPSIMD_SECOND, N, after="w_rows")
+        quantise_w1(0)
+
+        round_cand_gpsimd(0, GPSIMD_FIRST, HALF)
         for q in range(4):
             scale_x2(6 + q)
             triple_product(0, 0, q)
-        round_w1(on_scalar, 1, 0)
-        round_w1(on_scalar, 1, 64)
+        round_w1(nc.scalar.copy, 1, 0)
+        round_w1(nc.scalar.copy, 1, M_PIECE)
         for k in range(4, 8):
             pair_product(k)
-        prior_cols = load_prior()
-        round_cand_rest(0, 0, 384, HALF)
-        round_cand(on_scalar, 0, HALF, N)
-        scale_x2(10, slot="then_cand_0")
-        scale_x2(11, slot="then_w1_1_rest")
-        quantise_w1(1, "scaled6")
-        quantise_first_half(0, "then_w1_1")
-        quantise_cand(0, 0, HALF, None)
-        round_cand_gpsimd(1, 0, 160, 2 * P)
-        for k, x2_slot, x3_slot in ((12, "w1_round1", "h_round00"), (13, "then_cand_0_rest", "scaled7")):
-            scale_x2(k, slot=x2_slot)
-            copy_x3(k, x3_slot)
-            pair_product_gpsimd(k, "then_cand_1")
+        prior_cols = load_prior(after="scaled5")
+        round_cand_rest(0, GPSIMD_FIRST, HALF)
+        round_cand_scalar(0, HALF, N)
+        scale_x2(10, after="w_dealt")
+        scale_x2(11, after="tab_rows")
+
+        quantise_w1(1, after="scaled6")
+        quantise_h_first(0, after="picked0")
+        quantise_cand(0, 0, HALF)
+
+        round_cand_gpsimd(1, GPSIMD_SECOND, 2 * P)
+        for k, x2_after, x3_after in ((12, "w1_round1", "h_first0"), (13, "w2_raw", "scaled7")):
+            scale_x2(k, after=x2_after)
+            copy_x3(k, after=x3_after)
+            pair_product_gpsimd(k, after="table")
         for q in range(4):
             triple_product(0, 1, q)
-        round_cand_rest(1, 0, 160, 2 * P)
-        round_cand(on_scalar, 1, 2 * P, N)
+        round_cand_rest(1, GPSIMD_SECOND, 2 * P)
+        round_cand_scalar(1, 2 * P, N)
         for k in range(8, 12):
             pair_product(k)
-        scale_x2(14, pair_bank[8])
-        quantise_first_half(1, "scaled7")
-        copy_x3(14, "x3_14", pair_bank[9])
-        quantise_cand(1, 0, 2 * P, "then_cand_0_rest")
-        scale_x2(15, pair_bank[10])
-        quantise_cand(1, 2 * P, N, "then_w1_1_rest")
-        copy_x3(15, "x3_15", pair_bank[11])
-        quantise_cand(0, HALF, N, "then_cand_0")
-        pair_product_gpsimd(14, "cand_round0_512")
-        pair_product_gpsimd(15, "cand_round0_512")
-        score(0, 0, HALF, 0, 1, 1)
-        score(0, 0, HALF, 1, 1, 1)
-        triple_product(1, 0, 0)
-        triple_product(1, 0, 1)
-        score(0, 0, HALF, 2, 2, 1)
-        triple_product(1, 1, 0)
-        triple_product(1, 1, 1)
-        score(0, 0, HALF, 4, 2, 1)
+
+        scale_x2(14, bank=pair_bank[8])
+        quantise_h_first(1, after="scaled7")
+        copy_x3(14, bank=pair_bank[9])
+        quantise_cand(1, 0, 2 * P, after="w2_raw")
+        scale_x2(15, bank=pair_bank[10])
+        quantise_cand(1, 2 * P, N, after="tab_rows")
+        copy_x3(15, bank=pair_bank[11])
+        quantise_cand(0, HALF, N, after="w_dealt")
+
+        pair_product_gpsimd(14, after="cand_round0_512")
+        pair_product_gpsimd(15, after="cand_round0_512")
+        score(0, HALF, 0, 1)
+        score(0, HALF, 1, 1)
+        for b in range(2):
+            triple_product(1, b, 0)
+            triple_product(1, b, 1)
+            score(0, HALF, 2 + 2 * b, 2)
         triple_product(1, 0, 2)
-        quantise_third("x3_15")
-        triple_product(1, 1, 2)
-        score(1, 0, 2 * P, 0, 2, 2)
-        quantise_eighth(0, 2)
-        triple_product(1, 0, 3)
-        score(1, 0, 2 * P, 2, 4, 2)
-        quantise_eighth(1, 2)
-        triple_product(1, 1, 3)
-        quantise_eighth(0, 3)
-        score(1, 2 * P, P, 0, NT, 3)
-        last = open_scores(3)
-        quantise_eighth(1, 3)
-        close_scores(3, last)
-        finish_scores(3, last[0], 0, False)
-        finish_scores(3, last[1], 3, True)
+
+        project_x1(1, 1, 2)
+        project_x1(1, 0, 3)
+        project_x1(1, 1, 3)
+        quantise_h_middle(after="x3_15")
+        multiply_x1(1, 1, 2)
+        score(1, 2 * P, 0, 2)
+        quantise_h_last(0, 2)
+        multiply_x1(1, 0, 3)
+        score(1, 2 * P, 2, 4)
+        quantise_h_last(1, 2)
+        multiply_x1(1, 1, 3)
+        quantise_h_last(0, 3)
+        sums_2 = open_last(2)
+        last_passes(2, 1, sums_2)
+        finish_last(2, sums_2, 0)
+        sums_3 = open_last(3)
+        quantise_h_last(1, 3)
+        finish_last(2, sums_2, 1)
+        last_passes(3, 1, sums_3)
+        finish_last(3, sums_3, 0)
+        finish_last(3, sums_3, 1)

@@ -22,7 +22,7 @@ HALF = 512
 BANKS = 8
 TILES = N // P
 M_PIECE = 64
-GPSIMD_FIRST, GPSIMD_SECOND = 384, 160
+GPSIMD_FIRST, GPSIMD_SECOND = 448, 160
 WARM_UP_PASSES = 3
 
 
@@ -294,9 +294,9 @@ def tile_list_hyper_relational_scoring_kernel(
         def multiply_x1(h, b, q):
             lo = 0 if h == 0 else q // 2 * 2 * P
             nc.vector.tensor_tensor(
-                h_round[h, b, q].rearrange("p (n e t) -> p n t e", e=2, t=4),
-                x1_banks[h, b, q][:].rearrange("p t (n e) -> p n t e", e=2),
-                pair[h, lo, b][:, :, q * P - lo : (q + 1) * P - lo].rearrange("p t (n e) -> p n t e", e=2),
+                h_round[h, b, q].rearrange("p (n e t) -> p n t e", e=4, t=4),
+                x1_banks[h, b, q][:].rearrange("p t (n e) -> p n t e", e=4),
+                pair[h, lo, b][:, :, q * P - lo : (q + 1) * P - lo].rearrange("p t (n e) -> p n t e", e=4),
                 MULT,
             )
 
@@ -328,8 +328,8 @@ def tile_list_hyper_relational_scoring_kernel(
             spread = prior_cols[:, c0 : c0 + count].unsqueeze(2).to_broadcast([P, count, P])
             nc.vector.tensor_tensor(staged, sums[:, 0:count, :], spread, ADD)
 
-        def store(staged, first, width, c0, count):
-            nc.sync.dma_start(out_view[:, c0 : c0 + count, first : first + width], staged[:])
+        def store(staged, first, width, c0, count, queue=nc.sync):
+            queue.dma_start(out_view[:, c0 : c0 + count, first : first + width], staged[:])
 
         def score(h, width, c0, count):
             per_bank = HALF // width
@@ -352,11 +352,11 @@ def tile_list_hyper_relational_scoring_kernel(
             last_passes(q, 0, sums)
             return sums
 
-        def finish_last(q, sums, half_of_tiles):
+        def finish_last(q, sums, half_of_tiles, queue=nc.sync):
             c0 = half_of_tiles * share
             staged = keep.tile([P, share, P], F32, name="staged_last_%d_%d" % (q, c0))
             (add_prior_scalar, add_prior_vector)[half_of_tiles](staged[:], sums[half_of_tiles], c0, share)
-            store(staged, HALF + q * P, P, c0, share)
+            store(staged, HALF + q * P, P, c0, share, queue)
 
         for k in range(3):
             scale_x2(k)
@@ -440,5 +440,5 @@ def tile_list_hyper_relational_scoring_kernel(
         quantise_h_last(1, 3)
         finish_last(2, sums_2, 1)
         last_passes(3, 1, sums_3)
-        finish_last(3, sums_3, 0)
+        finish_last(3, sums_3, 0, nc.scalar)
         finish_last(3, sums_3, 1)

@@ -54,10 +54,10 @@ def tile_list_hyper_relational_scoring_kernel(
             nc.sync.dma_start(
                 tab_rows[e:P:2, :].bitcast(I32), scale_words[e:16:2, :].unsqueeze(1).to_broadcast([8, 8, T // 4])
             )
-        w_rows = sbuf("w_rows", [P, H], U8)
+        w_rows = sbuf("w_rows", [P, HALF], U8)
         for w, scales in enumerate((w2_scales, w3_scales)):
             nc.sync.dma_start(
-                w_rows[w:32:2, :].bitcast(I32), scales[0].bitcast(I32).rearrange("(d q) c -> q d c", q=4)
+                w_rows[w:64:2, :].bitcast(I32), scales[0].bitcast(I32).rearrange("row (b c) -> (row b) c", b=2)
             )
         w2_raw = sbuf("w2_raw", [P, H // 2], I32)
         nc.sync.dma_start(w2_raw[:], w2_words[0].bitcast(I32))
@@ -71,11 +71,10 @@ def tile_list_hyper_relational_scoring_kernel(
 
         w_plane = sbuf("w_plane", [P, 2 * H], U8)
         nc.vector.memset(w_plane[:].bitcast(I32), 0)
-        nc.vector.memset(w_rows[32:64, :].bitcast(I32), 0)
         v_planes = [sbuf("v_plane%d" % h, [P, HALF], U8) for h in range(2)]
         for plane in v_planes:
             nc.vector.memset(plane[96:P, :].bitcast(I32), 0)
-        nc.scalar.copy(w_rows[64:P, :].bitcast(U32), w_plane[64:P, 0:H].bitcast(U32))
+        nc.scalar.copy(w_rows[64:P, :].bitcast(U32), w_plane[64:P, 0:HALF].bitcast(U32))
 
         def load_prior(after):
             cols = sbuf("prior_cols", [P, TILES], F32, after)
@@ -89,7 +88,7 @@ def tile_list_hyper_relational_scoring_kernel(
         def gather_scales(h, after=None):
             picked = sbuf("picked%d" % h, [P, HALF], U8, after)
             nc.vector.tensor_copy(picked[:], tab_rows[:].indirect(lists(h)))
-            nc.sync.dma_start(v_planes[h][0:112, :].bitcast(I32), picked[14:126, :].bitcast(I32))
+            nc.sync.dma_start(v_planes[h][0:100, :].bitcast(I32), picked[14:114, :].bitcast(I32))
             return picked
 
         def gather_words(h, after=None):
@@ -116,19 +115,16 @@ def tile_list_hyper_relational_scoring_kernel(
             return cand_raw[b, first][:, :, lo - first : hi - first]
 
         picked0 = gather_scales(0)
-        w_dealt = sbuf("w_dealt", [P, H], U8)
+        w_dealt = sbuf("w_dealt", [P, HALF], U8)
         nc.vector.tensor_copy(
-            w_dealt[:].rearrange("p (b t m) -> p b t m", b=2, t=4),
-            w_rows[:].rearrange("p (b m t) -> p b t m", b=2, t=4),
+            w_dealt[:].rearrange("p (t m) -> p t m", t=4), w_rows[:].rearrange("p (m t) -> p t m", t=4)
         )
-        w_plane_words = w_plane[:].bitcast(I32).rearrange("p (w c) -> p w c", w=2)
-        for q in range(4):
-            nc.sync.dma_start(w_plane_words[q:P:32], w_dealt[8 * q : 8 * q + 8, :].bitcast(I32))
-        w2_plane = w_plane[:, 0:H]
-        w3_plane = w_plane[:, H:]
+        for d in range(4):
+            nc.sync.dma_start(w_plane[32 * d : 32 * d + 4, :].bitcast(I32), w_dealt[16 * d : 16 * d + 16, :].bitcast(I32))
+        w2_plane, w3_plane = 0, 1
         load_w1(0, 0, P, after="w_rows")
         w2_codes = sbuf("w2_codes", [P, H // 2], I32)
-        nc.vector.tensor_copy(
+        nc.scalar.copy(
             w2_codes[:].bitcast(U16).rearrange("p (b t m) -> p b t m", b=2, t=4),
             w2_raw[:].bitcast(U16).rearrange("p (b m t) -> p b t m", b=2, t=4),
         )
@@ -149,10 +145,11 @@ def tile_list_hyper_relational_scoring_kernel(
         load_w1(1, M_PIECE, P, after="tab_rows")
         v_words = [gather_words(0)]
         w3_codes = sbuf("w3_codes", [P, H], I32)
-        nc.vector.tensor_copy(
-            w3_codes[:].rearrange("p (b t m) -> p b m t", b=2, t=4),
-            w3_raw[:].rearrange("p (b m t) -> p b m t", b=2, t=4),
-        )
+        for b, copy in enumerate((nc.scalar.copy, nc.vector.tensor_copy)):
+            copy(
+                w3_codes[:, b * HALF : (b + 1) * HALF].bitcast(U32).rearrange("p (t m) -> p m t", t=4),
+                w3_raw[:, b * HALF : (b + 1) * HALF].bitcast(U32).rearrange("p (m t) -> p m t", t=4),
+            )
         v_words.append(gather_words(1, after="w3_raw"))
         load_cand(0, GPSIMD_FIRST, N, after="w2_raw")
         load_cand(1, 0, GPSIMD_SECOND, after="table")
@@ -240,7 +237,7 @@ def tile_list_hyper_relational_scoring_kernel(
                 nc.tensor.matmul_mx(
                     out=sums[:, g, :],
                     lhsT=weight_tile(b, t),
-                    lhsT_scale=plane[:, (4 * b + t) * P : (4 * b + t + 1) * P],
+                    lhsT_scale=w_plane[:, (8 * b + 4 * plane + t) * P : (8 * b + 4 * plane + t + 1) * P],
                     rhs=v_words[h][:, lo : lo + width].bitcast(FP8X4),
                     rhs_scale=v_planes[h][:, lo : lo + width],
                     start=True,
@@ -343,8 +340,8 @@ def tile_list_hyper_relational_scoring_kernel(
 
         share = TILES // 2
 
-        def last_passes(q, b, sums):
-            for half_of_tiles in range(2):
+        def last_passes(q, b, sums, order=(0, 1)):
+            for half_of_tiles in order:
                 score_passes(sums[half_of_tiles], 1, q * P, half_of_tiles * share, share, b)
 
         def open_last(q):
@@ -429,7 +426,8 @@ def tile_list_hyper_relational_scoring_kernel(
         score(1, 2 * P, 0, 2)
         quantise_h_last(0, 2)
         multiply_x1(1, 0, 3)
-        score(1, 2 * P, 2, 4)
+        score(1, 2 * P, 2, 2)
+        score(1, 2 * P, 4, 2)
         quantise_h_last(1, 2)
         multiply_x1(1, 1, 3)
         quantise_h_last(0, 3)
@@ -439,6 +437,6 @@ def tile_list_hyper_relational_scoring_kernel(
         sums_3 = open_last(3)
         quantise_h_last(1, 3)
         finish_last(2, sums_2, 1)
-        last_passes(3, 1, sums_3)
-        finish_last(3, sums_3, 0, nc.scalar)
+        last_passes(3, 1, sums_3, order=(1, 0))
         finish_last(3, sums_3, 1)
+        finish_last(3, sums_3, 0, nc.scalar)

@@ -21,9 +21,11 @@ P = 128
 HALF = 512
 BANKS = 8
 TILES = N // P
+SIDE = N // 2
+GPSIMD_SHARE = 320
 M_PIECE = 64
-GPSIMD_FIRST, GPSIMD_SECOND = 448, 160
 WARM_UP_PASSES = 3
+QUADRANTS = (0, 2, 1, 3)
 
 
 def tile_list_hyper_relational_scoring_kernel(
@@ -37,64 +39,37 @@ def tile_list_hyper_relational_scoring_kernel(
         def sbuf(name, shape, dtype, after=None):
             return keep.tile(shape, dtype, name=name, tag=after or name, align_bytes=64)
 
-        banks_taken, banks_in_turn = [], []
+        banks_taken = []
 
-        def next_bank(groups, bank=None):
-            if bank is None:
-                bank = len(banks_in_turn) % BANKS
-                banks_in_turn.append(bank)
-            banks_taken.append(bank)
-            return psum.tile([P, groups, HALF // groups], F32, name="ps%d" % len(banks_taken), tag="bank%d" % bank)
+        def next_bank(groups):
+            banks_taken.append(len(banks_taken) % BANKS)
+            return psum.tile(
+                [P, groups, HALF // groups], F32, name="ps%d" % len(banks_taken), tag="bank%d" % banks_taken[-1]
+            )
+
+        tab_rows = sbuf("tab_rows", [P, T], U8)
+        w_plane = sbuf("w_plane", [P, H], U8)
+        v_plane = sbuf("v_plane", [P, S], U8)
+        for zeroed in (tab_rows, w_plane, v_plane):
+            nc.vector.memset(zeroed[:].bitcast(I32), 0)
 
         offsets = keep.tile([P, S // 16], U16, name="offsets")
         nc.sync.dma_start(offsets[:], offs)
-        tab_rows = sbuf("tab_rows", [P, T], U8)
-        scale_words = tab_scales[0].bitcast(I32)
-        for e in range(2):
-            nc.sync.dma_start(
-                tab_rows[e:P:2, :].bitcast(I32), scale_words[e:16:2, :].unsqueeze(1).to_broadcast([8, 8, T // 4])
-            )
-        w_rows = sbuf("w_rows", [P, HALF], U8)
+        w_rows = sbuf("w_rows", [P, H], U8)
         for w, scales in enumerate((w2_scales, w3_scales)):
             nc.sync.dma_start(
-                w_rows[w:64:2, :].bitcast(I32), scales[0].bitcast(I32).rearrange("row (b c) -> (row b) c", b=2)
+                w_rows[16 * w : 16 * (w + 1), :].bitcast(I32), scales[0].bitcast(I32).rearrange("(d q) c -> q d c", q=4)
             )
-        w2_raw = sbuf("w2_raw", [P, H // 2], I32)
-        nc.sync.dma_start(w2_raw[:], w2_words[0].bitcast(I32))
+        nc.sync.dma_start(tab_rows[0:P:8, :].bitcast(I32), tab_scales[0].bitcast(I32))
         table = sbuf("table", [P, T], I32)
         nc.sync.dma_start(table[:], tab_words[0].rearrange("p n t -> p (n t)").bitcast(I32))
-        w3_raw = sbuf("w3_raw", [P, H], I32)
-        nc.sync.dma_start(w3_raw[:], w3_words[0].rearrange("p n t -> p (n t)").bitcast(I32))
+        w2_raw = sbuf("w2_raw", [P, H // 2], I32)
+        nc.sync.dma_start(w2_raw[:], w2_words[0].bitcast(I32))
 
         rel_cols = sbuf("rel_cols", [P, 2, 4], F32)
         nc.gpsimd.dma_start(rel_cols[:], rel.rearrange("(b p t) -> p b t", b=2, t=4))
-
-        w_plane = sbuf("w_plane", [P, 2 * H], U8)
-        nc.vector.memset(w_plane[:].bitcast(I32), 0)
-        v_planes = [sbuf("v_plane%d" % h, [P, HALF], U8) for h in range(2)]
-        for plane in v_planes:
-            nc.vector.memset(plane[96:P, :].bitcast(I32), 0)
-        nc.scalar.copy(w_rows[64:P, :].bitcast(U32), w_plane[64:P, 0:HALF].bitcast(U32))
-
-        def load_prior(after):
-            cols = sbuf("prior_cols", [P, TILES], F32, after)
-            with nc.allow_non_contiguous_dma(reason="one prior for each partition and tile of candidates"):
-                nc.sync.dma_start(cols[:], prior.rearrange("(c p) -> p c", p=P))
-            return cols
-
-        def lists(h):
-            return offsets[:, h * (HALF // 16) : (h + 1) * (HALF // 16)]
-
-        def gather_scales(h, after=None):
-            picked = sbuf("picked%d" % h, [P, HALF], U8, after)
-            nc.vector.tensor_copy(picked[:], tab_rows[:].indirect(lists(h)))
-            nc.sync.dma_start(v_planes[h][0:100, :].bitcast(I32), picked[14:114, :].bitcast(I32))
-            return picked
-
-        def gather_words(h, after=None):
-            words = sbuf("v_words%d" % h, [P, HALF], I32, after)
-            nc.vector.tensor_copy(words[:].bitcast(U32), table[:].bitcast(U32).indirect(lists(h)))
-            return words
+        nc.vector.memset(w_rows[32:64, :].bitcast(I32), 0)
+        nc.scalar.copy(w_rows[64:P, :].bitcast(U32), w_plane[64:P, :].bitcast(U32))
 
         w1_raw, cand_raw = {}, {}
 
@@ -105,54 +80,63 @@ def tile_list_hyper_relational_scoring_kernel(
             for m in range(lo, hi, M_PIECE):
                 w1_raw[b, m] = raw[:, :, 4 * (m - lo) : 4 * (m - lo + M_PIECE)]
 
-        def load_cand(b, lo, hi, after):
-            raw = sbuf("cand_raw%d_%d" % (b, lo), [P, 4, hi - lo], F32, after)
-            nc.sync.dma_start(raw[:], cand[b * HALF : (b + 1) * HALF, lo:hi].rearrange("(p t) n -> p t n", t=4))
-            cand_raw[b, lo] = raw
+        def load_cand(b, side, after):
+            cand_raw[b, side] = sbuf("cand_raw%d_%d" % (b, side), [P, 4, SIDE], F32, after)
+            rows = cand[b * HALF : (b + 1) * HALF, side * SIDE : (side + 1) * SIDE]
+            nc.sync.dma_start(cand_raw[b, side][:], rows.rearrange("(p t) n -> p t n", t=4))
 
-        def cand_columns(b, lo, hi):
-            first = max(start for (of_pass, start) in cand_raw if of_pass == b and start <= lo)
-            return cand_raw[b, first][:, :, lo - first : hi - first]
+        def load_prior(after):
+            cols = sbuf("prior_cols", [P, TILES], F32, after)
+            with nc.allow_non_contiguous_dma(reason="one prior for each partition and tile of candidates"):
+                nc.sync.dma_start(cols[:], prior.rearrange("(c p) -> p c", p=P))
+            return cols
 
-        picked0 = gather_scales(0)
-        w_dealt = sbuf("w_dealt", [P, HALF], U8)
+        def gather_words(h, after=None):
+            words = sbuf("v_words%d" % h, [P, HALF], I32, after)
+            lists = offsets[:, h * (HALF // 16) : (h + 1) * (HALF // 16)]
+            nc.vector.tensor_copy(words[:].bitcast(U32), table[:].bitcast(U32).indirect(lists))
+            return words
+
+        w_dealt = sbuf("w_dealt", [P, H], U8)
         nc.vector.tensor_copy(
-            w_dealt[:].rearrange("p (t m) -> p t m", t=4), w_rows[:].rearrange("p (m t) -> p t m", t=4)
+            w_dealt[:].rearrange("p (b t m) -> p b t m", b=2, t=4), w_rows[:].rearrange("p (b m t) -> p b t m", b=2, t=4)
         )
-        for d in range(4):
-            nc.sync.dma_start(w_plane[32 * d : 32 * d + 4, :].bitcast(I32), w_dealt[16 * d : 16 * d + 16, :].bitcast(I32))
-        w2_plane, w3_plane = 0, 1
-        load_w1(0, 0, P, after="w_rows")
+        for d in QUADRANTS:
+            nc.sync.dma_start(w_plane[32 * d : 32 * d + 8, :].bitcast(I32), w_dealt[d:32:4, :].bitcast(I32))
+        w2_plane, w3_plane = 0, 4
+        w3_raw = sbuf("w3_raw", [P, H], I32, after="w_rows")
+        nc.sync.dma_start(w3_raw[:], w3_words[0].rearrange("p n t -> p (n t)").bitcast(I32))
+        picked = sbuf("picked", [P, S], U8)
+        nc.vector.tensor_copy(picked[:], tab_rows[:].indirect(offsets[:]))
+        for d in QUADRANTS:
+            nc.sync.dma_start(
+                v_plane[32 * d : 32 * d + 4, :].bitcast(I32), picked[32 * d : 32 * (d + 1) : 8, :].bitcast(I32)
+            )
+        load_w1(0, 0, P, after="tab_rows")
         w2_codes = sbuf("w2_codes", [P, H // 2], I32)
         nc.scalar.copy(
             w2_codes[:].bitcast(U16).rearrange("p (b t m) -> p b t m", b=2, t=4),
             w2_raw[:].bitcast(U16).rearrange("p (b m t) -> p b t m", b=2, t=4),
         )
-        gather_scales(1, after="w2_raw")
+        v_words = [gather_words(h) for h in range(2)]
         unread = next_bank(1)
         for repeat in range(WARM_UP_PASSES):
             nc.tensor.matmul_mx(
                 out=unread[:, 0, :],
-                lhsT=w2_codes[:, 0 : P // 2].bitcast(FP4X4),
-                lhsT_scale=picked0[:, 0:P],
+                lhsT=table[:, 0:P].bitcast(FP8X4),
+                lhsT_scale=picked[:, 0:P],
                 rhs=table[:, 0:HALF].bitcast(FP8X4),
-                rhs_scale=picked0[:],
+                rhs_scale=picked[:, 0:HALF],
                 start=True,
                 stop=True,
             )
-        load_cand(0, 0, GPSIMD_FIRST, after="picked0")
-        load_w1(1, 0, M_PIECE, after="w_dealt")
-        load_w1(1, M_PIECE, P, after="tab_rows")
-        v_words = [gather_words(0)]
+        load_cand(0, 0, after="table")
         w3_codes = sbuf("w3_codes", [P, H], I32)
         for b, copy in enumerate((nc.scalar.copy, nc.vector.tensor_copy)):
             copy(
                 w3_codes[:, b * HALF : (b + 1) * HALF].bitcast(U32).rearrange("p (t m) -> p m t", t=4),
                 w3_raw[:, b * HALF : (b + 1) * HALF].bitcast(U32).rearrange("p (m t) -> p m t", t=4),
             )
-        v_words.append(gather_words(1, after="w3_raw"))
-        load_cand(0, GPSIMD_FIRST, N, after="w2_raw")
-        load_cand(1, 0, GPSIMD_SECOND, after="table")
 
         w1_round = [sbuf("w1_round%d" % b, [P, 4 * HALF], BF16) for b in range(2)]
         cand_round, scaled, pair, h_round, h_first = {}, {}, {}, {}, {}
@@ -182,28 +166,23 @@ def tile_list_hyper_relational_scoring_kernel(
         def quantise_w1(b, after=None):
             w1_mx[b] = quantise("w1_%d" % b, w1_round[b][:], HALF, after)
 
-        def round_cand_columns(rounded, b, lo, hi):
-            dst = rounded.rearrange("p (c e t) -> p c t e", e=4, t=4)
-            nc.scalar.copy(dst, cand_columns(b, lo, hi).rearrange("p t (c e) -> p c t e", e=4))
+        def round_cand_scalar(b, side, lo):
+            if lo == 0:
+                cand_round[b, side] = sbuf("cand_round%d_%d" % (b, side), [P, 4 * SIDE], BF16)
+            dst = cand_round[b, side][:, 4 * lo :].rearrange("p (c e t) -> p c t e", e=4, t=4)
+            nc.scalar.copy(dst, cand_raw[b, side][:, :, lo:].rearrange("p t (c e) -> p c t e", e=4))
 
-        def round_cand_scalar(b, lo, hi):
-            cand_round[b, lo] = sbuf("cand_round%d_%d" % (b, lo), [P, 4 * (hi - lo)], BF16)
-            round_cand_columns(cand_round[b, lo][:], b, lo, hi)
-
-        def round_cand_gpsimd(b, share, hi):
-            cand_round[b, 0] = sbuf("cand_round%d_0" % b, [P, 4 * hi], BF16, after="w1_round0")
-            dst = cand_round[b, 0][:, 0 : 4 * share].rearrange("p (c t) -> p c t", t=4)
-            src = cand_columns(b, 0, share).rearrange("p t c -> p c t")
+        def round_cand_gpsimd(b, side, hi, after):
+            cand_round[b, side] = sbuf("cand_round%d_%d" % (b, side), [P, 4 * SIDE], BF16, after)
+            dst = cand_round[b, side][:, 0 : 4 * hi].rearrange("p (c t) -> p c t", t=4)
+            src = cand_raw[b, side][:, :, 0:hi].rearrange("p t c -> p c t")
             nc.gpsimd.tensor_scalar(dst, src, 1.0, 0.0, MULT, ADD)
 
-        def round_cand_rest(b, share, hi):
-            round_cand_columns(cand_round[b, 0][:, 4 * share :], b, share, hi)
-
-        def quantise_cand(b, lo, hi, after=None):
-            codes, plane = quantise("cand%d_%d" % (b, lo), cand_round[b, lo][:], hi - lo, after)
-            for c in range(lo // P, hi // P):
-                cols = slice(c * P - lo, (c + 1) * P - lo)
-                cand_mx[b, c] = codes[:, cols], plane[:, cols]
+        def quantise_cand(b, side, after=None):
+            codes, plane = quantise("cand%d_%d" % (b, side), cand_round[b, side][:], SIDE, after)
+            for g in range(SIDE // P):
+                cols = slice(g * P, (g + 1) * P)
+                cand_mx[b, side * (SIDE // P) + g] = codes[:, cols], plane[:, cols]
 
         def quantise_h_first(b, after):
             codes, plane = quantise("h_first%d" % b, h_first[b][:], HALF, after)
@@ -215,13 +194,13 @@ def tile_list_hyper_relational_scoring_kernel(
                 cols = slice(b * 2 * P, (b + 1) * 2 * P)
                 h_mx[1, b, 0] = codes[:, cols], plane[:, cols]
 
-        def quantise_h_last(b, q):
-            codes, plane = quantise("h_last%d%d" % (b, q), h_round[1, b, q], P, None)
+        def quantise_h_last(b, q, after=None):
+            codes, plane = quantise("h_last%d%d" % (b, q), h_round[1, b, q], P, after)
             h_mx[1, b, q * P] = codes[:], plane[:]
 
         steps = [(0, 0, HALF, b, t) for b in range(2) for t in range(4)]
         steps = steps + [(1, lo, 2 * P, b, t) for lo in (0, 2 * P) for b in range(2) for t in (0, 2)]
-        pair_bank, x3_rows, x1_banks = {}, {}, {}
+        x3_rows, x1_banks, x2_banks, x3_banks = {}, {}, {}, {}
 
         def w2_tile(b, t):
             return w2_codes[:, (4 * b + t) * P // 2 : (4 * b + t + 1) * P // 2].bitcast(FP4X4)
@@ -229,25 +208,33 @@ def tile_list_hyper_relational_scoring_kernel(
         def w3_tile(b, t):
             return w3_codes[:, (4 * b + t) * P : (4 * b + t + 1) * P].bitcast(FP8X4)
 
-        def project(k, weight_tile, plane, bank=None):
+        def project(k, weight_tile, plane):
             h, lo, width, b, t0 = steps[k]
-            sums = next_bank(HALF // width, bank)
+            sums = next_bank(HALF // width)
             for g in range(HALF // width):
                 t = t0 + g
                 nc.tensor.matmul_mx(
                     out=sums[:, g, :],
                     lhsT=weight_tile(b, t),
-                    lhsT_scale=w_plane[:, (8 * b + 4 * plane + t) * P : (8 * b + 4 * plane + t + 1) * P],
+                    lhsT_scale=w_plane[plane:P, (4 * b + t) * P : (4 * b + t + 1) * P],
                     rhs=v_words[h][:, lo : lo + width].bitcast(FP8X4),
-                    rhs_scale=v_planes[h][:, lo : lo + width],
+                    rhs_scale=v_plane[:, h * HALF + lo : h * HALF + lo + width],
                     start=True,
                     stop=True,
                 )
             return sums
 
-        def scale_x2(k, after=None, bank=None):
+        def project_x2(k):
+            x2_banks[k] = project(k, w2_tile, w2_plane)
+
+        def project_x3(k):
+            x3_banks[k] = project(k, w3_tile, w3_plane)
+
+        def scale_x2(k, after=None):
             h, lo, width, b, t0 = steps[k]
-            x2 = project(k, w2_tile, w2_plane, bank)
+            if k not in x2_banks:
+                project_x2(k)
+            x2 = x2_banks[k]
             scaled[k] = sbuf("scaled%d" % k, [P, HALF // width, width], F32, after)
             for g in range(HALF // width):
                 t = t0 + g
@@ -260,15 +247,16 @@ def tile_list_hyper_relational_scoring_kernel(
             return pair[h, lo, b][:, t0 : t0 + HALF // width, :]
 
         def pair_product(k):
-            x3 = project(k, w3_tile, w3_plane)
-            pair_bank[k] = banks_taken[-1]
-            nc.vector.tensor_tensor(pair_rows(k), x3[:], scaled[k][:], MULT)
+            if k not in x3_banks:
+                project_x3(k)
+            nc.vector.tensor_tensor(pair_rows(k), x3_banks[k][:], scaled[k][:], MULT)
 
-        def copy_x3(k, after=None, bank=None):
+        def copy_x3(k, after=None):
             h, lo, width, b, t0 = steps[k]
-            x3 = project(k, w3_tile, w3_plane, bank)
+            if k not in x3_banks:
+                project_x3(k)
             x3_rows[k] = sbuf("x3_%d" % k, [P, HALF // width, width], F32, after)
-            nc.scalar.copy(x3_rows[k][:], x3[:])
+            nc.scalar.copy(x3_rows[k][:], x3_banks[k][:])
 
         def pair_product_gpsimd(k, after):
             nc.gpsimd.tensor_tensor(pair_rows(k, after), x3_rows[k][:], scaled[k][:], MULT)
@@ -283,7 +271,7 @@ def tile_list_hyper_relational_scoring_kernel(
                     lhsT=codes[:, t * P : (t + 1) * P].bitcast(FP8X4),
                     lhsT_scale=plane[:, t * P : (t + 1) * P],
                     rhs=v_words[h][:, cols].bitcast(FP8X4),
-                    rhs_scale=v_planes[h][:, cols],
+                    rhs_scale=v_plane[:, h * HALF + q * P : h * HALF + (q + 1) * P],
                     start=True,
                     stop=True,
                 )
@@ -298,7 +286,8 @@ def tile_list_hyper_relational_scoring_kernel(
             )
 
         def triple_product(h, b, q):
-            project_x1(h, b, q)
+            if (h, b, q) not in x1_banks:
+                project_x1(h, b, q)
             multiply_x1(h, b, q)
 
         out_view = out.rearrange("(c p) j -> p c j", p=P)
@@ -355,83 +344,117 @@ def tile_list_hyper_relational_scoring_kernel(
             (add_prior_scalar, add_prior_vector)[half_of_tiles](staged[:], sums[half_of_tiles], c0, share)
             store(staged, HALF + q * P, P, c0, share, queue)
 
-        for k in range(3):
-            scale_x2(k)
+        scale_x2(0)
+        project_x3(0)
+        scale_x2(1)
         pair_product(0)
-        scale_x2(3)
+        load_w1(1, 0, M_PIECE, after="scaled0")
+        project_x3(1)
+        scale_x2(2)
         pair_product(1)
-        round_w1(nc.scalar.copy, 0, 0)
+        load_w1(1, M_PIECE, P, after="scaled1")
         pair_product(2)
-        pair_product(3)
-        scale_x2(4)
+        load_cand(1, 0, after="scaled2")
+        round_w1(nc.scalar.copy, 0, 0)
         round_w1(nc.vector.tensor_copy, 0, M_PIECE)
+        scale_x2(3)
+        project_x3(3)
+        scale_x2(4)
         scale_x2(5)
-        load_cand(1, GPSIMD_SECOND, N, after="w_rows")
+        project_x3(4)
         quantise_w1(0)
 
-        round_cand_gpsimd(0, GPSIMD_FIRST, HALF)
+        round_cand_gpsimd(0, 0, SIDE, after="w1_round0")
+        pair_product(3)
+        load_cand(0, 1, after="scaled3")
+        scale_x2(6)
+        scale_x2(7)
+        pair_product(4)
+        load_cand(1, 1, after="scaled4")
+        project_x1(0, 0, 0)
         for q in range(4):
-            scale_x2(6 + q)
             triple_product(0, 0, q)
         round_w1(nc.scalar.copy, 1, 0)
         round_w1(nc.scalar.copy, 1, M_PIECE)
-        for k in range(4, 8):
-            pair_product(k)
+        pair_product(5)
         prior_cols = load_prior(after="scaled5")
-        round_cand_rest(0, GPSIMD_FIRST, HALF)
-        round_cand_scalar(0, HALF, N)
-        scale_x2(10, after="w_dealt")
-        scale_x2(11, after="tab_rows")
+        pair_product(6)
+        pair_product(7)
+        scale_x2(8, after="scaled0")
+        scale_x2(9, after="scaled1")
+        project_x3(8)
+        quantise_w1(1, after="table")
+        quantise_h_first(0, after="scaled6")
+        quantise_cand(0, 0, after="scaled7")
 
-        quantise_w1(1, after="scaled6")
-        quantise_h_first(0, after="picked0")
-        quantise_cand(0, 0, HALF)
-
-        round_cand_gpsimd(1, GPSIMD_SECOND, 2 * P)
-        for k, x2_after, x3_after in ((12, "w1_round1", "h_first0"), (13, "w2_raw", "scaled7")):
-            scale_x2(k, after=x2_after)
-            copy_x3(k, after=x3_after)
-            pair_product_gpsimd(k, after="table")
+        round_cand_gpsimd(1, 0, GPSIMD_SHARE, after="w1_round0")
+        scale_x2(10, after="w1_round1")
+        scale_x2(11, after="h_first0")
+        round_cand_scalar(1, 0, GPSIMD_SHARE)
+        round_cand_scalar(0, 1, 0)
+        pair_product(8)
         for q in range(4):
             triple_product(0, 1, q)
-        round_cand_rest(1, GPSIMD_SECOND, 2 * P)
-        round_cand_scalar(1, 2 * P, N)
-        for k in range(8, 12):
-            pair_product(k)
+        project_x3(9)
+        project_x3(10)
+        scale_x2(12)
+        copy_x3(12)
+        project_x2(13)
+        project_x2(14)
+        quantise_cand(1, 0)
+        quantise_h_first(1, after=None)
+        quantise_cand(0, 1, after="scaled0")
 
-        scale_x2(14, bank=pair_bank[8])
-        quantise_h_first(1, after="scaled7")
-        copy_x3(14, bank=pair_bank[9])
-        quantise_cand(1, 0, 2 * P, after="w2_raw")
-        scale_x2(15, bank=pair_bank[10])
-        quantise_cand(1, 2 * P, N, after="tab_rows")
-        copy_x3(15, bank=pair_bank[11])
-        quantise_cand(0, HALF, N, after="w_dealt")
-
-        pair_product_gpsimd(14, after="cand_round0_512")
-        pair_product_gpsimd(15, after="cand_round0_512")
+        round_cand_gpsimd(1, 1, GPSIMD_SHARE, after="cand_round0_1")
+        round_cand_scalar(1, 1, GPSIMD_SHARE)
+        scale_x2(13)
+        pair_product(9)
         score(0, HALF, 0, 1)
+        pair_product(10)
+        project_x3(11)
+        scale_x2(14)
         score(0, HALF, 1, 1)
-        for b in range(2):
-            triple_product(1, b, 0)
-            triple_product(1, b, 1)
-            score(0, HALF, 2 + 2 * b, 2)
-        triple_product(1, 0, 2)
+        pair_product(11)
+        project_x1(1, 0, 0)
+        project_x1(1, 0, 1)
+        copy_x3(14)
+        score(0, HALF, 2, 1)
+        triple_product(1, 0, 0)
+        triple_product(1, 0, 1)
+        project_x1(1, 1, 0)
+        project_x1(1, 1, 1)
+        scale_x2(15)
+        quantise_cand(1, 1)
 
-        project_x1(1, 1, 2)
+        pair_product_gpsimd(12, after="cand_round0_1")
+        triple_product(1, 1, 0)
+        project_x3(13)
+        score(0, HALF, 3, 1)
+        triple_product(1, 1, 1)
+        pair_product(13)
+        project_x3(15)
+        score(0, HALF, 4, 1)
+        score(0, HALF, 5, 1)
+        quantise_h_middle(after="x3_12")
+
+        pair_product_gpsimd(14, after="h_middle")
+        pair_product(15)
+        project_x1(1, 0, 2)
         project_x1(1, 0, 3)
-        project_x1(1, 1, 3)
-        quantise_h_middle(after="x3_15")
-        multiply_x1(1, 1, 2)
         score(1, 2 * P, 0, 2)
-        quantise_h_last(0, 2)
-        multiply_x1(1, 0, 3)
+        multiply_x1(1, 0, 2)
+        project_x1(1, 1, 2)
         score(1, 2 * P, 2, 2)
+        multiply_x1(1, 0, 3)
+        project_x1(1, 1, 3)
         score(1, 2 * P, 4, 2)
-        quantise_h_last(1, 2)
-        multiply_x1(1, 1, 3)
+
+        multiply_x1(1, 1, 2)
+        quantise_h_last(0, 2, after="x3_14")
         quantise_h_last(0, 3)
         sums_2 = open_last(2)
+        quantise_h_last(1, 2)
+        multiply_x1(1, 1, 3)
         last_passes(2, 1, sums_2)
         finish_last(2, sums_2, 0)
         sums_3 = open_last(3)

@@ -22,7 +22,7 @@ HALF = 512
 BANKS = 8
 TILES = N // P
 SIDE = N // 2
-GPSIMD_SHARE = 320
+GPSIMD_FIRST, GPSIMD_SHARE = 576, 320
 M_PIECE = 64
 WARM_UP_PASSES = 3
 QUADRANTS = (0, 2, 1, 3)
@@ -55,11 +55,10 @@ def tile_list_hyper_relational_scoring_kernel(
 
         offsets = keep.tile([P, S // 16], U16, name="offsets")
         nc.sync.dma_start(offsets[:], offs)
-        w_rows = sbuf("w_rows", [P, H], U8)
+        w_rows = sbuf("w_rows", [P, HALF], U8)
         for w, scales in enumerate((w2_scales, w3_scales)):
-            nc.sync.dma_start(
-                w_rows[16 * w : 16 * (w + 1), :].bitcast(I32), scales[0].bitcast(I32).rearrange("(d q) c -> q d c", q=4)
-            )
+            rows = scales[0].bitcast(I32).rearrange("(d q) (b c) -> (q b) d c", q=4, b=2)
+            nc.sync.dma_start(w_rows[32 * w : 32 * (w + 1), :].bitcast(I32), rows)
         nc.sync.dma_start(tab_rows[0:P:8, :].bitcast(I32), tab_scales[0].bitcast(I32))
         table = sbuf("table", [P, T], I32)
         nc.sync.dma_start(table[:], tab_words[0].rearrange("p n t -> p (n t)").bitcast(I32))
@@ -68,8 +67,7 @@ def tile_list_hyper_relational_scoring_kernel(
 
         rel_cols = sbuf("rel_cols", [P, 2, 4], F32)
         nc.gpsimd.dma_start(rel_cols[:], rel.rearrange("(b p t) -> p b t", b=2, t=4))
-        nc.vector.memset(w_rows[32:64, :].bitcast(I32), 0)
-        nc.scalar.copy(w_rows[64:P, :].bitcast(U32), w_plane[64:P, :].bitcast(U32))
+        nc.scalar.copy(w_rows[64:P, :].bitcast(U32), w_plane[64:P, 0:HALF].bitcast(U32))
 
         w1_raw, cand_raw = {}, {}
 
@@ -80,10 +78,14 @@ def tile_list_hyper_relational_scoring_kernel(
             for m in range(lo, hi, M_PIECE):
                 w1_raw[b, m] = raw[:, :, 4 * (m - lo) : 4 * (m - lo + M_PIECE)]
 
-        def load_cand(b, side, after):
-            cand_raw[b, side] = sbuf("cand_raw%d_%d" % (b, side), [P, 4, SIDE], F32, after)
-            rows = cand[b * HALF : (b + 1) * HALF, side * SIDE : (side + 1) * SIDE]
-            nc.sync.dma_start(cand_raw[b, side][:], rows.rearrange("(p t) n -> p t n", t=4))
+        def load_cand(b, lo, hi, after):
+            raw = sbuf("cand_raw%d_%d" % (b, lo), [P, 4, hi - lo], F32, after)
+            nc.sync.dma_start(raw[:], cand[b * HALF : (b + 1) * HALF, lo:hi].rearrange("(p t) n -> p t n", t=4))
+            cand_raw[b, lo] = raw
+
+        def cand_columns(b, lo, hi):
+            first = max(start for (of_pass, start) in cand_raw if of_pass == b and start <= lo)
+            return cand_raw[b, first][:, :, lo - first : hi - first]
 
         def load_prior(after):
             cols = sbuf("prior_cols", [P, TILES], F32, after)
@@ -97,12 +99,12 @@ def tile_list_hyper_relational_scoring_kernel(
             nc.vector.tensor_copy(words[:].bitcast(U32), table[:].bitcast(U32).indirect(lists))
             return words
 
-        w_dealt = sbuf("w_dealt", [P, H], U8)
+        w_dealt = sbuf("w_dealt", [P, HALF], U8)
         nc.vector.tensor_copy(
-            w_dealt[:].rearrange("p (b t m) -> p b t m", b=2, t=4), w_rows[:].rearrange("p (b m t) -> p b t m", b=2, t=4)
+            w_dealt[:].rearrange("p (t m) -> p t m", t=4), w_rows[:].rearrange("p (m t) -> p t m", t=4)
         )
         for d in QUADRANTS:
-            nc.sync.dma_start(w_plane[32 * d : 32 * d + 8, :].bitcast(I32), w_dealt[d:32:4, :].bitcast(I32))
+            nc.sync.dma_start(w_plane[32 * d : 32 * d + 8, :].bitcast(I32), w_dealt[d:64:4, :].bitcast(I32))
         w2_plane, w3_plane = 0, 4
         w3_raw = sbuf("w3_raw", [P, H], I32, after="w_rows")
         nc.sync.dma_start(w3_raw[:], w3_words[0].rearrange("p n t -> p (n t)").bitcast(I32))
@@ -130,7 +132,7 @@ def tile_list_hyper_relational_scoring_kernel(
                 start=True,
                 stop=True,
             )
-        load_cand(0, 0, after="table")
+        load_cand(0, 0, GPSIMD_FIRST, after="table")
         w3_codes = sbuf("w3_codes", [P, H], I32)
         for b, copy in enumerate((nc.scalar.copy, nc.vector.tensor_copy)):
             copy(
@@ -166,20 +168,22 @@ def tile_list_hyper_relational_scoring_kernel(
         def quantise_w1(b, after=None):
             w1_mx[b] = quantise("w1_%d" % b, w1_round[b][:], HALF, after)
 
-        def round_cand_scalar(b, side, lo):
-            if lo == 0:
-                cand_round[b, side] = sbuf("cand_round%d_%d" % (b, side), [P, 4 * SIDE], BF16)
-            dst = cand_round[b, side][:, 4 * lo :].rearrange("p (c e t) -> p c t e", e=4, t=4)
-            nc.scalar.copy(dst, cand_raw[b, side][:, :, lo:].rearrange("p t (c e) -> p c t e", e=4))
+        def rounded_columns(b, lo, hi):
+            first = max(start for (of_pass, start) in cand_round if of_pass == b and start <= lo)
+            return cand_round[b, first][:, 4 * (lo - first) : 4 * (hi - first)]
 
-        def round_cand_gpsimd(b, side, hi, after):
-            cand_round[b, side] = sbuf("cand_round%d_%d" % (b, side), [P, 4 * SIDE], BF16, after)
-            dst = cand_round[b, side][:, 0 : 4 * hi].rearrange("p (c t) -> p c t", t=4)
-            src = cand_raw[b, side][:, :, 0:hi].rearrange("p t c -> p c t")
-            nc.gpsimd.tensor_scalar(dst, src, 1.0, 0.0, MULT, ADD)
+        def round_cand_gpsimd(b, lo, hi, end, after):
+            cand_round[b, lo] = sbuf("cand_round%d_%d" % (b, lo), [P, 4 * (end - lo)], BF16, after)
+            dst = rounded_columns(b, lo, hi).rearrange("p (c t) -> p c t", t=4)
+            nc.gpsimd.tensor_scalar(dst, cand_columns(b, lo, hi).rearrange("p t c -> p c t"), 1.0, 0.0, MULT, ADD)
+
+        def round_cand_scalar(b, lo, hi):
+            dst = rounded_columns(b, lo, hi).rearrange("p (c e t) -> p c t e", e=4, t=4)
+            nc.scalar.copy(dst, cand_columns(b, lo, hi).rearrange("p t (c e) -> p c t e", e=4))
 
         def quantise_cand(b, side, after=None):
-            codes, plane = quantise("cand%d_%d" % (b, side), cand_round[b, side][:], SIDE, after)
+            rounded = rounded_columns(b, side * SIDE, (side + 1) * SIDE)
+            codes, plane = quantise("cand%d_%d" % (b, side), rounded, SIDE, after)
             for g in range(SIDE // P):
                 cols = slice(g * P, (g + 1) * P)
                 cand_mx[b, side * (SIDE // P) + g] = codes[:, cols], plane[:, cols]
@@ -354,7 +358,7 @@ def tile_list_hyper_relational_scoring_kernel(
         pair_product(1)
         load_w1(1, M_PIECE, P, after="scaled1")
         pair_product(2)
-        load_cand(1, 0, after="scaled2")
+        load_cand(1, 0, SIDE, after="scaled2")
         round_w1(nc.scalar.copy, 0, 0)
         round_w1(nc.vector.tensor_copy, 0, M_PIECE)
         scale_x2(3)
@@ -364,14 +368,13 @@ def tile_list_hyper_relational_scoring_kernel(
         project_x3(4)
         quantise_w1(0)
 
-        round_cand_gpsimd(0, 0, SIDE, after="w1_round0")
+        round_cand_gpsimd(0, 0, GPSIMD_FIRST, N, after="w1_round0")
         pair_product(3)
-        load_cand(0, 1, after="scaled3")
+        load_cand(0, GPSIMD_FIRST, N, after="scaled3")
         scale_x2(6)
         scale_x2(7)
         pair_product(4)
-        load_cand(1, 1, after="scaled4")
-        project_x1(0, 0, 0)
+        load_cand(1, SIDE, N, after="scaled4")
         for q in range(4):
             triple_product(0, 0, q)
         round_w1(nc.scalar.copy, 1, 0)
@@ -384,76 +387,77 @@ def tile_list_hyper_relational_scoring_kernel(
         scale_x2(9, after="scaled1")
         project_x3(8)
         quantise_w1(1, after="table")
+        quantise_cand(0, 0)
         quantise_h_first(0, after="scaled6")
-        quantise_cand(0, 0, after="scaled7")
 
-        round_cand_gpsimd(1, 0, GPSIMD_SHARE, after="w1_round0")
+        round_cand_gpsimd(1, 0, GPSIMD_SHARE, SIDE, after="h_first0")
         scale_x2(10, after="w1_round1")
-        scale_x2(11, after="h_first0")
-        round_cand_scalar(1, 0, GPSIMD_SHARE)
-        round_cand_scalar(0, 1, 0)
+        scale_x2(11, after="scaled7")
+        project_x3(10)
+        project_x2(12)
+        round_cand_scalar(1, GPSIMD_SHARE, SIDE)
+        round_cand_scalar(0, GPSIMD_FIRST, N)
         pair_product(8)
         for q in range(4):
-            triple_product(0, 1, q)
-        project_x3(9)
-        project_x3(10)
+            project_x1(0, 1, q)
+            multiply_x1(0, 1, q)
+        copy_x3(10)
         scale_x2(12)
+        project_x3(9)
         copy_x3(12)
-        project_x2(13)
-        project_x2(14)
+        scale_x2(13)
+        project_x3(11)
         quantise_cand(1, 0)
         quantise_h_first(1, after=None)
         quantise_cand(0, 1, after="scaled0")
 
-        round_cand_gpsimd(1, 1, GPSIMD_SHARE, after="cand_round0_1")
-        round_cand_scalar(1, 1, GPSIMD_SHARE)
-        scale_x2(13)
+        pair_product_gpsimd(10, after="w1_round0")
+        cand_round[1, SIDE] = sbuf("cand_round1_%d" % SIDE, [P, 4 * SIDE], BF16)
+        round_cand_scalar(1, SIDE, N)
         pair_product(9)
         score(0, HALF, 0, 1)
-        pair_product(10)
-        project_x3(11)
-        scale_x2(14)
-        score(0, HALF, 1, 1)
         pair_product(11)
         project_x1(1, 0, 0)
         project_x1(1, 0, 1)
-        copy_x3(14)
-        score(0, HALF, 2, 1)
+        score(0, HALF, 1, 1)
         triple_product(1, 0, 0)
-        triple_product(1, 0, 1)
         project_x1(1, 1, 0)
+        triple_product(1, 0, 1)
         project_x1(1, 1, 1)
-        scale_x2(15)
-        quantise_cand(1, 1)
-
-        pair_product_gpsimd(12, after="cand_round0_1")
-        triple_product(1, 1, 0)
+        score(0, HALF, 2, 1)
         project_x3(13)
+        scale_x2(14)
+        copy_x3(14)
+        scale_x2(15)
+        quantise_cand(1, 1, after="x3_10")
+
+        pair_product_gpsimd(12, after="cand_round1_%d" % SIDE)
+        triple_product(1, 1, 0)
         score(0, HALF, 3, 1)
         triple_product(1, 1, 1)
-        pair_product(13)
         project_x3(15)
         score(0, HALF, 4, 1)
+        pair_product(13)
+        project_x1(1, 0, 2)
+        project_x1(1, 0, 3)
         score(0, HALF, 5, 1)
         quantise_h_middle(after="x3_12")
 
         pair_product_gpsimd(14, after="h_middle")
         pair_product(15)
-        project_x1(1, 0, 2)
-        project_x1(1, 0, 3)
+        project_x1(1, 1, 2)
         score(1, 2 * P, 0, 2)
         multiply_x1(1, 0, 2)
-        project_x1(1, 1, 2)
+        project_x1(1, 1, 3)
         score(1, 2 * P, 2, 2)
         multiply_x1(1, 0, 3)
-        project_x1(1, 1, 3)
         score(1, 2 * P, 4, 2)
 
         multiply_x1(1, 1, 2)
         quantise_h_last(0, 2, after="x3_14")
-        quantise_h_last(0, 3)
-        sums_2 = open_last(2)
         quantise_h_last(1, 2)
+        sums_2 = open_last(2)
+        quantise_h_last(0, 3)
         multiply_x1(1, 1, 3)
         last_passes(2, 1, sums_2)
         finish_last(2, sums_2, 0)

@@ -22,7 +22,7 @@ HALF = 512
 BANKS = 8
 TILES = N // P
 SIDE = N // 2
-GPSIMD_FIRST, GPSIMD_SHARE = 576, 320
+GPSIMD_FIRST = 544
 M_PIECE = 64
 WARM_UP_PASSES = 3
 QUADRANTS = (0, 2, 1, 3)
@@ -203,7 +203,8 @@ def tile_list_hyper_relational_scoring_kernel(
             h_mx[1, b, q * P] = codes[:], plane[:]
 
         steps = [(0, 0, HALF, b, t) for b in range(2) for t in range(4)]
-        steps = steps + [(1, lo, 2 * P, b, t) for lo in (0, 2 * P) for b in range(2) for t in (0, 2)]
+        steps = steps + [(1, 0, 2 * P, b, t) for b in range(2) for t in (0, 2)]
+        steps = steps + [(1, lo, P, b, 0) for lo in (2 * P, 3 * P) for b in range(2)]
         x3_rows, x1_banks, x2_banks, x3_banks = {}, {}, {}, {}
 
         def w2_tile(b, t):
@@ -212,8 +213,8 @@ def tile_list_hyper_relational_scoring_kernel(
         def w3_tile(b, t):
             return w3_codes[:, (4 * b + t) * P : (4 * b + t + 1) * P].bitcast(FP8X4)
 
-        def project(k, weight_tile, plane):
-            h, lo, width, b, t0 = steps[k]
+        def project(step, weight_tile, plane):
+            h, lo, width, b, t0 = step
             sums = next_bank(HALF // width)
             for g in range(HALF // width):
                 t = t0 + g
@@ -228,21 +229,34 @@ def tile_list_hyper_relational_scoring_kernel(
                 )
             return sums
 
-        def project_x2(k):
-            x2_banks[k] = project(k, w2_tile, w2_plane)
+        def project_x2(j):
+            x2_banks[j] = project((j // 8, 0, HALF, j // 4 % 2, j % 4), w2_tile, w2_plane)
 
         def project_x3(k):
-            x3_banks[k] = project(k, w3_tile, w3_plane)
+            x3_banks[k] = project(steps[k], w3_tile, w3_plane)
 
-        def scale_x2(k, after=None):
+        def scaled_row(j, after):
+            if j not in x2_banks:
+                project_x2(j)
+            rows = 1 if j < 8 else 4
+            first = j - j % rows
+            if j == first:
+                scaled[j] = sbuf("scaled%d" % j, [P, rows, HALF], F32, after)
+            return scaled[first][:, j - first, :], x2_banks[j][:, 0, :], rel_cols[:, j // 4 % 2, j % 4 : j % 4 + 1]
+
+        def scale_x2(j, after=None):
+            row, x2, factor = scaled_row(j, after)
+            nc.scalar.activation(row, x2, ACT.Copy, scale=factor)
+
+        def scale_x2_vector(j):
+            row, x2, factor = scaled_row(j, None)
+            nc.vector.tensor_scalar(row, x2, factor, None, MULT)
+
+        def scaled_rows(k):
             h, lo, width, b, t0 = steps[k]
-            if k not in x2_banks:
-                project_x2(k)
-            x2 = x2_banks[k]
-            scaled[k] = sbuf("scaled%d" % k, [P, HALF // width, width], F32, after)
-            for g in range(HALF // width):
-                t = t0 + g
-                nc.scalar.activation(scaled[k][:, g, :], x2[:, g, :], ACT.Copy, scale=rel_cols[:, b, t : t + 1])
+            if h == 0:
+                return scaled[4 * b + t0][:]
+            return scaled[8 + 4 * b][:, t0 : t0 + HALF // width, lo : lo + width]
 
         def pair_rows(k, after=None):
             h, lo, width, b, t0 = steps[k]
@@ -253,7 +267,7 @@ def tile_list_hyper_relational_scoring_kernel(
         def pair_product(k):
             if k not in x3_banks:
                 project_x3(k)
-            nc.vector.tensor_tensor(pair_rows(k), x3_banks[k][:], scaled[k][:], MULT)
+            nc.vector.tensor_tensor(pair_rows(k), x3_banks[k][:], scaled_rows(k), MULT)
 
         def copy_x3(k, after=None):
             h, lo, width, b, t0 = steps[k]
@@ -263,7 +277,7 @@ def tile_list_hyper_relational_scoring_kernel(
             nc.scalar.copy(x3_rows[k][:], x3_banks[k][:])
 
         def pair_product_gpsimd(k, after):
-            nc.gpsimd.tensor_tensor(pair_rows(k, after), x3_rows[k][:], scaled[k][:], MULT)
+            nc.gpsimd.tensor_tensor(pair_rows(k, after), x3_rows[k][:], scaled_rows(k), MULT)
 
         def project_x1(h, b, q):
             cols = slice(q * P, (q + 1) * P)
@@ -281,7 +295,7 @@ def tile_list_hyper_relational_scoring_kernel(
                 )
 
         def multiply_x1(h, b, q):
-            lo = 0 if h == 0 else q // 2 * 2 * P
+            lo = 0 if h == 0 or q < 2 else q * P
             nc.vector.tensor_tensor(
                 h_round[h, b, q].rearrange("p (n e t) -> p n t e", e=4, t=4),
                 x1_banks[h, b, q][:].rearrange("p t (n e) -> p n t e", e=4),
@@ -348,119 +362,115 @@ def tile_list_hyper_relational_scoring_kernel(
             (add_prior_scalar, add_prior_vector)[half_of_tiles](staged[:], sums[half_of_tiles], c0, share)
             store(staged, HALF + q * P, P, c0, share, queue)
 
-        scale_x2(0)
-        project_x3(0)
+        scale_x2_vector(0)
         scale_x2(1)
         pair_product(0)
         load_w1(1, 0, M_PIECE, after="scaled0")
-        project_x3(1)
         scale_x2(2)
         pair_product(1)
         load_w1(1, M_PIECE, P, after="scaled1")
+        scale_x2(3)
         pair_product(2)
         load_cand(1, 0, SIDE, after="scaled2")
         round_w1(nc.scalar.copy, 0, 0)
         round_w1(nc.vector.tensor_copy, 0, M_PIECE)
-        scale_x2(3)
-        project_x3(3)
+        pair_product(3)
+        load_cand(0, GPSIMD_FIRST, N, after="scaled3")
         scale_x2(4)
-        scale_x2(5)
         project_x3(4)
+        scale_x2(5)
+        project_x3(5)
         quantise_w1(0)
 
         round_cand_gpsimd(0, 0, GPSIMD_FIRST, N, after="w1_round0")
-        pair_product(3)
-        load_cand(0, GPSIMD_FIRST, N, after="scaled3")
         scale_x2(6)
         scale_x2(7)
         pair_product(4)
         load_cand(1, SIDE, N, after="scaled4")
+        pair_product(5)
+        prior_cols = load_prior(after="scaled5")
         for q in range(4):
             triple_product(0, 0, q)
         round_w1(nc.scalar.copy, 1, 0)
         round_w1(nc.scalar.copy, 1, M_PIECE)
-        pair_product(5)
-        prior_cols = load_prior(after="scaled5")
         pair_product(6)
         pair_product(7)
-        scale_x2(8, after="scaled0")
-        scale_x2(9, after="scaled1")
+        scale_x2(8, after="scaled1")
+        scale_x2(9)
         project_x3(8)
+        scale_x2(10)
+        scale_x2(11)
         quantise_w1(1, after="table")
         quantise_cand(0, 0)
         quantise_h_first(0, after="scaled6")
 
-        round_cand_gpsimd(1, 0, GPSIMD_SHARE, SIDE, after="h_first0")
-        scale_x2(10, after="w1_round1")
-        scale_x2(11, after="scaled7")
-        project_x3(10)
+        round_cand_gpsimd(1, 0, SIDE, SIDE, after="h_first0")
         project_x2(12)
-        round_cand_scalar(1, GPSIMD_SHARE, SIDE)
-        round_cand_scalar(0, GPSIMD_FIRST, N)
+        project_x2(13)
         pair_product(8)
-        for q in range(4):
-            project_x1(0, 1, q)
-            multiply_x1(0, 1, q)
-        copy_x3(10)
-        scale_x2(12)
-        project_x3(9)
-        copy_x3(12)
+        scale_x2(12, after="w1_round1")
         scale_x2(13)
+        for q in range(4):
+            triple_product(0, 1, q)
+        pair_product(9)
+        round_cand_scalar(0, GPSIMD_FIRST, N)
+        copy_x3(10)
+        scale_x2(14)
+        scale_x2(15)
         project_x3(11)
+        project_x1(1, 0, 0)
+        project_x1(1, 0, 1)
+        project_x3(13)
         quantise_cand(1, 0)
         quantise_h_first(1, after=None)
-        quantise_cand(0, 1, after="scaled0")
+        quantise_cand(0, 1, after="pair0_0_1")
 
         pair_product_gpsimd(10, after="w1_round0")
         cand_round[1, SIDE] = sbuf("cand_round1_%d" % SIDE, [P, 4 * SIDE], BF16)
         round_cand_scalar(1, SIDE, N)
-        pair_product(9)
-        score(0, HALF, 0, 1)
+        copy_x3(13)
         pair_product(11)
-        project_x1(1, 0, 0)
-        project_x1(1, 0, 1)
-        score(0, HALF, 1, 1)
+        score(0, HALF, 0, 1)
         triple_product(1, 0, 0)
         project_x1(1, 1, 0)
         triple_product(1, 0, 1)
+        score(0, HALF, 1, 1)
         project_x1(1, 1, 1)
         score(0, HALF, 2, 1)
-        project_x3(13)
-        scale_x2(14)
-        copy_x3(14)
-        scale_x2(15)
+        project_x3(12)
+        copy_x3(15)
         quantise_cand(1, 1, after="x3_10")
 
-        pair_product_gpsimd(12, after="cand_round1_%d" % SIDE)
+        pair_product_gpsimd(13, after="cand_round1_%d" % SIDE)
         triple_product(1, 1, 0)
         score(0, HALF, 3, 1)
         triple_product(1, 1, 1)
-        project_x3(15)
-        score(0, HALF, 4, 1)
-        pair_product(13)
         project_x1(1, 0, 2)
-        project_x1(1, 0, 3)
-        score(0, HALF, 5, 1)
-        quantise_h_middle(after="x3_12")
-
-        pair_product_gpsimd(14, after="h_middle")
-        pair_product(15)
+        score(0, HALF, 4, 1)
+        pair_product(12)
+        project_x3(14)
         project_x1(1, 1, 2)
-        score(1, 2 * P, 0, 2)
+        score(0, HALF, 5, 1)
+        quantise_h_middle(after="x3_13")
+
+        pair_product_gpsimd(15, after="h_middle")
+        pair_product(14)
         multiply_x1(1, 0, 2)
-        project_x1(1, 1, 3)
+        score(1, 2 * P, 0, 2)
+        project_x1(1, 0, 3)
+        multiply_x1(1, 1, 2)
         score(1, 2 * P, 2, 2)
         multiply_x1(1, 0, 3)
+        project_x1(1, 1, 3)
         score(1, 2 * P, 4, 2)
 
-        multiply_x1(1, 1, 2)
-        quantise_h_last(0, 2, after="x3_14")
+        quantise_h_last(0, 2, after="x3_15")
         quantise_h_last(1, 2)
-        sums_2 = open_last(2)
         quantise_h_last(0, 3)
-        multiply_x1(1, 1, 3)
+        sums_2 = open_last(2)
         last_passes(2, 1, sums_2)
         finish_last(2, sums_2, 0)
+        multiply_x1(1, 1, 3)
         sums_3 = open_last(3)
         quantise_h_last(1, 3)
         finish_last(2, sums_2, 1)

@@ -22,7 +22,7 @@ HALF = 512
 BANKS = 8
 TILES = N // P
 SIDE = N // 2
-GPSIMD_FIRST = 544
+GPSIMD_FIRST = 4 * P
 M_PIECE = 64
 WARM_UP_PASSES = 3
 QUADRANTS = (0, 2, 1, 3)
@@ -37,7 +37,7 @@ def tile_list_hyper_relational_scoring_kernel(
         psum = ctx.enter_context(tc.psum_pool(name="psum", bufs=1))
 
         def sbuf(name, shape, dtype, after=None):
-            return keep.tile(shape, dtype, name=name, tag=after or name, align_bytes=64)
+            return keep.tile(shape, dtype, name=name, tag=after or name, align_bytes=256)
 
         banks_taken = []
 
@@ -82,10 +82,6 @@ def tile_list_hyper_relational_scoring_kernel(
             raw = sbuf("cand_raw%d_%d" % (b, lo), [P, 4, hi - lo], F32, after)
             nc.sync.dma_start(raw[:], cand[b * HALF : (b + 1) * HALF, lo:hi].rearrange("(p t) n -> p t n", t=4))
             cand_raw[b, lo] = raw
-
-        def cand_columns(b, lo, hi):
-            first = max(start for (of_pass, start) in cand_raw if of_pass == b and start <= lo)
-            return cand_raw[b, first][:, :, lo - first : hi - first]
 
         def load_prior(after):
             cols = sbuf("prior_cols", [P, TILES], F32, after)
@@ -140,7 +136,7 @@ def tile_list_hyper_relational_scoring_kernel(
                 w3_raw[:, b * HALF : (b + 1) * HALF].bitcast(U32).rearrange("p (m t) -> p m t", t=4),
             )
 
-        w1_round = [sbuf("w1_round%d" % b, [P, 4 * HALF], BF16) for b in range(2)]
+        w1_round = {}
         cand_round, scaled, pair, h_round, h_first = {}, {}, {}, {}, {}
         w1_mx, cand_mx, h_mx = {}, {}, {}
 
@@ -161,32 +157,30 @@ def tile_list_hyper_relational_scoring_kernel(
             for q in range(2):
                 h_round[1, b, q] = h_middle[:, b, q, :]
 
-        def round_w1(copy, b, lo):
+        def round_w1(copy, b, lo, after=None):
+            if lo == 0:
+                w1_round[b] = sbuf("w1_round%d" % b, [P, 4 * HALF], BF16, after)
             dst = w1_round[b][:].rearrange("p (t m j) -> p m j t", t=4, j=4)
             copy(dst[:, lo : lo + M_PIECE], w1_raw[b, lo].rearrange("p j (m t) -> p m j t", t=4))
 
         def quantise_w1(b, after=None):
             w1_mx[b] = quantise("w1_%d" % b, w1_round[b][:], HALF, after)
 
-        def rounded_columns(b, lo, hi):
-            first = max(start for (of_pass, start) in cand_round if of_pass == b and start <= lo)
-            return cand_round[b, first][:, 4 * (lo - first) : 4 * (hi - first)]
+        def round_cand_gpsimd(b, lo, hi, after):
+            cand_round[b, lo] = sbuf("cand_round%d_%d" % (b, lo), [P, 4 * (hi - lo)], BF16, after)
+            dst = cand_round[b, lo][:].rearrange("p (c t) -> p c t", t=4)
+            nc.gpsimd.tensor_scalar(dst, cand_raw[b, lo][:].rearrange("p t c -> p c t"), 1.0, 0.0, MULT, ADD)
 
-        def round_cand_gpsimd(b, lo, hi, end, after):
-            cand_round[b, lo] = sbuf("cand_round%d_%d" % (b, lo), [P, 4 * (end - lo)], BF16, after)
-            dst = rounded_columns(b, lo, hi).rearrange("p (c t) -> p c t", t=4)
-            nc.gpsimd.tensor_scalar(dst, cand_columns(b, lo, hi).rearrange("p t c -> p c t"), 1.0, 0.0, MULT, ADD)
+        def round_cand_scalar(b, lo, hi, after):
+            cand_round[b, lo] = sbuf("cand_round%d_%d" % (b, lo), [P, 4 * (hi - lo)], BF16, after)
+            dst = cand_round[b, lo][:].rearrange("p (c e t) -> p c t e", e=4, t=4)
+            nc.scalar.copy(dst, cand_raw[b, lo][:].rearrange("p t (c e) -> p c t e", e=4))
 
-        def round_cand_scalar(b, lo, hi):
-            dst = rounded_columns(b, lo, hi).rearrange("p (c e t) -> p c t e", e=4, t=4)
-            nc.scalar.copy(dst, cand_columns(b, lo, hi).rearrange("p t (c e) -> p c t e", e=4))
-
-        def quantise_cand(b, side, after=None):
-            rounded = rounded_columns(b, side * SIDE, (side + 1) * SIDE)
-            codes, plane = quantise("cand%d_%d" % (b, side), rounded, SIDE, after)
-            for g in range(SIDE // P):
-                cols = slice(g * P, (g + 1) * P)
-                cand_mx[b, side * (SIDE // P) + g] = codes[:, cols], plane[:, cols]
+        def quantise_cand(b, lo, hi, after=None):
+            codes, plane = quantise("cand%d_%d" % (b, lo), cand_round[b, lo][:], hi - lo, after)
+            for c in range(lo // P, hi // P):
+                cols = slice(c * P - lo, (c + 1) * P - lo)
+                cand_mx[b, c] = codes[:, cols], plane[:, cols]
 
         def quantise_h_first(b, after):
             codes, plane = quantise("h_first%d" % b, h_first[b][:], HALF, after)
@@ -368,52 +362,52 @@ def tile_list_hyper_relational_scoring_kernel(
         load_w1(1, 0, M_PIECE, after="scaled0")
         scale_x2(2)
         pair_product(1)
-        load_w1(1, M_PIECE, P, after="scaled1")
         scale_x2(3)
         pair_product(2)
-        load_cand(1, 0, SIDE, after="scaled2")
-        round_w1(nc.scalar.copy, 0, 0)
+        load_w1(1, M_PIECE, P, after="scaled2")
+        round_w1(nc.scalar.copy, 0, 0, after="scaled1")
         round_w1(nc.vector.tensor_copy, 0, M_PIECE)
         pair_product(3)
-        load_cand(0, GPSIMD_FIRST, N, after="scaled3")
+        load_cand(1, 0, SIDE, after="scaled3")
         scale_x2(4)
         project_x3(4)
         scale_x2(5)
         project_x3(5)
         quantise_w1(0)
 
-        round_cand_gpsimd(0, 0, GPSIMD_FIRST, N, after="w1_round0")
+        round_cand_gpsimd(0, 0, GPSIMD_FIRST, after="scaled1")
         scale_x2(6)
         scale_x2(7)
         pair_product(4)
-        load_cand(1, SIDE, N, after="scaled4")
+        load_cand(0, GPSIMD_FIRST, N, after="scaled4")
         pair_product(5)
-        prior_cols = load_prior(after="scaled5")
         for q in range(4):
             triple_product(0, 0, q)
-        round_w1(nc.scalar.copy, 1, 0)
+        round_w1(nc.scalar.copy, 1, 0, after="scaled5")
         round_w1(nc.scalar.copy, 1, M_PIECE)
+        prior_cols = load_prior(after="pair0_0_0")
         pair_product(6)
+        load_cand(1, SIDE, N, after="scaled6")
         pair_product(7)
-        scale_x2(8, after="scaled1")
+        scale_x2(8, after="scaled2")
         scale_x2(9)
         project_x3(8)
         scale_x2(10)
         scale_x2(11)
         quantise_w1(1, after="table")
-        quantise_cand(0, 0)
-        quantise_h_first(0, after="scaled6")
+        quantise_cand(0, 0, GPSIMD_FIRST)
+        quantise_h_first(0, after="scaled7")
 
-        round_cand_gpsimd(1, 0, SIDE, SIDE, after="h_first0")
+        round_cand_gpsimd(1, 0, SIDE, after="h_first0")
         project_x2(12)
         project_x2(13)
         pair_product(8)
-        scale_x2(12, after="w1_round1")
+        scale_x2(12, after="scaled5")
         scale_x2(13)
         for q in range(4):
             triple_product(0, 1, q)
         pair_product(9)
-        round_cand_scalar(0, GPSIMD_FIRST, N)
+        round_cand_scalar(0, GPSIMD_FIRST, N, after="scaled1")
         copy_x3(10)
         scale_x2(14)
         scale_x2(15)
@@ -421,13 +415,12 @@ def tile_list_hyper_relational_scoring_kernel(
         project_x1(1, 0, 0)
         project_x1(1, 0, 1)
         project_x3(13)
-        quantise_cand(1, 0)
+        quantise_cand(1, 0, SIDE)
         quantise_h_first(1, after=None)
-        quantise_cand(0, 1, after="pair0_0_1")
+        quantise_cand(0, GPSIMD_FIRST, N, after="pair0_0_1")
 
-        pair_product_gpsimd(10, after="w1_round0")
-        cand_round[1, SIDE] = sbuf("cand_round1_%d" % SIDE, [P, 4 * SIDE], BF16)
-        round_cand_scalar(1, SIDE, N)
+        pair_product_gpsimd(10, after="scaled1")
+        round_cand_scalar(1, SIDE, N, after="h_first0")
         copy_x3(13)
         pair_product(11)
         score(0, HALF, 0, 1)
@@ -439,9 +432,9 @@ def tile_list_hyper_relational_scoring_kernel(
         score(0, HALF, 2, 1)
         project_x3(12)
         copy_x3(15)
-        quantise_cand(1, 1, after="x3_10")
+        quantise_cand(1, SIDE, N, after="x3_10")
 
-        pair_product_gpsimd(13, after="cand_round1_%d" % SIDE)
+        pair_product_gpsimd(13, after="h_first0")
         triple_product(1, 1, 0)
         score(0, HALF, 3, 1)
         triple_product(1, 1, 1)
@@ -465,7 +458,7 @@ def tile_list_hyper_relational_scoring_kernel(
         score(1, 2 * P, 4, 2)
 
         quantise_h_last(0, 2, after="x3_15")
-        quantise_h_last(1, 2)
+        quantise_h_last(1, 2, after="scaled5")
         quantise_h_last(0, 3)
         sums_2 = open_last(2)
         last_passes(2, 1, sums_2)

@@ -23,6 +23,7 @@ BANKS = 8
 TILES = N // P
 SIDE = N // 2
 GPSIMD_FIRST = 4 * P
+GPSIMD_SECOND, GPSIMD_THIRD = 336, 80
 M_PIECE = 64
 WARM_UP_PASSES = 3
 QUADRANTS = (0, 2, 1, 3)
@@ -166,15 +167,17 @@ def tile_list_hyper_relational_scoring_kernel(
         def quantise_w1(b, after=None):
             w1_mx[b] = quantise("w1_%d" % b, w1_round[b][:], HALF, after)
 
-        def round_cand_gpsimd(b, lo, hi, after):
+        def open_rounded(b, lo, hi, after):
             cand_round[b, lo] = sbuf("cand_round%d_%d" % (b, lo), [P, 4 * (hi - lo)], BF16, after)
-            dst = cand_round[b, lo][:].rearrange("p (c t) -> p c t", t=4)
-            nc.gpsimd.tensor_scalar(dst, cand_raw[b, lo][:].rearrange("p t c -> p c t"), 1.0, 0.0, MULT, ADD)
 
-        def round_cand_scalar(b, lo, hi, after):
-            cand_round[b, lo] = sbuf("cand_round%d_%d" % (b, lo), [P, 4 * (hi - lo)], BF16, after)
-            dst = cand_round[b, lo][:].rearrange("p (c e t) -> p c t e", e=4, t=4)
-            nc.scalar.copy(dst, cand_raw[b, lo][:].rearrange("p t (c e) -> p c t e", e=4))
+        def round_cand_gpsimd(b, lo, share):
+            dst = cand_round[b, lo][:, 0 : 4 * share].rearrange("p (c t) -> p c t", t=4)
+            src = cand_raw[b, lo][:, :, 0:share].rearrange("p t c -> p c t")
+            nc.gpsimd.tensor_scalar(dst, src, 1.0, 0.0, MULT, ADD)
+
+        def round_cand_scalar(b, lo, skip):
+            dst = cand_round[b, lo][:, 4 * skip :].rearrange("p (c e t) -> p c t e", e=4, t=4)
+            nc.scalar.copy(dst, cand_raw[b, lo][:, :, skip:].rearrange("p t (c e) -> p c t e", e=4))
 
         def quantise_cand(b, lo, hi, after=None):
             codes, plane = quantise("cand%d_%d" % (b, lo), cand_round[b, lo][:], hi - lo, after)
@@ -375,7 +378,8 @@ def tile_list_hyper_relational_scoring_kernel(
         project_x3(5)
         quantise_w1(0)
 
-        round_cand_gpsimd(0, 0, GPSIMD_FIRST, after="scaled1")
+        open_rounded(0, 0, GPSIMD_FIRST, after="scaled1")
+        round_cand_gpsimd(0, 0, GPSIMD_FIRST)
         scale_x2(6)
         scale_x2(7)
         pair_product(4)
@@ -398,35 +402,41 @@ def tile_list_hyper_relational_scoring_kernel(
         quantise_cand(0, 0, GPSIMD_FIRST)
         quantise_h_first(0, after="scaled7")
 
-        round_cand_gpsimd(1, 0, SIDE, after="h_first0")
+        open_rounded(1, 0, SIDE, after="scaled1")
+        round_cand_gpsimd(1, 0, GPSIMD_SECOND)
         project_x2(12)
         project_x2(13)
         pair_product(8)
+        round_cand_scalar(1, 0, GPSIMD_SECOND)
         scale_x2(12, after="scaled5")
         scale_x2(13)
         for q in range(4):
             triple_product(0, 1, q)
-        pair_product(9)
-        round_cand_scalar(0, GPSIMD_FIRST, N, after="scaled1")
+        open_rounded(0, GPSIMD_FIRST, N, after="h_first0")
+        round_cand_scalar(0, GPSIMD_FIRST, 0)
         copy_x3(10)
+        project_x3(9)
         scale_x2(14)
         scale_x2(15)
-        project_x3(11)
         project_x1(1, 0, 0)
         project_x1(1, 0, 1)
+        project_x3(11)
         project_x3(13)
         quantise_cand(1, 0, SIDE)
         quantise_h_first(1, after=None)
         quantise_cand(0, GPSIMD_FIRST, N, after="pair0_0_1")
 
-        pair_product_gpsimd(10, after="scaled1")
-        round_cand_scalar(1, SIDE, N, after="h_first0")
+        open_rounded(1, SIDE, N, after="h_first1")
+        round_cand_gpsimd(1, SIDE, GPSIMD_THIRD)
+        pair_product_gpsimd(10, after="h_first0")
+        round_cand_scalar(1, SIDE, GPSIMD_THIRD)
+        pair_product(9)
         copy_x3(13)
-        pair_product(11)
         score(0, HALF, 0, 1)
         triple_product(1, 0, 0)
         project_x1(1, 1, 0)
         triple_product(1, 0, 1)
+        pair_product(11)
         score(0, HALF, 1, 1)
         project_x1(1, 1, 1)
         score(0, HALF, 2, 1)
@@ -434,7 +444,7 @@ def tile_list_hyper_relational_scoring_kernel(
         copy_x3(15)
         quantise_cand(1, SIDE, N, after="x3_10")
 
-        pair_product_gpsimd(13, after="h_first0")
+        pair_product_gpsimd(13, after="h_first1")
         triple_product(1, 1, 0)
         score(0, HALF, 3, 1)
         triple_product(1, 1, 1)

@@ -26,6 +26,7 @@ GPSIMD_FIRST = 4 * P
 GPSIMD_SECOND, GPSIMD_THIRD = 336, 80
 M_PIECE = 64
 WARM_UP_PASSES = 3
+STATIONARY_SHIFT = 32
 QUADRANTS = (0, 2, 1, 3)
 
 
@@ -51,12 +52,12 @@ def tile_list_hyper_relational_scoring_kernel(
         tab_rows = sbuf("tab_rows", [P, T], U8)
         w_plane = sbuf("w_plane", [P, H], U8)
         v_plane = sbuf("v_plane", [P, S], U8)
-        for zeroed in (tab_rows, w_plane, v_plane):
-            nc.vector.memset(zeroed[:].bitcast(I32), 0)
+        w_rows = sbuf("w_rows", [P, HALF], U8)
+        for zeroed in (tab_rows[:], w_rows[64:P, :], w_plane[:, 0:HALF], v_plane[:]):
+            nc.vector.memset(zeroed.bitcast(I32), 0)
 
         offsets = keep.tile([P, S // 16], U16, name="offsets")
         nc.sync.dma_start(offsets[:], offs)
-        w_rows = sbuf("w_rows", [P, HALF], U8)
         for w, scales in enumerate((w2_scales, w3_scales)):
             rows = scales[0].bitcast(I32).rearrange("(d q) (b c) -> (q b) d c", q=4, b=2)
             nc.sync.dma_start(w_rows[32 * w : 32 * (w + 1), :].bitcast(I32), rows)
@@ -68,7 +69,7 @@ def tile_list_hyper_relational_scoring_kernel(
 
         rel_cols = sbuf("rel_cols", [P, 2, 4], F32)
         nc.gpsimd.dma_start(rel_cols[:], rel.rearrange("(b p t) -> p b t", b=2, t=4))
-        nc.scalar.copy(w_rows[64:P, :].bitcast(U32), w_plane[64:P, 0:HALF].bitcast(U32))
+        nc.scalar.copy(w_plane[:, HALF:H].bitcast(U32), w_plane[:, 0:HALF].bitcast(U32))
 
         w1_raw, cand_raw = {}, {}
 
@@ -112,7 +113,7 @@ def tile_list_hyper_relational_scoring_kernel(
                 v_plane[32 * d : 32 * d + 4, :].bitcast(I32), picked[32 * d : 32 * (d + 1) : 8, :].bitcast(I32)
             )
         load_w1(0, 0, P, after="tab_rows")
-        w2_codes = sbuf("w2_codes", [P, H // 2], I32)
+        w2_codes = sbuf("w2_codes", [P, STATIONARY_SHIFT + H // 2], I32)[:, STATIONARY_SHIFT:]
         nc.scalar.copy(
             w2_codes[:].bitcast(U16).rearrange("p (b t m) -> p b t m", b=2, t=4),
             w2_raw[:].bitcast(U16).rearrange("p (b m t) -> p b t m", b=2, t=4),
@@ -130,7 +131,7 @@ def tile_list_hyper_relational_scoring_kernel(
                 stop=True,
             )
         load_cand(0, 0, GPSIMD_FIRST, after="table")
-        w3_codes = sbuf("w3_codes", [P, H], I32)
+        w3_codes = sbuf("w3_codes", [P, STATIONARY_SHIFT + H], I32)[:, STATIONARY_SHIFT:]
         for b, copy in enumerate((nc.scalar.copy, nc.vector.tensor_copy)):
             copy(
                 w3_codes[:, b * HALF : (b + 1) * HALF].bitcast(U32).rearrange("p (t m) -> p m t", t=4),
@@ -141,10 +142,10 @@ def tile_list_hyper_relational_scoring_kernel(
         cand_round, scaled, pair, h_round, h_first = {}, {}, {}, {}, {}
         w1_mx, cand_mx, h_mx = {}, {}, {}
 
-        def quantise(name, rounded, width, after):
-            codes = sbuf(name + "_codes", [P, width], U32, after)
+        def quantise(name, rounded, width, after, shift=0):
+            codes = sbuf(name + "_codes", [P, shift + width], U32, after)[:, shift:]
             plane = sbuf(name + "_plane", [P, width], U8)
-            nc.vector.quantize_mx(out=codes[:].bitcast(FP8X4), scales=plane[:], in_=rounded)
+            nc.vector.quantize_mx(out=codes.bitcast(FP8X4), scales=plane[:], in_=rounded)
             return codes, plane
 
         for b in range(2):
@@ -165,7 +166,7 @@ def tile_list_hyper_relational_scoring_kernel(
             copy(dst[:, lo : lo + M_PIECE], w1_raw[b, lo].rearrange("p j (m t) -> p m j t", t=4))
 
         def quantise_w1(b, after=None):
-            w1_mx[b] = quantise("w1_%d" % b, w1_round[b][:], HALF, after)
+            w1_mx[b] = quantise("w1_%d" % b, w1_round[b][:], HALF, after, STATIONARY_SHIFT)
 
         def open_rounded(b, lo, hi, after):
             cand_round[b, lo] = sbuf("cand_round%d_%d" % (b, lo), [P, 4 * (hi - lo)], BF16, after)
@@ -180,7 +181,7 @@ def tile_list_hyper_relational_scoring_kernel(
             nc.scalar.copy(dst, cand_raw[b, lo][:, :, skip:].rearrange("p t (c e) -> p c t e", e=4))
 
         def quantise_cand(b, lo, hi, after=None):
-            codes, plane = quantise("cand%d_%d" % (b, lo), cand_round[b, lo][:], hi - lo, after)
+            codes, plane = quantise("cand%d_%d" % (b, lo), cand_round[b, lo][:], hi - lo, after, STATIONARY_SHIFT)
             for c in range(lo // P, hi // P):
                 cols = slice(c * P - lo, (c + 1) * P - lo)
                 cand_mx[b, c] = codes[:, cols], plane[:, cols]

@@ -26,7 +26,6 @@ GPSIMD_FIRST = 4 * P
 GPSIMD_SECOND, GPSIMD_THIRD = 336, 80
 M_PIECE = 64
 WARM_UP_PASSES = 3
-STATIONARY_SHIFT = 32
 QUADRANTS = (0, 2, 1, 3)
 
 
@@ -113,7 +112,7 @@ def tile_list_hyper_relational_scoring_kernel(
                 v_plane[32 * d : 32 * d + 4, :].bitcast(I32), picked[32 * d : 32 * (d + 1) : 8, :].bitcast(I32)
             )
         load_w1(0, 0, P, after="tab_rows")
-        w2_codes = sbuf("w2_codes", [P, STATIONARY_SHIFT + H // 2], I32)[:, STATIONARY_SHIFT:]
+        w2_codes = sbuf("w2_codes", [P, H // 2], I32)
         nc.scalar.copy(
             w2_codes[:].bitcast(U16).rearrange("p (b t m) -> p b t m", b=2, t=4),
             w2_raw[:].bitcast(U16).rearrange("p (b m t) -> p b t m", b=2, t=4),
@@ -131,7 +130,7 @@ def tile_list_hyper_relational_scoring_kernel(
                 stop=True,
             )
         load_cand(0, 0, GPSIMD_FIRST, after="table")
-        w3_codes = sbuf("w3_codes", [P, STATIONARY_SHIFT + H], I32)[:, STATIONARY_SHIFT:]
+        w3_codes = sbuf("w3_codes", [P, H], I32)
         for b, copy in enumerate((nc.scalar.copy, nc.vector.tensor_copy)):
             copy(
                 w3_codes[:, b * HALF : (b + 1) * HALF].bitcast(U32).rearrange("p (t m) -> p m t", t=4),
@@ -142,10 +141,10 @@ def tile_list_hyper_relational_scoring_kernel(
         cand_round, scaled, pair, h_round, h_first = {}, {}, {}, {}, {}
         w1_mx, cand_mx, h_mx = {}, {}, {}
 
-        def quantise(name, rounded, width, after, shift=0):
-            codes = sbuf(name + "_codes", [P, shift + width], U32, after)[:, shift:]
+        def quantise(name, rounded, width, after):
+            codes = sbuf(name + "_codes", [P, width], U32, after)
             plane = sbuf(name + "_plane", [P, width], U8)
-            nc.vector.quantize_mx(out=codes.bitcast(FP8X4), scales=plane[:], in_=rounded)
+            nc.vector.quantize_mx(out=codes[:].bitcast(FP8X4), scales=plane[:], in_=rounded)
             return codes, plane
 
         for b in range(2):
@@ -166,7 +165,7 @@ def tile_list_hyper_relational_scoring_kernel(
             copy(dst[:, lo : lo + M_PIECE], w1_raw[b, lo].rearrange("p j (m t) -> p m j t", t=4))
 
         def quantise_w1(b, after=None):
-            w1_mx[b] = quantise("w1_%d" % b, w1_round[b][:], HALF, after, STATIONARY_SHIFT)
+            w1_mx[b] = quantise("w1_%d" % b, w1_round[b][:], HALF, after)
 
         def open_rounded(b, lo, hi, after):
             cand_round[b, lo] = sbuf("cand_round%d_%d" % (b, lo), [P, 4 * (hi - lo)], BF16, after)
@@ -177,11 +176,11 @@ def tile_list_hyper_relational_scoring_kernel(
             nc.gpsimd.tensor_scalar(dst, src, 1.0, 0.0, MULT, ADD)
 
         def round_cand_scalar(b, lo, skip):
-            dst = cand_round[b, lo][:, 4 * skip :].rearrange("p (c e t) -> p c t e", e=4, t=4)
-            nc.scalar.copy(dst, cand_raw[b, lo][:, :, skip:].rearrange("p t (c e) -> p c t e", e=4))
+            dst = cand_round[b, lo][:, 4 * skip :].rearrange("p (c e t) -> p c t e", e=2, t=4)
+            nc.scalar.copy(dst, cand_raw[b, lo][:, :, skip:].rearrange("p t (c e) -> p c t e", e=2))
 
         def quantise_cand(b, lo, hi, after=None):
-            codes, plane = quantise("cand%d_%d" % (b, lo), cand_round[b, lo][:], hi - lo, after, STATIONARY_SHIFT)
+            codes, plane = quantise("cand%d_%d" % (b, lo), cand_round[b, lo][:], hi - lo, after)
             for c in range(lo // P, hi // P):
                 cols = slice(c * P - lo, (c + 1) * P - lo)
                 cand_mx[b, c] = codes[:, cols], plane[:, cols]
@@ -295,9 +294,9 @@ def tile_list_hyper_relational_scoring_kernel(
         def multiply_x1(h, b, q):
             lo = 0 if h == 0 or q < 2 else q * P
             nc.vector.tensor_tensor(
-                h_round[h, b, q].rearrange("p (n e t) -> p n t e", e=4, t=4),
-                x1_banks[h, b, q][:].rearrange("p t (n e) -> p n t e", e=4),
-                pair[h, lo, b][:, :, q * P - lo : (q + 1) * P - lo].rearrange("p t (n e) -> p n t e", e=4),
+                h_round[h, b, q].rearrange("p (n e t) -> p n t e", e=2, t=4),
+                x1_banks[h, b, q][:].rearrange("p t (n e) -> p n t e", e=2),
+                pair[h, lo, b][:, :, q * P - lo : (q + 1) * P - lo].rearrange("p t (n e) -> p n t e", e=2),
                 MULT,
             )
 

from contextlib import ExitStack

import concourse.mybir as mybir

K, T, S, H, N = 512, 2048, 1024, 1024, 768
FLOPS = 2 * K * H * S * 3 + 2 * H * N * S

F32 = mybir.dt.float32
BF16 = mybir.dt.bfloat16
I32 = mybir.dt.int32
U32 = mybir.dt.uint32
U16 = mybir.dt.uint16
U8 = mybir.dt.uint8
FP8X4 = mybir.dt.float8_e4m3fn_x4
FP4X4 = mybir.dt.float4_e2m1fn_x4
MULT = mybir.AluOpType.mult
ADD = mybir.AluOpType.add
ACT = mybir.ActivationFunctionType

P = 128
HALF = 512
BANKS = 8
TILES = N // P
SIDE = N // 2
GPSIMD_FIRST = 4 * P
GPSIMD_SECOND, GPSIMD_THIRD = 336, 80
M_PIECE = 64
WARM_UP_PASSES = 3
QUADRANTS = (0, 2, 1, 3)


def tile_list_hyper_relational_scoring_kernel(
    tc, tab_words, tab_scales, offs, w1, w2_words, w2_scales, w3_words, w3_scales, rel, cand, prior, out
):
    nc = tc.nc
    with ExitStack() as ctx:
        keep = ctx.enter_context(tc.tile_pool(name="keep", bufs=1))
        psum = ctx.enter_context(tc.psum_pool(name="psum", bufs=1))

        def sbuf(name, shape, dtype, after=None):
            return keep.tile(shape, dtype, name=name, tag=after or name, align_bytes=256)

        banks_taken = []

        def next_bank(groups):
            banks_taken.append(len(banks_taken) % BANKS)
            return psum.tile(
                [P, groups, HALF // groups], F32, name="ps%d" % len(banks_taken), tag="bank%d" % banks_taken[-1]
            )

        tab_rows = sbuf("tab_rows", [P, T], U8)
        w_plane = sbuf("w_plane", [P, H], U8)
        v_plane = sbuf("v_plane", [P, S], U8)
        w_rows = sbuf("w_rows", [P, HALF], U8)
        for zeroed in (tab_rows[:], w_rows[64:P, :], w_plane[:, 0:HALF], v_plane[:]):
            nc.vector.memset(zeroed.bitcast(I32), 0)

        offsets = keep.tile([P, S // 16], U16, name="offsets")
        nc.sync.dma_start(offsets[:], offs)
        for w, scales in enumerate((w2_scales, w3_scales)):
            rows = scales[0].bitcast(I32).rearrange("(d q) (b c) -> (q b) d c", q=4, b=2)
            nc.sync.dma_start(w_rows[32 * w : 32 * (w + 1), :].bitcast(I32), rows)
        nc.sync.dma_start(tab_rows[0:P:8, :].bitcast(I32), tab_scales[0].bitcast(I32))
        table = sbuf("table", [P, T], I32)
        nc.sync.dma_start(table[:], tab_words[0].rearrange("p n t -> p (n t)").bitcast(I32))
        w2_raw = sbuf("w2_raw", [P, H // 2], I32)
        nc.sync.dma_start(w2_raw[:], w2_words[0].bitcast(I32))

        rel_cols = sbuf("rel_cols", [P, 2, 4], F32)
        nc.gpsimd.dma_start(rel_cols[:], rel.rearrange("(b p t) -> p b t", b=2, t=4))
        nc.scalar.copy(w_plane[:, HALF:H].bitcast(U32), w_plane[:, 0:HALF].bitcast(U32))

        w1_raw, cand_raw = {}, {}

        def load_w1(b, lo, hi, after):
            raw = sbuf("w1_raw%d_%d" % (b, lo), [P, 4, 4 * (hi - lo)], F32, after)
            columns = w1[:, b * HALF + 4 * lo : b * HALF + 4 * hi]
            nc.sync.dma_start(raw[:], columns.rearrange("(p j) c -> p j c", j=4))
            for m in range(lo, hi, M_PIECE):
                w1_raw[b, m] = raw[:, :, 4 * (m - lo) : 4 * (m - lo + M_PIECE)]

        def load_cand(b, lo, hi, after):
            raw = sbuf("cand_raw%d_%d" % (b, lo), [P, 4, hi - lo], F32, after)
            nc.sync.dma_start(raw[:], cand[b * HALF : (b + 1) * HALF, lo:hi].rearrange("(p t) n -> p t n", t=4))
            cand_raw[b, lo] = raw

        def load_prior(after):
            cols = sbuf("prior_cols", [P, TILES], F32, after)
            with nc.allow_non_contiguous_dma(reason="one prior for each partition and tile of candidates"):
                nc.sync.dma_start(cols[:], prior.rearrange("(c p) -> p c", p=P))
            return cols

        def gather_words(h, after=None):
            words = sbuf("v_words%d" % h, [P, HALF], I32, after)
            lists = offsets[:, h * (HALF // 16) : (h + 1) * (HALF // 16)]
            nc.vector.tensor_copy(words[:].bitcast(U32), table[:].bitcast(U32).indirect(lists))
            return words

        w_dealt = sbuf("w_dealt", [P, HALF], U8)
        nc.vector.tensor_copy(
            w_dealt[:].rearrange("p (t m) -> p t m", t=4), w_rows[:].rearrange("p (m t) -> p t m", t=4)
        )
        for d in QUADRANTS:
            nc.sync.dma_start(w_plane[32 * d : 32 * d + 8, :].bitcast(I32), w_dealt[d:64:4, :].bitcast(I32))
        w2_plane, w3_plane = 0, 4
        w3_raw = sbuf("w3_raw", [P, H], I32, after="w_rows")
        nc.sync.dma_start(w3_raw[:], w3_words[0].rearrange("p n t -> p (n t)").bitcast(I32))
        picked = sbuf("picked", [P, S], U8)
        nc.vector.tensor_copy(picked[:], tab_rows[:].indirect(offsets[:]))
        for d in QUADRANTS:
            nc.sync.dma_start(
                v_plane[32 * d : 32 * d + 4, :].bitcast(I32), picked[32 * d : 32 * (d + 1) : 8, :].bitcast(I32)
            )
        load_w1(0, 0, P, after="tab_rows")
        w2_codes = sbuf("w2_codes", [P, H // 2], I32)
        nc.scalar.copy(
            w2_codes[:].bitcast(U16).rearrange("p (b t m) -> p b t m", b=2, t=4),
            w2_raw[:].bitcast(U16).rearrange("p (b m t) -> p b t m", b=2, t=4),
        )
        v_words = [gather_words(h) for h in range(2)]
        unread = next_bank(1)
        for repeat in range(WARM_UP_PASSES):
            nc.tensor.matmul_mx(
                out=unread[:, 0, :],
                lhsT=table[:, 0:P].bitcast(FP8X4),
                lhsT_scale=picked[:, 0:P],
                rhs=table[:, 0:HALF].bitcast(FP8X4),
                rhs_scale=picked[:, 0:HALF],
                start=True,
                stop=True,
            )
        load_cand(0, 0, GPSIMD_FIRST, after="table")
        w3_codes = sbuf("w3_codes", [P, H], I32)
        for b, copy in enumerate((nc.scalar.copy, nc.vector.tensor_copy)):
            copy(
                w3_codes[:, b * HALF : (b + 1) * HALF].bitcast(U32).rearrange("p (t m) -> p m t", t=4),
                w3_raw[:, b * HALF : (b + 1) * HALF].bitcast(U32).rearrange("p (m t) -> p m t", t=4),
            )

        w1_round = {}
        cand_round, scaled, pair, h_round, h_first = {}, {}, {}, {}, {}
        w1_mx, cand_mx, h_mx = {}, {}, {}

        def quantise(name, rounded, width, after):
            codes = sbuf(name + "_codes", [P, width], U32, after)
            plane = sbuf(name + "_plane", [P, width], U8)
            nc.vector.quantize_mx(out=codes[:].bitcast(FP8X4), scales=plane[:], in_=rounded)
            return codes, plane

        for b in range(2):
            h_first[b] = sbuf("h_first%d" % b, [P, 4 * HALF], BF16)
            for q in range(4):
                h_round[0, b, q] = h_first[b][:, 4 * q * P : 4 * (q + 1) * P]
            for q in range(2, 4):
                h_round[1, b, q] = sbuf("h_last%d%d" % (b, q), [P, 4 * P], BF16)[:]
        h_middle = sbuf("h_middle", [P, 2, 2, 4 * P], BF16)
        for b in range(2):
            for q in range(2):
                h_round[1, b, q] = h_middle[:, b, q, :]

        def round_w1(copy, b, lo, after=None):
            if lo == 0:
                w1_round[b] = sbuf("w1_round%d" % b, [P, 4 * HALF], BF16, after)
            dst = w1_round[b][:].rearrange("p (t m j) -> p m j t", t=4, j=4)
            copy(dst[:, lo : lo + M_PIECE], w1_raw[b, lo].rearrange("p j (m t) -> p m j t", t=4))

        def quantise_w1(b, after=None):
            w1_mx[b] = quantise("w1_%d" % b, w1_round[b][:], HALF, after)

        def open_rounded(b, lo, hi, after):
            cand_round[b, lo] = sbuf("cand_round%d_%d" % (b, lo), [P, 4 * (hi - lo)], BF16, after)

        def round_cand_gpsimd(b, lo, share):
            dst = cand_round[b, lo][:, 0 : 4 * share].rearrange("p (c t) -> p c t", t=4)
            src = cand_raw[b, lo][:, :, 0:share].rearrange("p t c -> p c t")
            nc.gpsimd.tensor_scalar(dst, src, 1.0, 0.0, MULT, ADD)

        def round_cand_scalar(b, lo, skip):
            dst = cand_round[b, lo][:, 4 * skip :].rearrange("p (c e t) -> p c t e", e=2, t=4)
            nc.scalar.copy(dst, cand_raw[b, lo][:, :, skip:].rearrange("p t (c e) -> p c t e", e=2))

        def quantise_cand(b, lo, hi, after=None):
            codes, plane = quantise("cand%d_%d" % (b, lo), cand_round[b, lo][:], hi - lo, after)
            for c in range(lo // P, hi // P):
                cols = slice(c * P - lo, (c + 1) * P - lo)
                cand_mx[b, c] = codes[:, cols], plane[:, cols]

        def quantise_h_first(b, after):
            codes, plane = quantise("h_first%d" % b, h_first[b][:], HALF, after)
            h_mx[0, b, 0] = codes[:], plane[:]

        def quantise_h_middle(after):
            codes, plane = quantise("h_middle", h_middle[:].rearrange("p b q n -> p (b q n)"), HALF, after)
            for b in range(2):
                cols = slice(b * 2 * P, (b + 1) * 2 * P)
                h_mx[1, b, 0] = codes[:, cols], plane[:, cols]

        def quantise_h_last(b, q, after=None):
            codes, plane = quantise("h_last%d%d" % (b, q), h_round[1, b, q], P, after)
            h_mx[1, b, q * P] = codes[:], plane[:]

        steps = [(0, 0, HALF, b, t) for b in range(2) for t in range(4)]
        steps = steps + [(1, 0, 2 * P, b, t) for b in range(2) for t in (0, 2)]
        steps = steps + [(1, lo, P, b, 0) for lo in (2 * P, 3 * P) for b in range(2)]
        x3_rows, x1_banks, x2_banks, x3_banks = {}, {}, {}, {}

        def w2_tile(b, t):
            return w2_codes[:, (4 * b + t) * P // 2 : (4 * b + t + 1) * P // 2].bitcast(FP4X4)

        def w3_tile(b, t):
            return w3_codes[:, (4 * b + t) * P : (4 * b + t + 1) * P].bitcast(FP8X4)

        def project(step, weight_tile, plane):
            h, lo, width, b, t0 = step
            sums = next_bank(HALF // width)
            for g in range(HALF // width):
                t = t0 + g
                nc.tensor.matmul_mx(
                    out=sums[:, g, :],
                    lhsT=weight_tile(b, t),
                    lhsT_scale=w_plane[plane:P, (4 * b + t) * P : (4 * b + t + 1) * P],
                    rhs=v_words[h][:, lo : lo + width].bitcast(FP8X4),
                    rhs_scale=v_plane[:, h * HALF + lo : h * HALF + lo + width],
                    start=True,
                    stop=True,
                )
            return sums

        def project_x2(j):
            x2_banks[j] = project((j // 8, 0, HALF, j // 4 % 2, j % 4), w2_tile, w2_plane)

        def project_x3(k):
            x3_banks[k] = project(steps[k], w3_tile, w3_plane)

        def scaled_row(j, after):
            if j not in x2_banks:
                project_x2(j)
            rows = 1 if j < 8 else 4
            first = j - j % rows
            if j == first:
                scaled[j] = sbuf("scaled%d" % j, [P, rows, HALF], F32, after)
            return scaled[first][:, j - first, :], x2_banks[j][:, 0, :], rel_cols[:, j // 4 % 2, j % 4 : j % 4 + 1]

        def scale_x2(j, after=None):
            row, x2, factor = scaled_row(j, after)
            nc.scalar.activation(row, x2, ACT.Copy, scale=factor)

        def scale_x2_vector(j):
            row, x2, factor = scaled_row(j, None)
            nc.vector.tensor_scalar(row, x2, factor, None, MULT)

        def scaled_rows(k):
            h, lo, width, b, t0 = steps[k]
            if h == 0:
                return scaled[4 * b + t0][:]
            return scaled[8 + 4 * b][:, t0 : t0 + HALF // width, lo : lo + width]

        def pair_rows(k, after=None):
            h, lo, width, b, t0 = steps[k]
            if (h, lo, b) not in pair:
                pair[h, lo, b] = sbuf("pair%d_%d_%d" % (h, lo, b), [P, 4, width], F32, after)
            return pair[h, lo, b][:, t0 : t0 + HALF // width, :]

        def pair_product(k):
            if k not in x3_banks:
                project_x3(k)
            nc.vector.tensor_tensor(pair_rows(k), x3_banks[k][:], scaled_rows(k), MULT)

        def copy_x3(k, after=None):
            h, lo, width, b, t0 = steps[k]
            if k not in x3_banks:
                project_x3(k)
            x3_rows[k] = sbuf("x3_%d" % k, [P, HALF // width, width], F32, after)
            nc.scalar.copy(x3_rows[k][:], x3_banks[k][:])

        def pair_product_gpsimd(k, after):
            nc.gpsimd.tensor_tensor(pair_rows(k, after), x3_rows[k][:], scaled_rows(k), MULT)

        def project_x1(h, b, q):
            cols = slice(q * P, (q + 1) * P)
            x1_banks[h, b, q] = next_bank(4)
            codes, plane = w1_mx[b]
            for t in range(4):
                nc.tensor.matmul_mx(
                    out=x1_banks[h, b, q][:, t, :],
                    lhsT=codes[:, t * P : (t + 1) * P].bitcast(FP8X4),
                    lhsT_scale=plane[:, t * P : (t + 1) * P],
                    rhs=v_words[h][:, cols].bitcast(FP8X4),
                    rhs_scale=v_plane[:, h * HALF + q * P : h * HALF + (q + 1) * P],
                    start=True,
                    stop=True,
                )

        def multiply_x1(h, b, q):
            lo = 0 if h == 0 or q < 2 else q * P
            nc.vector.tensor_tensor(
                h_round[h, b, q].rearrange("p (n e t) -> p n t e", e=2, t=4),
                x1_banks[h, b, q][:].rearrange("p t (n e) -> p n t e", e=2),
                pair[h, lo, b][:, :, q * P - lo : (q + 1) * P - lo].rearrange("p t (n e) -> p n t e", e=2),
                MULT,
            )

        def triple_product(h, b, q):
            if (h, b, q) not in x1_banks:
                project_x1(h, b, q)
            multiply_x1(h, b, q)

        out_view = out.rearrange("(c p) j -> p c j", p=P)

        def score_passes(sums, h, lo, c0, count, b):
            for g in range(count):
                nc.tensor.matmul_mx(
                    out=sums[:, g, :],
                    lhsT=cand_mx[b, c0 + g][0].bitcast(FP8X4),
                    lhsT_scale=cand_mx[b, c0 + g][1],
                    rhs=h_mx[h, b, lo][0].bitcast(FP8X4),
                    rhs_scale=h_mx[h, b, lo][1],
                    start=(b == 0 and g == 0),
                    stop=(b == 1 and g == count - 1),
                )

        def add_prior_scalar(staged, sums, c0, count):
            for g in range(count):
                nc.scalar.activation(
                    staged[:, g, :], sums[:, g, :], ACT.Identity, bias=prior_cols[:, c0 + g : c0 + g + 1]
                )

        def add_prior_vector(staged, sums, c0, count):
            spread = prior_cols[:, c0 : c0 + count].unsqueeze(2).to_broadcast([P, count, P])
            nc.vector.tensor_tensor(staged, sums[:, 0:count, :], spread, ADD)

        def store(staged, first, width, c0, count, queue=nc.sync):
            queue.dma_start(out_view[:, c0 : c0 + count, first : first + width], staged[:])

        def score(h, width, c0, count):
            per_bank = HALF // width
            staged = keep.tile([P, count, width], F32, name="staged_%d_%d" % (h, c0))
            for g in range(0, count, per_bank):
                sums = next_bank(per_bank)
                for b in range(2):
                    score_passes(sums, h, 0, c0 + g, per_bank, b)
                add_prior_scalar(staged[:, g : g + per_bank, :], sums, c0 + g, per_bank)
            store(staged, h * HALF, width, c0, count)

        share = TILES // 2

        def last_passes(q, b, sums, order=(0, 1)):
            for half_of_tiles in order:
                score_passes(sums[half_of_tiles], 1, q * P, half_of_tiles * share, share, b)

        def open_last(q):
            sums = [next_bank(4), next_bank(4)]
            last_passes(q, 0, sums)
            return sums

        def finish_last(q, sums, half_of_tiles, queue=nc.sync):
            c0 = half_of_tiles * share
            staged = keep.tile([P, share, P], F32, name="staged_last_%d_%d" % (q, c0))
            (add_prior_scalar, add_prior_vector)[half_of_tiles](staged[:], sums[half_of_tiles], c0, share)
            store(staged, HALF + q * P, P, c0, share, queue)

        scale_x2_vector(0)
        scale_x2(1)
        pair_product(0)
        load_w1(1, 0, M_PIECE, after="scaled0")
        scale_x2(2)
        pair_product(1)
        scale_x2(3)
        pair_product(2)
        load_w1(1, M_PIECE, P, after="scaled2")
        round_w1(nc.scalar.copy, 0, 0, after="scaled1")
        round_w1(nc.vector.tensor_copy, 0, M_PIECE)
        pair_product(3)
        load_cand(1, 0, SIDE, after="scaled3")
        scale_x2(4)
        project_x3(4)
        scale_x2(5)
        project_x3(5)
        quantise_w1(0)

        open_rounded(0, 0, GPSIMD_FIRST, after="scaled1")
        round_cand_gpsimd(0, 0, GPSIMD_FIRST)
        scale_x2(6)
        scale_x2(7)
        pair_product(4)
        load_cand(0, GPSIMD_FIRST, N, after="scaled4")
        pair_product(5)
        for q in range(4):
            triple_product(0, 0, q)
        round_w1(nc.scalar.copy, 1, 0, after="scaled5")
        round_w1(nc.scalar.copy, 1, M_PIECE)
        prior_cols = load_prior(after="pair0_0_0")
        pair_product(6)
        load_cand(1, SIDE, N, after="scaled6")
        pair_product(7)
        scale_x2(8, after="scaled2")
        scale_x2(9)
        project_x3(8)
        scale_x2(10)
        scale_x2(11)
        quantise_w1(1, after="table")
        quantise_cand(0, 0, GPSIMD_FIRST)
        quantise_h_first(0, after="scaled7")

        open_rounded(1, 0, SIDE, after="scaled1")
        round_cand_gpsimd(1, 0, GPSIMD_SECOND)
        project_x2(12)
        project_x2(13)
        pair_product(8)
        round_cand_scalar(1, 0, GPSIMD_SECOND)
        scale_x2(12, after="scaled5")
        scale_x2(13)
        for q in range(4):
            triple_product(0, 1, q)
        open_rounded(0, GPSIMD_FIRST, N, after="h_first0")
        round_cand_scalar(0, GPSIMD_FIRST, 0)
        copy_x3(10)
        project_x3(9)
        scale_x2(14)
        scale_x2(15)
        project_x1(1, 0, 0)
        project_x1(1, 0, 1)
        project_x3(11)
        project_x3(13)
        quantise_cand(1, 0, SIDE)
        quantise_h_first(1, after=None)
        quantise_cand(0, GPSIMD_FIRST, N, after="pair0_0_1")

        open_rounded(1, SIDE, N, after="h_first1")
        round_cand_gpsimd(1, SIDE, GPSIMD_THIRD)
        pair_product_gpsimd(10, after="h_first0")
        round_cand_scalar(1, SIDE, GPSIMD_THIRD)
        pair_product(9)
        copy_x3(13)
        score(0, HALF, 0, 1)
        triple_product(1, 0, 0)
        project_x1(1, 1, 0)
        triple_product(1, 0, 1)
        pair_product(11)
        score(0, HALF, 1, 1)
        project_x1(1, 1, 1)
        score(0, HALF, 2, 1)
        project_x3(12)
        copy_x3(15)
        quantise_cand(1, SIDE, N, after="x3_10")

        pair_product_gpsimd(13, after="h_first1")
        triple_product(1, 1, 0)
        score(0, HALF, 3, 1)
        triple_product(1, 1, 1)
        project_x1(1, 0, 2)
        score(0, HALF, 4, 1)
        pair_product(12)
        project_x3(14)
        project_x1(1, 1, 2)
        score(0, HALF, 5, 1)
        quantise_h_middle(after="x3_13")

        pair_product_gpsimd(15, after="h_middle")
        pair_product(14)
        multiply_x1(1, 0, 2)
        score(1, 2 * P, 0, 2)
        project_x1(1, 0, 3)
        multiply_x1(1, 1, 2)
        score(1, 2 * P, 2, 2)
        multiply_x1(1, 0, 3)
        project_x1(1, 1, 3)
        score(1, 2 * P, 4, 2)

        quantise_h_last(0, 2, after="x3_15")
        quantise_h_last(1, 2, after="scaled5")
        quantise_h_last(0, 3)
        sums_2 = open_last(2)
        last_passes(2, 1, sums_2)
        finish_last(2, sums_2, 0)
        multiply_x1(1, 1, 3)
        sums_3 = open_last(3)
        quantise_h_last(1, 3)
        finish_last(2, sums_2, 1)
        last_passes(3, 1, sums_3, order=(1, 0))
        finish_last(3, sums_3, 1)
        finish_last(3, sums_3, 0, nc.scalar)
